import numpy as np, ml_dtypes
CORES = [9,25,41,57]
N = 4
import mx_ref
BF = ml_dtypes.bfloat16
def gcols(t, e):
    v = np.concatenate([t.reshape(8, 16, -1, 4), np.zeros((8, 16, 1, 4), BF)], axis=2)
    return np.ascontiguousarray(np.stack([v[g][:, e[g]] for g in range(8)])).reshape(128, -1)
def tile(rs):
    return np.stack(rs, axis=2).reshape(128, -1).astype(BF)
def pick(q, e):
    c = np.concatenate([q[0].reshape(128, -1, 4), np.zeros((128, 1, 4), np.uint8)], axis=1); s = np.concatenate([q[1], np.ones((16, 1), np.uint8)], axis=1)
    return (np.ascontiguousarray(c[:, e].reshape(128, -1)), np.ascontiguousarray(s[:, e]))
def join(*qs):
    return (np.concatenate([q[0] for q in qs], axis=1), np.concatenate([q[1] for q in qs], axis=1))
def put(q, e, v):
    c, s = q[0].reshape(128, -1, 4).copy(), q[1].copy(); c[:, e] = v[0].reshape(128, -1, 4); s[:, e] = v[1]
    return (c.reshape(128, -1), s)
def pk(c, s):
    return (np.ascontiguousarray(c), mx_ref.live(s))
def emit(q):
    return q[0], q[1]
def packed(v, rng):
    q = [mx_ref.quantize(np.ascontiguousarray(v[r])) for r in range(N)]
    return np.stack([a for a, b in q]), np.stack([mx_ref.plane(b, rng) for a, b in q])
def values_of_codes():
    e, c = np.zeros((128, 128, 4), np.float32), np.zeros((128, 2, 4), np.uint8)
    e[np.arange(128), np.arange(128), 0] = 1
    c[:127, :, 0] = np.arange(256).reshape(2, 128).T[:127]
    return mx_ref.matmul(mx_ref.quantize(e.reshape(128, 512).astype(BF)), (c.reshape(128, 8), np.full((16, 2), 127, np.uint8))).T.reshape(-1).astype(np.float64)
CODE_VALUE, SCALE_VALUE = values_of_codes(), 2.0 ** (np.arange(256) - 127.0)
def decode(q):
    return (CODE_VALUE[q[0]].reshape(16, 8, -1, 4) * SCALE_VALUE[q[1]][:, None, :, None] + 0.0).reshape(128, -1).astype(np.float32)
def f(rng, *shape):
    return mx_ref.flush((rng.standard_normal(shape, dtype=np.float32) * np.exp2(rng.integers(-2, 3, shape[:-1] + (1,)))).astype(BF))
def wide(rng, *shape, cols=0):
    v = rng.standard_normal(shape, dtype=np.float32) * np.exp2(rng.integers(-12, 13, shape)).astype(np.float32)
    if cols: v *= np.repeat(np.exp2(rng.integers(-cols, cols + 1, shape[:-2] + (1, shape[-1] // 4))) * (rng.random(shape[:-2] + (1, shape[-1] // 4)) > 0.0625), 4, axis=-1).astype(np.float32)
    return mx_ref.flush(v.astype(BF))
C, I, ST, M, R = 384, 32, 12, 64, 3
def big(v):
    v = v.astype(np.float32)
    v[np.abs(v) < np.float32(2.0 ** -16)] = 0
    return v.astype(BF)
def numbers_of(rng):
    return {"x": big(f(rng, N, 128, 4 * C)), "u": np.array(f(rng, N, 128, 512)), "v": np.array(f(rng, N, 128, 512))}
def layers(rng):
    return big(f(rng, N, 128, 2048)).reshape(N, 8, 16, 4, 8, 16, 4)
def through(w, some):
    for i in some:
        w[:, :, i] = 0
        w[:, :, :, :, :, i] = 0
        for g in range(8):
            for b in range(4): w[:, g, i, b, g, i, b] = 32
    return w
def weights(rng, w):
    c, p = packed(np.ascontiguousarray(w).reshape(N, 128, 2048), rng)
    return {"wc": c, "ws": p}
def setup_inputs(rng):
    return {**numbers_of(rng), **weights(rng, layers(rng))}
def setup_inputs_ties(rng):
    d = numbers_of(rng)
    x = d["x"].astype(np.float32).reshape(N, 8, 16, C, 4)
    x[:, :, 0] = 0
    x[:, :, 0, :, 0] = rng.integers(0, 3, (N, 8, C))
    x[:, :, 0, :, 1] = 1.125
    some = rng.permutation(8)[:4]
    k = np.exp2(rng.integers(-2, 3, (N, 8, 1, C, 1)))
    k[:, some] = 1
    s = (N, 8, 8, C, 4)
    e = rng.integers(-21, -14, s)
    for j in range(4): e[:, some[j]] = j - 21
    x[:, :, 8:] = (129 + 2 * rng.integers(0, 64, s)) * np.exp2(e) * rng.choice([-1.0, 1.0], s) * k
    x[:, :, 8, :, 0] = 1.96875 * k[:, :, 0, :, 0]
    u = d["u"].reshape(N, 128, 128, 4)
    u[:, :, ::16] = 0
    o = rng.permutation(N)
    for r in range(N):
        for h in range(0, 128, 16):
            if r != o[0]:
                if h // 16 in some: u[r, h + 9:h + 16, h] = rng.choice([-1.0, 1.0], (7, 4)).astype(np.float32).astype(BF)
                else: u[r, h, h, 0] = -1.0 if r == o[1] else 1.0
            for i in (1, 2):
                if r == o[2] or r == o[3]: u[r, :, h + i] = 0
                if r == o[3]: u[r, h, h + i, 1] = 1
    w = through(layers(rng), [0])
    for g in some:
        w[:, :, :, :, g, 8:] = 0
        w[:, g, 0, 0, g, 8, 1] = 56
        for i in range(9, 16):
            for b in range(4): w[:, g, i, b, g, i, b] = 16
    return {"x": x.reshape(N, 128, 4 * C).astype(BF), "u": u.reshape(N, 128, 512), "v": d["v"], **weights(rng, w)}
def setup_inputs_near(rng):
    d = numbers_of(rng)
    x = d["x"].astype(np.float32).reshape(N, 8, 16, C, 4)
    x[:, :, 0] = 0
    x[:, :, 8:] = 0
    c = (rng.permutation(8) % 2 * 2.0 - 1.0)[:, None]
    s = rng.integers(0, 16, (N, 8, C))
    x[:, :, 8] = ((s[:, :, :, None] >> np.arange(4)) & 1) * np.exp2(np.arange(4) - 23.0)
    u = d["u"].reshape(N, 128, 128, 4)
    u[:, :, ::16] = 0
    o = rng.permutation(N) % 4
    for r in range(N):
        if o[r] % 2 == 0:
            x[r, :, 0, :, 0] = c
            x[r, :, 11, :, 0] = 2.0 ** -10
        else:
            for g in rng.permutation(8)[:4]: x[r, g, 0, rng.integers(C), 0] = 2.0 ** 26 * rng.choice([-1.0, 1.0])
        k = 1.0 if o[r] < 2 else 2.0 ** -30
        for h in range(0, 128, 16):
            u[r, h, h, 0] = k
            u[r, h + 8, h] = k
            u[r, h + 11, h, 0] = k
    return {"x": x.reshape(N, 128, 4 * C).astype(BF), "u": u.reshape(N, 128, 512), "v": d["v"], **weights(rng, through(layers(rng), [0, 8, 9, 10, 11, 12, 13, 14, 15]))}
def setup_inputs_huge(rng):
    d = numbers_of(rng)
    o = rng.permutation(N)
    c = rng.choice([-1.0, 1.0], (N, 1, 1, C, 1))
    c[o < N // 2] = (rng.permutation(N // 2) % 2 * 2.0 - 1.0).reshape(-1, 1, 1, 1, 1)
    x = 0.9 * 2.0 ** 30 * c * (0.8 + 0.2 * rng.random((N, 1, 1, C, 1))) * (0.95 + 0.05 * rng.random((N, 8, 16, C, 4)))
    x[:, :, 0] = np.abs(x[:, :, 0])
    x[:, :, 1, :, :2] *= rng.choice([-1.0, 1.0], (N, 8, C, 2))
    u = d["u"].reshape(N, 128, 128, 4)
    a = 2.0 ** 30 * (1.0 - 0.1 * rng.random((N, 8, 16, 8, 4))) * (rng.permutation(8) % 2 * 2.0 - 1.0)[:, None]
    a[:, :, :2] = 0
    u[:, :, ::16] = a.reshape(N, 128, 8, 4).astype(np.float32).astype(BF)
    for h in range(0, 128, 16):
        u[:, :, h + 1:h + 3] = 0
        u[:, h + 1, h + 1, 0] = 1
        u[:, h + 1, h + 2, 1] = 1
    w = np.zeros((N, 128, 4, 128, 4), np.float32)
    i = np.arange(128)
    j = i[i % 16 > 1]
    for r in range(N):
        for b in range(4):
            if o[r] < N // 2: w[r, j - j % 16, b, j, b] = -16.0 * c[r, 0, 0, 0, 0]
            else: w[r, i, b, i, b] = -1
    return {"x": x.astype(np.float32).reshape(N, 128, 4 * C).astype(BF), "u": u.reshape(N, 128, 512), "v": d["v"], **weights(rng, w.astype(BF))}
def setup_inputs_few(rng):
    d = numbers_of(rng)
    x = d["x"].reshape(N, 8, 16, C, 4)
    c = np.where(rng.random((N, 8, C, 2)) < 0.0625, 1.0, -1.0)
    e = rng.permutation(N)
    c[e[1], :, :, 0] = 1
    c[e[1], :, :, 1] = -1
    c[e[2]] = -1
    for g in range(8):
        for b in range(2): c[e[2], g, rng.integers(C), b] = 1
    u = d["u"].reshape(N, 128, 128, 4)
    for h in range(0, 128, 16):
        u[:, :, h + 1:h + 3] = 0
        u[:, h + 1, h + 1, 0] = 1
        u[:, h + 1, h + 2, 1] = 1
    w = layers(rng)
    w[:, :, :, :, :, 1] = 0
    for r in e[1::2]:
        c[r] *= 2.0 ** -28
        x[r, :, :8] = 0
        x[r, :, 2:4, :, 0] = (rng.integers(-2, 3, (8, 1, C)) * 2.0 ** -28).astype(np.float32).astype(BF)
        u[r, :, ::16] = 0
        for h in range(0, 128, 16):
            u[r, h + 1, h + 1, 0] = 2.0 ** -30
            u[r, h + 1, h + 2, 1] = 2.0 ** -30
            u[r, h + 2, h, 0] = 1.875 * 2.0 ** -30
            u[r, h + 3, h, 0] = -1.75 * 2.0 ** -30
        w[r, :, :, :, :, :8] = 0
    x[:, :, 1, :, :2] = c.astype(np.float32).astype(BF)
    x[e[0]] = 0
    return {"x": x.reshape(N, 128, 4 * C), "u": u.reshape(N, 128, 512), "v": d["v"], **weights(rng, w)}
def setup_inputs_spread(rng):
    d = setup_inputs(rng)
    d["x"] = big(wide(rng, N, 128, 4 * C, cols=6))
    return d
def check_inputs(d):
    b = []
    for k in ("x", "u", "v"):
        a = np.abs(d[k].astype(np.float32))
        if not (np.isfinite(a).all() and ((a == 0) | (a >= 2.0 ** -30) & (a <= 2.0 ** 30)).all()): b.append("a value of " + k)
    none, least, most = [emit(mx_ref.quantize(np.full((128, 16), k, np.float32).astype(BF)))[1][0, 0] for k in (0.0, 2.0 ** -30, 2.0 ** 30)]
    for r in range(N):
        if ((d["wc"][r] == 0x7F) | (d["wc"][r] == 0xFF)).any(): b.append("wc: a code that is no number")
        s = mx_ref.live(d["ws"][r])
        if ((s != none) & ((s < least) | (s > most))).any(): b.append("ws: a scale out of range")
    return b
def reference(x, u, v, wc, ws):
    qu = [mx_ref.quantize(u[r]) for r in range(N)]
    lay = [pk(wc[r], ws[r]) for r in range(N)]
    now = [x[r] for r in range(N)]
    k = np.arange(I)
    taken = np.zeros((N, 8, C), np.int64)
    half = np.float32(0.5)
    for t in range(R):
        own, mine, sent = [], [], []
        for r in range(N):
            q = mx_ref.quantize(now[r])
            s = mx_ref.matmul(qu[r], q) + np.float32(0.0)
            own.append(decode(q))
            order = np.argsort(-s[::16], axis=1, kind="stable")
            even, odd = (s[1::16] > 0).astype(np.int64), (s[2::16] > 0).astype(np.int64)
            place = np.zeros((8, C), np.int64)
            np.put_along_axis(place, order, np.arange(C)[None] * np.ones((8, 1), np.int64), axis=1)
            j = place // ST
            n = 2 * j + np.where(j % 2 == 0, even, odd)
            m = 2 * ((j + I - 1) % I) + np.where(j % 2 == 0, odd, even)
            mine.append((np.minimum(n, m), np.maximum(n, m)))
            first, last = np.full((8, M), -1), np.full((8, M), -1)
            for i in range(2 * ST):
                for to, at in ((last, i), (first, 2 * ST - 1 - i)):
                    e = order[:, (ST * k + at) % C]
                    c = np.where(k % 2 == 0, np.take_along_axis(even, e, axis=1), np.take_along_axis(odd, e, axis=1))
                    np.put_along_axis(to, 2 * k + c, e, axis=1)
            a = own[r].astype(BF)
            z = ((gcols(a, first).astype(np.float32) + gcols(a, last).astype(np.float32)) * half).astype(BF).astype(np.float32)
            sent.append(mx_ref.quantize(((z + np.roll(z, -8, axis=1)) * half).astype(BF)))
        for r in range(N):
            q = sent[(r + N - 1) % N]
            h = tile([mx_ref.matmul(pick(lay[r], np.arange(128 * b, 128 * b + 128)), q) * np.float32(0.03125) for b in range(4)])
            w = mx_ref.matmul(qu[r], mx_ref.quantize(h))[::16] + np.float32(0.0)
            lo, hi = mine[r]
            taken[r] = np.where(np.take_along_axis(w, hi, axis=1) > np.take_along_axis(w, lo, axis=1), hi, lo)
            now[r] = (own[r] + gcols(h, taken[r]).astype(np.float32)).astype(BF)
    y, nd = np.zeros((N, 128, C), np.float32), np.zeros((N, 8, C), np.float32)
    oc, osc = np.zeros((N, 128, 4 * C), np.uint8), np.zeros((N, 16, C), np.uint8)
    for r in range(N):
        q = mx_ref.quantize(now[r])
        y[r] = mx_ref.matmul(mx_ref.quantize(v[r]), q)
        nd[r] = taken[r]
        oc[r], osc[r] = emit(q)
    return {"y": y, "nd": nd, "oc": oc, "osc": osc}

@@ -1,0 +1,502 @@
+from concourse.mybir import dt, AluOpType as A, ActivationFunctionType as F
+
+C, NT, M, R = 384, 24, 64, 3
+HUGE = 2.0 ** 80
+BIG = 2.0 ** 20
+TINY = 2.0 ** -126
+PW = 400
+SLOTS = [[0, 23, 22, 21], [20, 19, 18, 17], [16, 15, 14, 13], [12, 11, 10, 9], [8, 7, 6, 5], [4, 3, 2, 1]]
+WIDTH = [384, 320, 256, 192, 128, 128]
+START = [0, 384, 704, 960, 1152, 1280]
+ON_SCALAR = [23, 22, 21, 20, 19, 18]
+MID = [17]
+CUT = 256
+LAND = [0, 192, 256]
+VIEW = [0, 128, 256]
+
+BF, F32, I32, U16, X4, U8 = "bfloat16", "float32", "int32", "uint16", "float8_e4m3fn_x4", "uint8"
+
+
+def _s(n, d):
+    return ("sbuf", [128, n], d)
+
+
+PSUM = ["pa", "pbk", "pcl", "pd", "pf0", "pf1", "pf2", "pf3"]
+SCRATCH = {
+    "xin": _s(4 * C, BF), "xt": _s(4 * C, BF), "qx": _s(C, X4), "sx": _s(C, U8),
+    "ut": _s(512, BF), "qu": _s(128, X4), "su": _s(128, U8), "qur": _s(384, X4), "sur": _s(384, U8),
+    "vt": _s(512, BF), "qv": _s(128, X4), "sv": _s(128, U8), "qw": _s(512, X4), "sw": _s(512, U8),
+    "pint": _s(1, I32), "ints": _s(8, I32), "pb": _s(8, F32), "pc": _s(32, F32), "t16": _s(NT, F32),
+    "uoff": _s(NT, U16), "k16": _s(C, BF), "jp": _s(128, BF), "gcol": _s(128, BF), "r24": _s(432, BF),
+    "idc": _s(C, F32), "idf": _s(C, F32), "keep2": _s(272, BF), "idp": _s(M, BF), "par": _s(34, BF),
+    "eq": _s(C, BF), "kc": _s(C, BF), "d0": _s(C, BF), "ax": _s(C, BF), "keep16": _s(C, BF), "kx": _s(C, F32),
+    "dec0": _s(420, BF), "dec": _s(420, BF), "mka": _s(34, F32), "cst": _s(NT, F32), "keepr": _s(640, BF),
+    "et": _s(1040, BF), "qe": _s(512, X4), "se": _s(512, U8),
+    "gt": _s(512, BF), "qg": _s(128, X4), "sg": _s(128, U8), "zt": _s(512, BF),
+    "d1": _s(C, F32), "bb": _s(C, F32), "mt": _s(4 * 1408, BF), "qm": _s(1408, X4), "sm": _s(1408, U8),
+    "sgn": _s(7 * C, BF), "junk": _s(2 * C, BF), "rs": _s(NT, F32), "rd": _s(C, BF), "w1": _s(NT, F32),
+    "rsc": _s(2560, BF), "roff": _s(2, U16), "sig": _s(C, BF), "val": _s(C, F32),
+    "ext": _s(C, F32), "poff": _s(NT, U16),
+    "srt": _s(420, F32), "scn": _s(420, F32), "ab": _s(34, F32), "bi": _s(17, I32), "bj": _s(17, I32),
+    "zoff": _s(18, U16), "f0": _s(2 * PW, BF), "f1": _s(2 * PW, BF), "gz": _s(544, BF), "zz": _s(544, BF),
+    "yt": _s(512, BF), "qy": _s(128, X4), "sy": _s(128, U8), "ql": _s(448, X4), "sl": _s(448, U8),
+    "ht": _s(512, BF), "qh": _s(128, X4), "sh": _s(128, U8), "hp": _s(256, BF), "hs": _s(512, BF),
+    "hg": _s(2 * C, BF), "vd": _s(128, F32), "vb": _s(128, F32), "k8": _s(128, BF), "kd0": _s(128, BF),
+    "kd": _s(128, BF), "d8": _s(128, BF), "n0": _s(8, F32), "n1": _s(8, F32), "n2": _s(8, F32), "noff": _s(8, U16),
+    "tyi": _s(8, I32), "tyj": _s(8, I32),
+    "mo": _s(C, BF), "e1": _s(C, F32), "e2": _s(C, F32), "tt": _s(6 * NT, F32), "ki": _s(NT, I32),
+    "kj": _s(NT, I32), "toff": _s(NT, U16), "ids": _s(128, BF), "ndb": _s(C, F32), "ys": _s(C, F32),
+}
+SCRATCH.update({k: ("psum", [128, 512], F32) for k in PSUM})
+SEMAPHORES = (["cv", "cs", "ct", "cg"] + ["arr%d" % r for r in range(R)] + ["left%d" % r for r in range(R)]
+              + ["d%d" % k for k in range(20)])
+
+
+def rank_program(g, core, T, topo):
+    rank = T.rank_of(core)
+    if rank is None:
+        return
+    nxt = T.cores[(rank + 1) % len(T.cores)]
+    rid, pid = topo.addr(nxt)[0], topo.addr(nxt)[1]
+    mask = topo.mask(core, nxt)
+    lanes = len(topo.engines(core, nxt))
+
+    queue = {"v": g.vector, "s": g.scalar, "t": g.tensor, "g": g, "y": g.sync}
+    count = {"cv": 0, "cs": 0, "ct": 0, "cg": 0}
+    known = {k: {} for k in queue}
+    clock, wrote, read, used = {}, {}, {}, [0]
+
+    def after(q, events):
+        need = {}
+        for s, c in events:
+            if known[q].get(s, 0) < c and need.get(s, 0) < c:
+                need[s] = c
+        for s, c in sorted(need.items()):
+            if any(o != s and clock.get((o, d), {}).get(s, 0) >= c for o, d in need.items()):
+                continue
+            queue[q].wait_ge(T.sem[s], c)
+        for s, c in need.items():
+            for o, d in list(clock.get((s, c), {}).items()) + [(s, c)]:
+                if known[q].get(o, 0) < d:
+                    known[q][o] = d
+
+    def order(q, rd, wr, skip=()):
+        ev = []
+        for k in rd:
+            if k in wrote:
+                ev.append(wrote[k])
+            if k in PSUM:
+                ev += [e for e in read.get(k, []) if e[0] != "c" + q]
+        for k in wr:
+            if k in wrote and k not in skip:
+                ev.append(wrote[k])
+            ev += read.get(k, [])
+        after(q, ev)
+
+    def note(q, e, rd, wr):
+        clock[e] = dict(known[q])
+        for k in rd:
+            read.setdefault(k, []).append(e)
+        for k in wr:
+            wrote[k] = e
+            read[k] = []
+
+    def op(q, rd, wr, call, skip=()):
+        order(q, rd, wr, skip)
+        s = "c" + q
+        count[s] += 1
+        call().then_inc(T.sem[s], 1)
+        note(q, (s, count[s]), rd, wr)
+
+    def dma(q, out, in_, rd, wr, **kw):
+        order(q, rd, wr)
+        s = "d%d" % used[0]
+        used[0] += 1
+        count[s] = 16
+        queue[q].dma_start(out, in_, **kw).then_inc(T.sem[s], 16)
+        note(q, (s, 16), rd, wr)
+
+    V, S, P = g.vector, g.scalar, g.tensor
+
+    def ts(out, in0, s1, s2, o0, o1, rd, wr):
+        if o1 is None:
+            op("v", rd, wr, lambda: V.tensor_scalar(out, in0, s1, None, o0))
+        else:
+            op("v", rd, wr, lambda: V.tensor_scalar(out, in0, s1, s2, o0, o1))
+
+    def tt(out, a, b, o, rd, wr):
+        op("v", rd, wr, lambda: V.tensor_tensor(out, a, b, o))
+
+    def cp(out, in_, rd, wr):
+        op("v", rd, wr, lambda: V.tensor_copy(out, in_))
+
+    def scan(out, a, b, init, o0, o1, rd, wr):
+        op("v", rd, wr, lambda: V.tensor_tensor_scan(out, a, b, init, o0, o1))
+
+    def fill(ap, c, wr):
+        op("v", [], wr, lambda: V.memset(ap, c))
+
+    def quant(q, s, in_, rd, wr):
+        op("v", rd, wr, lambda: V.quantize_mx(q, s, in_))
+
+    def act(out, in_, f, rd, wr, bias=0.0, scale=1.0, acc=None):
+        if f == F.Copy:
+            op("s", rd, wr, lambda: S.activation(out, in_, f))
+        elif acc is None:
+            op("s", rd, wr, lambda: S.activation(out, in_, f, bias=bias, scale=scale))
+        else:
+            op("s", rd, wr, lambda: S.activation(out, in_, f, bias=bias, scale=scale, accum_out=acc))
+
+    def mm(bank, n, wq, ws, xq, xs, rd, start=True, stop=True):
+        op("t", rd, [bank], lambda: P.matmul_mx(T[bank][:, 0:n], wq, ws, xq, xs, start, stop),
+           skip=() if start else (bank,))
+
+    def iota(ap, pattern, base, cm, rd, wr):
+        op("g", rd, wr, lambda: g.iota(ap, pattern, base, cm, allow_small_or_imprecise_dtypes=True))
+
+    def pb(k):
+        return T.pb[:, k:k + 1]
+
+    def pc(k):
+        return T.pc[:, k:k + 1]
+
+    def pk(*ks):
+        return ["pc%d" % k for k in ks]
+
+    def col(k, src, scale, bias, rd):
+        act(pc(k), src, F.Identity, rd, pk(k), bias=bias, scale=scale)
+
+    QQ, PI, CC, BH, FL, GG, Q4 = range(7)
+    SC, SB, BO, DD, P12, CQ, NO, Z0 = range(8)
+    DCO, TA, TS_, TB, CA, QM, CB, WK, HH, AL, X1, GA = range(8, 20)
+    R1, R2, R3, R4, QN, OF, OG, CP, DF, DF0, WR, TH = range(20, 32)
+
+    dma("s", T.ut[:], T.u[:], [], ["ut"])
+    dma("y", T.xin[:], T.x[:], [], ["xin"])
+
+    op("g", [], ["pint"], lambda: g.iota(T.pint[:], [[0, 1]], 0, 1))
+    for name, pattern, base, cm in [
+            ("t16", [[16, NT]], 0, 0), ("k16", [[0, NT], [1, 16]], 0, 0), ("gcol", [[1, 8], [0, 16]], 0, 0),
+            ("jp", [[1, 128]], 0, -1), ("idc", [[1, C]], 1, 0), ("r24", [[0, 18], [1, 24]], 0, 0),
+            ("par", [[0, 17], [1, 2]], 0, 0), ("keep2", [[0, 136], [1, 2]], 0, 0), ("idp", [[1, M]], 0, 0),
+            ("k8", [[0, 16], [1, 8]], 0, 0)]:
+        iota(T[name][:], pattern, base, cm, [], [name])
+
+    fill(T.zt[:], 0.0, ["zt"])
+    for k, (sh, mk) in enumerate([(0, 15), (3, 1), (2, 1), (1, 1), (0, 1), (4, 7), (2, 3)]):
+        ts(T.ints[:, k:k + 1], T.pint[:], sh, mk, A.arith_shift_right, A.bitwise_and, ["pint"], ["ints%d" % k])
+    fill(T.et[:], 0.0, ["et0", "et1"])
+    cp(T.pb[:, 0:7], T.ints[:, 0:7], ["ints%d" % k for k in range(7)], ["pb"])
+    cp(T.uoff[:, 0:8], T.t16[:, 0:8], ["t16"], ["uoff0"])
+    ts(T.uoff[:, 8:16], T.t16[:, 0:8], pb(PI), 1.0, A.add, A.add, ["t16", "pb"], ["uoff1"])
+    ts(T.uoff[:, 16:24], T.t16[:, 0:8], pb(PI), 2.0, A.subtract, A.add, ["t16", "pb"], ["uoff2"])
+    ts(T.eq[:], T.k16[:], pb(QQ), None, A.is_equal, None, ["k16", "pb"], ["eq"])
+
+    col(SC, pb(CC), 2.0, -1.0, ["pb"])
+    col(SB, pb(CC), -1.0, 0.5, ["pb"])
+    col(DD, pb(FL), -(2.0 ** -11), 2.0 ** -12, ["pb"])
+    col(P12, pb(PI), 12.0, 0.0, ["pb"])
+    col(CQ, pb(QQ), 511.0, -7665.0, ["pb"])
+    col(BO, pb(BH), float(PW), 0.0, ["pb"])
+    act(T.keep16[:], T.k16[:], F.Sign, ["k16"], ["keep16"])
+    act(T.kc[:], T.eq[:], F.Identity, ["eq"], ["kc"], bias=-HUGE, scale=2 * HUGE)
+    act(T.d0[:], T.keep16[:], F.Identity, ["keep16"], ["d0"], bias=-HUGE, scale=2 * HUGE)
+
+    def tail(u):
+        lo = 16 * SLOTS[u][3]
+        return T.mt[:, 4 * (START[u] + lo):4 * (START[u] + WIDTH[u])], 4 * (WIDTH[u] - lo), ["m%d" % t for t in SLOTS[u]]
+
+    for u in (0, 1, 5):
+        fill(tail(u)[0], 0.0, tail(u)[2])
+    for e in range(2):
+        fill(T["f%d" % e][:, 0:1], 0.0, ["fz%d" % e])
+        fill(T["f%d" % e][:, C + 1:PW + 1], 0.0, ["fy%d" % e])
+    fill(T.keepr[:], 1.0, ["keepr"])
+    for u in range(2, 6):
+        a = START[u] - START[2]
+        iota(T.keepr[:, a:a + 1], [[0, 1]], 0, 0, ["keepr"], ["keepr%d" % u])
+    iota(T.rs[:, 0:1], [[0, 1]], 0, 0, [], ["rs0"])
+    quant(T.qu[:], T.su[:], T.ut[:], ["ut"], ["qu"])
+
+    def pick_u(a, b, names):
+        cp(T.qur[:, 16 * a:16 * b].bitcast(dt.uint32), T.qu[:, 0:128].bitcast(dt.uint32).indirect(T.uoff[:, a:b]),
+           ["qu"] + names, ["qur%d" % a])
+        act(T.sur[:, 16 * a:16 * b], T.su[:, 0:128].indirect(T.uoff[:, a:b]), F.Copy, ["qu"] + names, ["sur%d" % a])
+
+    pick_u(0, 16, ["uoff0", "uoff1"])
+    col(R1, pb(Q4), pb(Q4), pb(Q4), ["pb"])
+    col(Z0, T.eq[:, 0:1], -BIG, pc(CQ), ["eq"] + pk(CQ))
+    col(R2, pc(R1), -32.0, 2559.0, pk(R1))
+    act(tail(2)[0], T.zt[:, 0:tail(2)[1]], F.Copy, ["zt"], tail(2)[2])
+    col(R3, pb(BH), -1280.0, pc(R2), ["pb"] + pk(R2))
+    act(tail(3)[0], T.zt[:, 0:tail(3)[1]], F.Copy, ["zt"], tail(3)[2])
+    col(R4, pb(FL), -640.0, pc(R3), ["pb"] + pk(R3))
+    act(tail(4)[0], T.zt[:, 0:tail(4)[1]], F.Copy, ["zt"], tail(4)[2])
+    act(T.idf[:], T.idc[:], F.Identity, ["idc"], ["idf"], scale=2.0 ** -21)
+    for b in range(4):
+        ts(T.gt[:, b:512:4], T.gcol[:], pb(GG), None, A.is_equal, None, ["gcol", "pb"], ["gt%d" % b])
+    for h in range(2):
+        ts(T.et[:, 520 * h + 2 + h:520 * h + 514 + h:4], T.jp[:], 0.0, None, A.is_equal, None, ["jp"], ["et%d" % h])
+    quant(T.qg[:], T.sg[:], T.gt[:], ["gt%d" % b for b in range(4)], ["qg"])
+    for b in range(4):
+        o = 520 * (b % 2) + 2 - 2 * (b // 2)
+        quant(T.qe[:, 128 * b:128 * b + 128], T.se[:, 128 * b:128 * b + 128], T.et[:, o:o + 512],
+              ["et%d" % (b % 2)], ["qe%d" % b])
+
+    dma("y", T.qw[:].bitcast(dt.uint8), T.wc[:], ["xin"], ["qw"])
+    dma("y", T.sw[:], T.ws[:], [], ["sw"])
+    dma("y", T.vt[:], T.v[:], [], ["vt"])
+
+    US = (T.qur[:, 0:128], T.sur[:, 0:128])
+    UC = (T.qur[:, 128:256], T.sur[:, 128:256])
+    UD = (T.qur[:, 256:384], T.sur[:, 256:384])
+    UK = ["qur0", "sur0"]
+    RB = ["pa", "pd", "pf0", "pf1"]
+    XK = ["xt0", "xt1", "xt2", "xt3", "xt4"]
+
+    def fplane(b):
+        return T["f%d" % (b % 2)][:, PW * (b // 2) + 1:PW * (b // 2) + 1 + C]
+
+    def slot(t, n):
+        for u in range(6):
+            if t in SLOTS[u]:
+                a = 4 * START[u] + SLOTS[u].index(t)
+                return T.mt[:, a:a + 4 * n - 3:4]
+
+    def qtile(u):
+        a, b = START[u], START[u] + WIDTH[u]
+        quant(T.qm[:, a:b], T.sm[:, a:b], T.mt[:, 4 * a:4 * b], ["m%d" % t for t in SLOTS[u]], ["qm%d" % u])
+
+    def colsum(u, start, stop):
+        a, b = START[u], START[u] + WIDTH[u]
+        mm("pd", WIDTH[u], T.qg[:], T.sg[:], T.qm[:, a:b], T.sm[:, a:b], ["qg", "qm%d" % u], start, stop)
+
+    def own(t):
+        return T.bb[:, 16 * t + 15:16 * t + 16]
+
+    def compare(t):
+        ts(slot(t, 16 * t), T.pa[:, 0:16 * t], own(t), None, A.is_lt, None, ["pa", "bb"], ["m%d" % t])
+
+    def sign(k):
+        t = ON_SCALAR[k]
+        act(T.sgn[:, C * k:C * k + 16 * t], T.pbk[:, 0:16 * t], F.Sign, ["pbk", "bb"], ["sgn%d" % k],
+            bias=own(t), scale=-1.0)
+
+    def relu(k):
+        t = ON_SCALAR[k]
+        act(slot(t, 16 * t), T.sgn[:, C * k:C * k + 16 * t], F.Relu, ["sgn%d" % k], ["m%d" % t, "rs%d" % t],
+            acc=T.rs[:, t:t + 1])
+
+    def rows(b):
+        a = 4 * START[2] + b
+        scan(T.rsc[:, 640 * b:640 * b + 640], T.keepr[:], T.mt[:, a:a + 4 * 640 - 3:4], 0.0, A.mult, A.add,
+             ["keepr%d" % u for u in range(2, 6)] + ["m%d" % SLOTS[u][b] for u in range(2, 6)], ["rsc%d" % b])
+
+    def tk(k):
+        return T.tt[:, NT * k:NT * k + NT]
+
+    quant(T.qx[:], T.sx[:], T.xin[:], ["xin"], ["qx"])
+    for r in range(R):
+        mm("pa", C, US[0], US[1], T.qx[:], T.sx[:], UK + ["qx"])
+        mm("pcl", C, UC[0], UC[1], T.qx[:], T.sx[:], UK + ["qx"])
+        mm("pbk", C, US[0], US[1], T.qx[:], T.sx[:], UK + ["qx"])
+        for b in range(4):
+            mm("pf%d" % b, C, T.qe[:, 128 * b:128 * b + 128], T.se[:, 128 * b:128 * b + 128], T.qx[:], T.sx[:],
+               ["qe%d" % b, "qx"])
+        if r == 0:
+            ts(T.dec0[:], T.r24[:, 0:420], pc(P12), -4.0, A.is_equal, A.mult, ["r24"] + pk(P12), ["dec0"])
+            cp(T.roff[:, 0:1], pc(R4), pk(R4), ["roff"])
+            ts(T.cst[:], T.t16[:], pc(Z0), None, A.add, None, ["t16"] + pk(Z0), ["cst"])
+
+        tt(T.d1[:], T.pa[:, 0:C], T.kc[:], A.min, ["pa", "kc"], ["d1"])
+        if r == 0:
+            ts(T.mka[:], T.par[:], pb(PI), 2.0 ** 21, A.is_equal, A.mult, ["par", "pb"], ["mka"])
+        scan(T.bb[:], T.d0[:], T.d1[:], -HUGE, A.min, A.max, ["d0", "d1"], ["bb"])
+        act(T.sig[:], T.pcl[:, 0:C], F.Sign, ["pcl"], ["sig"])
+        act(T.val[:], T.sig[:], F.Sign, ["sig"] + pk(SC, SB), ["val"], bias=pc(SB), scale=pc(SC))
+        dma("g", T.val[:], T.idf[:], ["idf", "val"], ["val"], accum_op=A.add)
+        tt(slot(0, C), T.bb[:], T.pa[:, 0:C], A.is_ge, ["pa", "bb"], ["m0"])
+        for t in MID:
+            compare(t)
+        sign(0)
+        for k in range(1, len(ON_SCALAR)):
+            sign(k)
+            relu(k - 1)
+        relu(len(ON_SCALAR) - 1)
+        for k, t in enumerate(MID):
+            act(T.junk[:, C * k:C * k + 16 * t], slot(t, 16 * t), F.Identity, ["m%d" % t], ["junk%d" % k, "rs%d" % t],
+                acc=T.rs[:, t:t + 1])
+        if r == 0:
+            act(T.kx[:, 0:C - 1], T.eq[:, 1:C], F.Identity, ["eq"], ["kx"], bias=512.0, scale=-(BIG + 512.0))
+            col(OF, T.eq[:, 0:1], BIG, 0.0, ["eq"])
+            act(T.dec[:], T.dec0[:], F.Identity, ["dec0"] + pk(DD), ["dec"], bias=pc(DD))
+        for b in range(4):
+            act(fplane(b), T["pf%d" % b][:, 0:C], F.Copy, ["pf%d" % b], ["f%d" % b])
+        for t in (16, 15, 14, 13):
+            compare(t)
+        scan(T.rd[:], T.keep16[:], slot(0, C), 0.0, A.mult, A.add, ["keep16", "m0"], ["rd"])
+        qtile(2)
+        for t in (12, 11, 10, 9):
+            compare(t)
+        tt(T.w1[:], T.cst[:], T.rd[:, 15:C:16], A.subtract, ["cst", "rd"], ["w1"])
+        qtile(3)
+        for t in (8, 7, 6, 5, 4, 3, 2, 1):
+            compare(t)
+        qtile(0)
+        qtile(4)
+        qtile(5)
+        colsum(0, True, False)
+        for u in (2, 3, 4, 5):
+            colsum(u, False, False)
+        for b in range(4):
+            rows(b)
+        qtile(1)
+        colsum(1, False, True)
+        cp(T.rs[:, 1:17], T.rsc[:, 0:2560].indirect(T.roff[:, 0:1]), ["roff", "rsc0", "rsc1", "rsc2", "rsc3"],
+           ["rs%d" % t for t in range(1, 17)])
+        tt(T.kx[:, 15:C:16], T.w1[:], T.rs[:], A.subtract, ["w1", "kx"] + ["rs%d" % t for t in range(NT)], ["kx"])
+        scan(T.ext[:], T.pd[:, 0:C], T.kx[:], -HUGE, A.max, A.add, ["kx", "pd"], ["ext"])
+        ts(T.poff[:], T.ext[:, 15:C:16], pc(OF), None, A.add, None, ["ext"] + pk(OF), ["poff"])
+
+        cp(T.srt[:, 0:C].indirect(T.poff[:]), T.val[:], ["poff", "val"], ["srt"])
+        cp(T.srt[:, C:420], T.srt[:, 0:36], ["srt"], ["srt2"])
+        scan(T.scn[:], T.dec[:], T.srt[:], 0.0, A.add, A.max, ["dec", "srt", "srt2"], ["scn"])
+        tt(T.ab[:], T.scn[:, 23:420:12], T.mka[:], A.mult, ["scn", "mka"], ["ab"])
+        tt(T.bi[:], T.ab[:, 0:34:2], T.ab[:, 1:34:2], A.max, ["ab"], ["bi"])
+        ts(T.bj[:], T.bi[:], 511, None, A.bitwise_and, None, ["bi"], ["bj"])
+        ts(T.zoff[:, 0:17], T.bj[:], pc(BO), None, A.add, None, ["bj"] + pk(BO), ["zoff"])
+
+        ts(T.gz[:, 0:272], T.f0[:, 0:PW + C + 1].indirect(T.zoff[:, 0:17]), 0.25, None, A.mult, None,
+           ["zoff", "f0", "f2", "fz0", "fy0"], ["gz0"])
+        act(T.gz[:, 272:544], T.f1[:, 0:PW + C + 1].indirect(T.zoff[:, 0:17]), F.Identity,
+            ["zoff", "f1", "f3", "fz1", "fy1"], ["gz1"], scale=0.25)
+        if r == 0:
+            act(T.yt[:, 256:512], T.zt[:, 0:256], F.Copy, ["zt"], ["ytz"])
+        for e in range(2):
+            scan(T.zz[:, 272 * e:272 * e + 272], T.keep2[:], T.gz[:, 272 * e:272 * e + 272], 0.0,
+                 A.mult, A.add, ["keep2", "gz%d" % e], ["zz%d" % e])
+        for e in range(2):
+            tt(T.yt[:, e:256:2], T.zz[:, 272 * e + 1:272 * e + 256:2], T.zz[:, 272 * e + 9:272 * e + 264:2], A.add,
+               ["zz%d" % e], ["yt%d" % e])
+        quant(T.qy[:], T.sy[:], T.yt[:], ["yt0", "yt1", "ytz"], ["qy"])
+
+        order("g", ["qy"], [])
+        a = LAND[r]
+        g.remote_dma(T.ql[:, a:a + M].bitcast(dt.uint8), T.qy[:, 0:M].bitcast(dt.uint8), T.sem["arr%d" % r],
+                     T.sem["left%d" % r], pid, rid, mask)
+        g.remote_dma(T.sl[:, a:a + M], T.sy[:, 0:M], T.sem["arr%d" % r], T.sem["left%d" % r], pid, rid, mask)
+        count["left%d" % r] = 2 * lanes
+        note("g", ("left%d" % r, 2 * lanes), ["qy"], [])
+        wrote["land%d" % r] = ("arr%d" % r, 2 * lanes)
+
+        if r == 0:
+            pick_u(16, 24, ["uoff2"])
+            quant(T.ql[:, 64:192], T.sl[:, 64:192], T.zt[:], ["zt"], ["qlz0"])
+            quant(T.ql[:, 320:448], T.sl[:, 320:448], T.zt[:], ["zt"], ["qlz1"])
+            col(OG, pc(OF), 1.0, -5.5, pk(OF))
+            act(T.ax[:], T.eq[:], F.Identity, ["eq"], ["ax"], bias=512.0, scale=-(BIG + 512.0))
+            col(DCO, pb(BH), -1.0, pb(FL), ["pb"])
+            col(TS_, pb(BH), 1.0, pb(FL), ["pb"])
+            col(QM, pb(Q4), 2.0, 0.0, ["pb"])
+            col(QN, pb(Q4), 2.0, -2.0, ["pb"])
+            col(WK, pb(PI), 1.0, 1.0, ["pb"])
+            col(HH, pb(PI), -0.5, 1.0, ["pb"])
+            col(NO, pb(QQ), 512.0, -7680.0, ["pb"])
+            col(TA, pc(DCO), pb(CC), pb(BH), ["pb"] + pk(DCO))
+            col(AL, pc(HH), pc(SC), 0.0, pk(HH, SC))
+            col(TB, pc(TA), -1.0, pc(TS_), pk(TA, TS_))
+            col(CA, pc(TA), 1.0, pc(QM), pk(TA, QM))
+            col(X1, pc(AL), 1.0, pc(WK), pk(AL, WK))
+            col(CB, pc(TB), 1.0, pc(QN), pk(TB, QN))
+            col(GA, pc(X1), pc(NO), pc(HH), pk(X1, NO, HH))
+            col(CP, pc(TB), 1.0, pc(QM), pk(TB, QM))
+            col(DF, pc(CB), -1.0, pc(CA), pk(CA, CB))
+            act(pc(WR), pb(Q4), F.Relu, ["pb"], pk(WR), bias=1.0, scale=-1.0)
+            act(T.kd[:], T.k8[:], F.Sign, ["k8"], ["kd"])
+            col(DF0, pc(WR), -float(M), pc(DF), pk(WR, DF))
+            col(TH, pc(WR), -TINY, 0.0, pk(WR))
+            act(T.d8[:], T.kd[:], F.Identity, ["kd"], ["d8"], bias=-HUGE, scale=2 * HUGE)
+            act(T.ht[:, 256:512], T.zt[:, 0:256], F.Copy, ["zt"], ["htz"])
+        mm("pbk", C, UD[0], UD[1], T.qx[:], T.sx[:], ["qur16", "sur16", "qx"])
+        ts(tk(0), T.ext[:, 15:C:16], pc(OG), 1.0 / 12.0, A.add, A.mult, ["ext"] + pk(OG), ["tt0"])
+        ts(T.mo[:], T.pbk[:, 0:C], 0.0, None, A.is_gt, None, ["pbk"], ["mo"])
+        cp(T.ki[:], tk(0), ["tt0"], ["ki"])
+        scan(T.e1[:], T.ax[:], T.val[:], 0.0, A.add, A.max, ["ax", "val"], ["e1"])
+        ts(tk(2), T.ki[:], 4.0, None, A.mult, None, ["ki"], ["tt2"])
+        scan(T.e2[:], T.ax[:], T.mo[:], 0.0, A.add, A.max, ["ax", "mo"], ["e2"])
+        ts(tk(1), T.e1[:, 15:C:16], pc(AL), pc(GA), A.mult, A.add, ["e1"] + pk(AL, GA), ["tt1"])
+        ts(tk(4), T.e2[:, 15:C:16], pc(WK), None, A.mult, None, ["e2"] + pk(WK), ["tt4"])
+        tt(tk(3), tk(1), tk(2), A.add, ["tt1", "tt2"], ["tt3"])
+        if r == 0:
+            ts(T.tyi[:], T.t16[:, 8:16], 0.5, pc(CB), A.mult, A.add, ["t16"] + pk(CB), ["tyi"])
+        tt(tk(5), tk(3), tk(4), A.add, ["tt3", "tt4"], ["tt5"])
+        if r == 0:
+            ts(T.tyj[:], T.tyi[:], M - 1, None, A.bitwise_and, None, ["tyi"], ["tyj"])
+        cp(T.kj[:], tk(5), ["tt5"], ["kj"])
+        if r == 0:
+            ts(T.kd0[:, 0:M], T.k8[:, 0:M], pc(CA), 0.5, A.is_equal, A.subtract, ["k8"] + pk(CA), ["kd00"])
+            ts(T.kd0[:, M:128], T.k8[:, 0:M], pc(CP), 0.5, A.is_equal, A.subtract, ["k8"] + pk(CP), ["kd01"])
+            act(T.kd[:], T.kd0[:], F.Identity, ["kd00", "kd01"], ["kd"], scale=2 * HUGE)
+        cp(T.toff[:], T.kj[:], ["kj"], ["toff"])
+        if r == 1:
+            quant(T.qv[:], T.sv[:], T.vt[:], ["vt"], ["qv"])
+
+        w0 = VIEW[r]
+        o = LAND[r] - VIEW[r]
+        for b in (2, 0, 3, 1):
+            mm(RB[b], 128, T.qw[:, 128 * b:128 * b + 128], T.sw[:, 128 * b:128 * b + 128],
+               T.ql[:, w0:w0 + 128], T.sl[:, w0:w0 + 128], ["qw", "sw", "land%d" % r, "qlz0", "qlz1"])
+        for b in (2, 0, 3, 1):
+            src = T[RB[b]][:, o:o + M]
+            if b < 2:
+                ts(T.ht[:, b:256:4], src, 0.03125, None, A.mult, None, [RB[b]], ["ht%d" % b])
+            else:
+                act(T.ht[:, b:256:4], src, F.Identity, [RB[b]], ["ht%d" % b], scale=0.03125)
+        quant(T.qh[:], T.sh[:], T.ht[:], ["ht0", "ht1", "ht2", "ht3", "htz"], ["qh"])
+        mm("pcl", 128, US[0], US[1], T.qh[:], T.sh[:], UK + ["qh"])
+        for b in range(4):
+            act(T.hp[:, M * b:M * b + M], T.ht[:, b:256:4], F.Copy, ["ht%d" % b], ["hp%d" % b])
+
+        tt(T.vd[:, 0:M], T.pcl[:, 0:M], T.kd[:, 0:M], A.min, ["pcl", "kd"], ["vd0"])
+        tt(T.vd[:, M + 2:128], T.pcl[:, 0:M - 2], T.kd[:, M + 2:128], A.min, ["pcl", "kd"], ["vd1"])
+        tt(T.vd[:, M:M + 2], T.pcl[:, M - 2:M], T.kd[:, M:M + 2], A.min, ["pcl", "kd"], ["vd2"])
+        scan(T.vb[:], T.d8[:], T.vd[:], -HUGE, A.min, A.max, ["d8", "vd0", "vd1", "vd2"], ["vb"])
+        tt(T.n0[:], T.vb[:, 7:M:8], T.vb[:, M + 7:128:8], A.subtract, ["vb"], ["n0"])
+        ts(T.n1[:, 1:8], T.n0[:, 1:8], 0.0, pc(DF), A.is_gt, A.mult, ["n0"] + pk(DF), ["n1"])
+        ts(T.n1[:, 0:1], T.n0[:, 0:1], pc(TH), pc(DF0), A.is_gt, A.mult, ["n0"] + pk(TH, DF0), ["n10"])
+        tt(T.n2[:], T.n1[:], T.tyj[:], A.add, ["n1", "n10", "tyj"], ["n2"])
+        cp(T.noff[:], T.n2[:], ["n2"], ["noff"])
+        cp(T.hs[:, 0:128], T.hp[:, 0:M].indirect(T.noff[:]), ["hp0", "noff"], ["hs0"])
+        for b in (1, 3, 2):
+            act(T.hs[:, 128 * b:128 * b + 128], T.hp[:, M * b:M * b + M].indirect(T.noff[:]), F.Copy,
+                ["hp%d" % b, "noff"], ["hs%d" % b])
+            if b > 1:
+                n = C if b == 3 else CUT
+                act(T.hg[:, C * (b - 2):C * (b - 2) + n],
+                    T.hs[:, 128 * b:128 * b + 128].indirect(T.toff[:, 0:n // 16]), F.Copy,
+                    ["hs%d" % b, "toff"], ["hg%d" % b])
+        for b in range(2):
+            tt(T.xt[:, b:4 * C:4], T.hs[:, 128 * b:128 * b + 128].indirect(T.toff[:]), fplane(b), A.add,
+               ["hs%d" % b, "toff", "f%d" % b], ["xt%d" % b])
+        tt(T.xt[:, 3:4 * C:4], T.pf3[:, 0:C], T.hg[:, C:2 * C], A.add, ["hg3", "pf3"], ["xt3"])
+        tt(T.xt[:, 4 * CUT + 2:4 * C:4], T.hs[:, 256:384].indirect(T.toff[:, CUT // 16:NT]),
+           T.f0[:, PW + 1 + CUT:PW + 1 + C], A.add, ["hs2", "toff", "f2"], ["xt4"])
+        tt(T.xt[:, 2:4 * CUT:4], T.pf2[:, 0:CUT], T.hg[:, 0:CUT], A.add, ["hg2", "pf2"], ["xt2"])
+        if r == R - 1:
+            act(T.ids[:], T.idp[:, 0:M].indirect(T.noff[:]), F.Copy, ["idp", "noff"], ["ids"])
+            act(T.ndb[:], T.ids[:, 0:128].indirect(T.toff[:]), F.Copy, ["ids", "toff"], ["ndb"])
+            dma("s", T.nd[:], T.ndb[0:128:16, :], ["ndb"], [])
+        quant(T.qx[:], T.sx[:], T.xt[:], XK, ["qx"])
+
+    h = C // 2
+    mm("pa", h, T.qv[:], T.sv[:], T.qx[:, 0:h], T.sx[:, 0:h], ["qv", "qx"])
+    mm("pbk", h, T.qv[:], T.sv[:], T.qx[:, h:C], T.sx[:, h:C], ["qv", "qx"])
+    dma("y", T.oc[:], T.qx[:].bitcast(dt.uint8), ["qx"], [])
+    for k in range(4):
+        dma("g" if k < 2 else "y", T.osc[4 * k:4 * k + 4, :], T.sx[32 * k:32 * k + 4, :], ["qx"], [])
+    cp(T.ys[:, 0:h], T.pa[:, 0:h], ["pa"], ["ys0"])
+    act(T.ys[:, h:C], T.pbk[:, 0:h], F.Copy, ["pbk"], ["ys1"])
+    dma("y", T.y[:, 0:h], T.ys[:, 0:h], ["ys0"], [])
+    dma("s", T.y[:, h:C], T.ys[:, h:C], ["ys1"], [])
+    for s in sorted(count):
+        g.wait_ge(T.sem[s], count[s])

@@ -26,7 +26,7 @@ SCRATCH = {
     "xin": _s(4 * C, BF), "xt": _s(4 * C, BF), "qx": _s(C, X4), "sx": _s(C, U8),
     "ut": _s(512, BF), "qu": _s(128, X4), "su": _s(128, U8), "qur": _s(384, X4), "sur": _s(384, U8),
     "vt": _s(512, BF), "qv": _s(128, X4), "sv": _s(128, U8), "qw": _s(512, X4), "sw": _s(512, U8),
-    "pint": _s(1, I32), "ints": _s(8, I32), "pb": _s(8, F32), "pc": _s(32, F32), "t16": _s(NT, F32),
+    "pint": _s(1, I32), "ints": _s(8, I32), "pb": _s(8, F32), "pc": _s(40, F32), "t16": _s(NT, F32),
     "uoff": _s(NT, U16), "k16": _s(C, BF), "jp": _s(128, BF), "gcol": _s(128, BF), "r24": _s(432, BF),
     "idc": _s(C, F32), "idf": _s(C, F32), "keep2": _s(272, BF), "idp": _s(M, BF), "par": _s(34, BF),
     "eq": _s(C, BF), "kc": _s(C, BF), "d0": _s(C, BF), "ax": _s(C, BF), "keep16": _s(C, BF), "kx": _s(C, F32),
@@ -37,13 +37,13 @@ SCRATCH = {
     "sgn": _s(7 * C, BF), "junk": _s(2 * C, BF), "rs": _s(NT, F32), "rd": _s(C, BF), "w1": _s(NT, F32),
     "rsc": _s(2560, BF), "roff": _s(2, U16), "sig": _s(C, BF), "val": _s(C, F32),
     "ext": _s(C, F32), "poff": _s(NT, U16),
-    "srt": _s(420, F32), "scn": _s(420, F32), "ab": _s(34, F32), "bi": _s(17, I32), "bj": _s(17, I32),
+    "srt": _s(420, F32), "scn": _s(C, F32), "scw": _s(48, F32), "tq": _s(8, F32),
+    "ab": _s(34, F32), "bi": _s(17, I32), "bj": _s(17, I32),
     "zoff": _s(18, U16), "f0": _s(2 * PW, BF), "f1": _s(2 * PW, BF), "gz": _s(544, BF), "zz": _s(544, BF),
     "yt": _s(512, BF), "qy": _s(128, X4), "sy": _s(128, U8), "ql": _s(448, X4), "sl": _s(448, U8),
     "ht": _s(512, BF), "qh": _s(128, X4), "sh": _s(128, U8), "hp": _s(256, BF), "hs": _s(512, BF),
     "hg": _s(2 * C, BF), "vd": _s(128, F32), "vb": _s(128, F32), "k8": _s(128, BF), "kd0": _s(128, BF),
-    "kd": _s(128, BF), "d8": _s(128, BF), "n0": _s(8, F32), "n1": _s(8, F32), "n2": _s(8, F32), "noff": _s(8, U16),
-    "tyi": _s(8, I32), "tyj": _s(8, I32),
+    "kd": _s(128, BF), "d8": _s(128, BF), "n0": _s(8, F32), "n1": _s(8, F32), "noff": _s(8, U16),
     "mo": _s(C, BF), "e1": _s(C, F32), "e2": _s(C, F32), "tt": _s(6 * NT, F32), "ki": _s(NT, I32),
     "kj": _s(NT, I32), "toff": _s(NT, U16), "ids": _s(128, BF), "ndb": _s(C, F32), "ys": _s(C, F32),
 }
@@ -169,7 +169,7 @@ def rank_program(g, core, T, topo):
     QQ, PI, CC, BH, FL, GG, Q4 = range(7)
     SC, SB, BO, DD, P12, CQ, NO, Z0 = range(8)
     DCO, TA, TS_, TB, CA, QM, CB, WK, HH, AL, X1, GA = range(8, 20)
-    R1, R2, R3, R4, QN, OF, OG, CP, DF, DF0, WR, TH = range(20, 32)
+    R1, R2, R3, R4, QN, OF, OG, CP, DF, DF0, WR, TH, B0, B1, RC = range(20, 35)
 
     dma("s", T.ut[:], T.u[:], [], ["ut"])
     dma("y", T.xin[:], T.x[:], [], ["xin"])
@@ -215,7 +215,6 @@ def rank_program(g, core, T, topo):
     for u in range(2, 6):
         a = START[u] - START[2]
         iota(T.keepr[:, a:a + 1], [[0, 1]], 0, 0, ["keepr"], ["keepr%d" % u])
-    iota(T.rs[:, 0:1], [[0, 1]], 0, 0, [], ["rs0"])
     quant(T.qu[:], T.su[:], T.ut[:], ["ut"], ["qu"])
 
     def pick_u(a, b, names):
@@ -238,10 +237,16 @@ def rank_program(g, core, T, topo):
     for h in range(2):
         ts(T.et[:, 520 * h + 2 + h:520 * h + 514 + h:4], T.jp[:], 0.0, None, A.is_equal, None, ["jp"], ["et%d" % h])
     quant(T.qg[:], T.sg[:], T.gt[:], ["gt%d" % b for b in range(4)], ["qg"])
-    for b in range(4):
+
+    def quant_e(b):
         o = 520 * (b % 2) + 2 - 2 * (b // 2)
         quant(T.qe[:, 128 * b:128 * b + 128], T.se[:, 128 * b:128 * b + 128], T.et[:, o:o + 512],
               ["et%d" % (b % 2)], ["qe%d" % b])
+
+    quant_e(0)
+    quant_e(1)
+    act(T.kx[:, 0:C - 1], T.eq[:, 1:C], F.Identity, ["eq"], ["kx"], bias=512.0, scale=-(BIG + 512.0))
+    col(OF, T.eq[:, 0:1], BIG, 0.0, ["eq"])
 
     dma("y", T.qw[:].bitcast(dt.uint8), T.wc[:], ["xin"], ["qw"])
     dma("y", T.sw[:], T.ws[:], [], ["sw"])
@@ -251,8 +256,9 @@ def rank_program(g, core, T, topo):
     UC = (T.qur[:, 128:256], T.sur[:, 128:256])
     UD = (T.qur[:, 256:384], T.sur[:, 256:384])
     UK = ["qur0", "sur0"]
+    QX = ["qx", "qx2"]
+    NK = ["noff", "noff0"]
     RB = ["pa", "pd", "pf0", "pf1"]
-    XK = ["xt0", "xt1", "xt2", "xt3", "xt4"]
 
     def fplane(b):
         return T["f%d" % (b % 2)][:, PW * (b // 2) + 1:PW * (b // 2) + 1 + C]
@@ -275,11 +281,12 @@ def rank_program(g, core, T, topo):
         return T.bb[:, 16 * t + 15:16 * t + 16]
 
     def compare(t):
-        ts(slot(t, 16 * t), T.pa[:, 0:16 * t], own(t), None, A.is_lt, None, ["pa", "bb"], ["m%d" % t])
+        ts(slot(t, 16 * t), T.pa[:, 0:16 * t], own(t), None, A.is_lt, None, ["pa", "bb%d" % (16 * t // CUT)],
+           ["m%d" % t])
 
     def sign(k):
         t = ON_SCALAR[k]
-        act(T.sgn[:, C * k:C * k + 16 * t], T.pbk[:, 0:16 * t], F.Sign, ["pbk", "bb"], ["sgn%d" % k],
+        act(T.sgn[:, C * k:C * k + 16 * t], T.pbk[:, 0:16 * t], F.Sign, ["pbk", "bb1"], ["sgn%d" % k],
             bias=own(t), scale=-1.0)
 
     def relu(k):
@@ -289,36 +296,41 @@ def rank_program(g, core, T, topo):
 
     def rows(b):
         a = 4 * START[2] + b
-        scan(T.rsc[:, 640 * b:640 * b + 640], T.keepr[:], T.mt[:, a:a + 4 * 640 - 3:4], 0.0, A.mult, A.add,
+        scan(T.rsc[:, 640 * b:640 * b + 640], T.keepr[:], T.mt[:, a:a + 4 * 640 - 3:4], 0.0, A.mult, A.subtract,
              ["keepr%d" % u for u in range(2, 6)] + ["m%d" % SLOTS[u][b] for u in range(2, 6)], ["rsc%d" % b])
 
     def tk(k):
         return T.tt[:, NT * k:NT * k + NT]
 
-    quant(T.qx[:], T.sx[:], T.xin[:], ["xin"], ["qx"])
+    quant(T.qx[:, CUT:C], T.sx[:, CUT:C], T.xin[:, 4 * CUT:4 * C], ["xin"], ["qx2"])
+    quant(T.qx[:, 0:CUT], T.sx[:, 0:CUT], T.xin[:, 0:4 * CUT], ["xin"], ["qx"])
     for r in range(R):
-        mm("pa", C, US[0], US[1], T.qx[:], T.sx[:], UK + ["qx"])
-        mm("pcl", C, UC[0], UC[1], T.qx[:], T.sx[:], UK + ["qx"])
-        mm("pbk", C, US[0], US[1], T.qx[:], T.sx[:], UK + ["qx"])
-        for b in range(4):
-            mm("pf%d" % b, C, T.qe[:, 128 * b:128 * b + 128], T.se[:, 128 * b:128 * b + 128], T.qx[:], T.sx[:],
-               ["qe%d" % b, "qx"])
+        mm("pd", C - CUT, US[0], US[1], T.qx[:, CUT:C], T.sx[:, CUT:C], UK + ["qx2"])
+        mm("pcl", C, UC[0], UC[1], T.qx[:], T.sx[:], UK + QX)
+        mm("pa", C, US[0], US[1], T.qx[:], T.sx[:], UK + QX)
+        mm("pbk", C, US[0], US[1], T.qx[:], T.sx[:], UK + QX)
+        tt(T.d1[:, CUT:C], T.pd[:, 0:C - CUT], T.kc[:, CUT:C], A.min, ["pd", "kc"], ["d11"])
         if r == 0:
             ts(T.dec0[:], T.r24[:, 0:420], pc(P12), -4.0, A.is_equal, A.mult, ["r24"] + pk(P12), ["dec0"])
+            quant_e(2)
+            quant_e(3)
             cp(T.roff[:, 0:1], pc(R4), pk(R4), ["roff"])
             ts(T.cst[:], T.t16[:], pc(Z0), None, A.add, None, ["t16"] + pk(Z0), ["cst"])
+        for b in range(4):
+            mm("pf%d" % b, C, T.qe[:, 128 * b:128 * b + 128], T.se[:, 128 * b:128 * b + 128], T.qx[:], T.sx[:],
+               ["qe%d" % b] + QX)
 
-        tt(T.d1[:], T.pa[:, 0:C], T.kc[:], A.min, ["pa", "kc"], ["d1"])
-        if r == 0:
-            ts(T.mka[:], T.par[:], pb(PI), 2.0 ** 21, A.is_equal, A.mult, ["par", "pb"], ["mka"])
-        scan(T.bb[:], T.d0[:], T.d1[:], -HUGE, A.min, A.max, ["d0", "d1"], ["bb"])
-        act(T.sig[:], T.pcl[:, 0:C], F.Sign, ["pcl"], ["sig"])
-        act(T.val[:], T.sig[:], F.Sign, ["sig"] + pk(SC, SB), ["val"], bias=pc(SB), scale=pc(SC))
-        dma("g", T.val[:], T.idf[:], ["idf", "val"], ["val"], accum_op=A.add)
-        tt(slot(0, C), T.bb[:], T.pa[:, 0:C], A.is_ge, ["pa", "bb"], ["m0"])
+        scan(T.bb[:, CUT:C], T.d0[:, CUT:C], T.d1[:, CUT:C], -HUGE, A.min, A.max, ["d0", "d11"], ["bb1"])
+        tt(T.d1[:, 0:CUT], T.pa[:, 0:CUT], T.kc[:, 0:CUT], A.min, ["pa", "kc"], ["d10"])
         for t in MID:
             compare(t)
+        scan(T.bb[:, 0:CUT], T.d0[:, 0:CUT], T.d1[:, 0:CUT], -HUGE, A.min, A.max, ["d0", "d10"], ["bb0"])
+        compare(16)
+        tt(slot(0, C), T.bb[:], T.pa[:, 0:C], A.is_ge, ["pa", "bb0", "bb1"], ["m0"])
+        act(T.sig[:], T.pcl[:, 0:C], F.Sign, ["pcl"], ["sig"])
         sign(0)
+        act(T.val[:], T.sig[:], F.Sign, ["sig"] + pk(SC, SB), ["val"], bias=pc(SB), scale=pc(SC))
+        dma("g", T.val[:], T.idf[:], ["idf", "val"], ["val"], accum_op=A.add)
         for k in range(1, len(ON_SCALAR)):
             sign(k)
             relu(k - 1)
@@ -327,20 +339,18 @@ def rank_program(g, core, T, topo):
             act(T.junk[:, C * k:C * k + 16 * t], slot(t, 16 * t), F.Identity, ["m%d" % t], ["junk%d" % k, "rs%d" % t],
                 acc=T.rs[:, t:t + 1])
         if r == 0:
-            act(T.kx[:, 0:C - 1], T.eq[:, 1:C], F.Identity, ["eq"], ["kx"], bias=512.0, scale=-(BIG + 512.0))
-            col(OF, T.eq[:, 0:1], BIG, 0.0, ["eq"])
             act(T.dec[:], T.dec0[:], F.Identity, ["dec0"] + pk(DD), ["dec"], bias=pc(DD))
         for b in range(4):
             act(fplane(b), T["pf%d" % b][:, 0:C], F.Copy, ["pf%d" % b], ["f%d" % b])
-        for t in (16, 15, 14, 13):
+        for t in (15, 14, 13, 12):
             compare(t)
         scan(T.rd[:], T.keep16[:], slot(0, C), 0.0, A.mult, A.add, ["keep16", "m0"], ["rd"])
         qtile(2)
-        for t in (12, 11, 10, 9):
+        for t in (11, 10, 9, 8, 7):
             compare(t)
         tt(T.w1[:], T.cst[:], T.rd[:, 15:C:16], A.subtract, ["cst", "rd"], ["w1"])
         qtile(3)
-        for t in (8, 7, 6, 5, 4, 3, 2, 1):
+        for t in (6, 5, 4, 3, 2, 1):
             compare(t)
         qtile(0)
         qtile(4)
@@ -348,21 +358,28 @@ def rank_program(g, core, T, topo):
         colsum(0, True, False)
         for u in (2, 3, 4, 5):
             colsum(u, False, False)
-        for b in range(4):
+        for b in range(3):
             rows(b)
+        cp(T.kx[:, 15:16], T.w1[:, 0:1], ["w1", "kx"], ["kx0"])
+        if r == 0:
+            ts(T.mka[:], T.par[:], pb(PI), 2.0 ** 21, A.is_equal, A.mult, ["par", "pb"], ["mka"])
         qtile(1)
         colsum(1, False, True)
-        cp(T.rs[:, 1:17], T.rsc[:, 0:2560].indirect(T.roff[:, 0:1]), ["roff", "rsc0", "rsc1", "rsc2", "rsc3"],
-           ["rs%d" % t for t in range(1, 17)])
-        tt(T.kx[:, 15:C:16], T.w1[:], T.rs[:], A.subtract, ["w1", "kx"] + ["rs%d" % t for t in range(NT)], ["kx"])
-        scan(T.ext[:], T.pd[:, 0:C], T.kx[:], -HUGE, A.max, A.add, ["kx", "pd"], ["ext"])
+        rows(3)
+        tt(T.kx[:, 287:C:16], T.w1[:, 17:NT], T.rs[:, 17:NT], A.subtract,
+           ["w1", "kx"] + ["rs%d" % t for t in range(17, NT)], ["kx2"])
+        tt(T.kx[:, 31:272:16], T.rsc[:, 0:2560].indirect(T.roff[:, 0:1]), T.w1[:, 1:17], A.add,
+           ["roff", "w1", "kx", "rsc0", "rsc1", "rsc2", "rsc3"], ["kx1"])
+        scan(T.ext[:], T.pd[:, 0:C], T.kx[:], -HUGE, A.max, A.add, ["kx", "kx0", "kx1", "kx2", "pd"], ["ext"])
         ts(T.poff[:], T.ext[:, 15:C:16], pc(OF), None, A.add, None, ["ext"] + pk(OF), ["poff"])
 
         cp(T.srt[:, 0:C].indirect(T.poff[:]), T.val[:], ["poff", "val"], ["srt"])
         cp(T.srt[:, C:420], T.srt[:, 0:36], ["srt"], ["srt2"])
-        scan(T.scn[:], T.dec[:], T.srt[:], 0.0, A.add, A.max, ["dec", "srt", "srt2"], ["scn"])
-        tt(T.ab[:], T.scn[:, 23:420:12], T.mka[:], A.mult, ["scn", "mka"], ["ab"])
-        tt(T.bi[:], T.ab[:, 0:34:2], T.ab[:, 1:34:2], A.max, ["ab"], ["bi"])
+        scan(T.scn[:, 0:C], T.dec[:, 0:C], T.srt[:, 0:C], 0.0, A.add, A.max, ["dec", "srt"], ["scn"])
+        scan(T.scw[:], T.dec[:, 372:420], T.srt[:, 372:420], 0.0, A.add, A.max, ["dec", "srt", "srt2"], ["scw"])
+        tt(T.ab[:, 0:31], T.scn[:, 23:C:12], T.mka[:, 0:31], A.mult, ["scn", "mka"], ["ab"])
+        tt(T.ab[:, 31:34], T.scw[:, 23:48:12], T.mka[:, 31:34], A.mult, ["scw", "mka"], ["ab2"])
+        tt(T.bi[:], T.ab[:, 0:34:2], T.ab[:, 1:34:2], A.max, ["ab", "ab2"], ["bi"])
         ts(T.bj[:], T.bi[:], 511, None, A.bitwise_and, None, ["bi"], ["bj"])
         ts(T.zoff[:, 0:17], T.bj[:], pc(BO), None, A.add, None, ["bj"] + pk(BO), ["zoff"])
 
@@ -404,20 +421,22 @@ def rank_program(g, core, T, topo):
             col(NO, pb(QQ), 512.0, -7680.0, ["pb"])
             col(TA, pc(DCO), pb(CC), pb(BH), ["pb"] + pk(DCO))
             col(AL, pc(HH), pc(SC), 0.0, pk(HH, SC))
+            act(pc(WR), pb(Q4), F.Relu, ["pb"], pk(WR), bias=1.0, scale=-1.0)
+            act(T.kd[:], T.k8[:], F.Sign, ["k8"], ["kd"])
             col(TB, pc(TA), -1.0, pc(TS_), pk(TA, TS_))
             col(CA, pc(TA), 1.0, pc(QM), pk(TA, QM))
             col(X1, pc(AL), 1.0, pc(WK), pk(AL, WK))
-            col(CB, pc(TB), 1.0, pc(QN), pk(TB, QN))
-            col(GA, pc(X1), pc(NO), pc(HH), pk(X1, NO, HH))
-            col(CP, pc(TB), 1.0, pc(QM), pk(TB, QM))
-            col(DF, pc(CB), -1.0, pc(CA), pk(CA, CB))
-            act(pc(WR), pb(Q4), F.Relu, ["pb"], pk(WR), bias=1.0, scale=-1.0)
-            act(T.kd[:], T.k8[:], F.Sign, ["k8"], ["kd"])
-            col(DF0, pc(WR), -float(M), pc(DF), pk(WR, DF))
             col(TH, pc(WR), -TINY, 0.0, pk(WR))
+            col(CB, pc(TB), 1.0, pc(QN), pk(TB, QN))
+            col(CP, pc(TB), 1.0, pc(QM), pk(TB, QM))
+            col(GA, pc(X1), pc(NO), pc(HH), pk(X1, NO, HH))
             act(T.d8[:], T.kd[:], F.Identity, ["kd"], ["d8"], bias=-HUGE, scale=2 * HUGE)
+            col(DF, pc(CB), -1.0, pc(CA), pk(CA, CB))
+            col(B1, pc(CB), 1.0, 0.25, pk(CB))
             act(T.ht[:, 256:512], T.zt[:, 0:256], F.Copy, ["zt"], ["htz"])
-        mm("pbk", C, UD[0], UD[1], T.qx[:], T.sx[:], ["qur16", "sur16", "qx"])
+            col(DF0, pc(WR), -float(M), pc(DF), pk(WR, DF))
+            col(B0, pc(WR), float(M), pc(B1), pk(WR, B1))
+        mm("pbk", C, UD[0], UD[1], T.qx[:], T.sx[:], ["qur16", "sur16"] + QX)
         ts(tk(0), T.ext[:, 15:C:16], pc(OG), 1.0 / 12.0, A.add, A.mult, ["ext"] + pk(OG), ["tt0"])
         ts(T.mo[:], T.pbk[:, 0:C], 0.0, None, A.is_gt, None, ["pbk"], ["mo"])
         cp(T.ki[:], tk(0), ["tt0"], ["ki"])
@@ -428,18 +447,18 @@ def rank_program(g, core, T, topo):
         ts(tk(4), T.e2[:, 15:C:16], pc(WK), None, A.mult, None, ["e2"] + pk(WK), ["tt4"])
         tt(tk(3), tk(1), tk(2), A.add, ["tt1", "tt2"], ["tt3"])
         if r == 0:
-            ts(T.tyi[:], T.t16[:, 8:16], 0.5, pc(CB), A.mult, A.add, ["t16"] + pk(CB), ["tyi"])
+            op("v", pk(DF), pk(RC), lambda: V.reciprocal(pc(RC), pc(DF)))
         tt(tk(5), tk(3), tk(4), A.add, ["tt3", "tt4"], ["tt5"])
-        if r == 0:
-            ts(T.tyj[:], T.tyi[:], M - 1, None, A.bitwise_and, None, ["tyi"], ["tyj"])
-        cp(T.kj[:], tk(5), ["tt5"], ["kj"])
         if r == 0:
             ts(T.kd0[:, 0:M], T.k8[:, 0:M], pc(CA), 0.5, A.is_equal, A.subtract, ["k8"] + pk(CA), ["kd00"])
             ts(T.kd0[:, M:128], T.k8[:, 0:M], pc(CP), 0.5, A.is_equal, A.subtract, ["k8"] + pk(CP), ["kd01"])
             act(T.kd[:], T.kd0[:], F.Identity, ["kd00", "kd01"], ["kd"], scale=2 * HUGE)
-        cp(T.toff[:], T.kj[:], ["kj"], ["toff"])
+        cp(T.kj[:], tk(5), ["tt5"], ["kj"])
+        if r == 0:
+            ts(T.tq[:], T.t16[:, 0:8], 0.5, pc(RC), A.mult, A.mult, ["t16"] + pk(RC), ["tq"])
         if r == 1:
             quant(T.qv[:], T.sv[:], T.vt[:], ["vt"], ["qv"])
+        cp(T.toff[:], T.kj[:], ["kj"], ["toff"])
 
         w0 = VIEW[r]
         o = LAND[r] - VIEW[r]
@@ -460,43 +479,45 @@ def rank_program(g, core, T, topo):
         tt(T.vd[:, 0:M], T.pcl[:, 0:M], T.kd[:, 0:M], A.min, ["pcl", "kd"], ["vd0"])
         tt(T.vd[:, M + 2:128], T.pcl[:, 0:M - 2], T.kd[:, M + 2:128], A.min, ["pcl", "kd"], ["vd1"])
         tt(T.vd[:, M:M + 2], T.pcl[:, M - 2:M], T.kd[:, M:M + 2], A.min, ["pcl", "kd"], ["vd2"])
-        scan(T.vb[:], T.d8[:], T.vd[:], -HUGE, A.min, A.max, ["d8", "vd0", "vd1", "vd2"], ["vb"])
-        tt(T.n0[:], T.vb[:, 7:M:8], T.vb[:, M + 7:128:8], A.subtract, ["vb"], ["n0"])
-        ts(T.n1[:, 1:8], T.n0[:, 1:8], 0.0, pc(DF), A.is_gt, A.mult, ["n0"] + pk(DF), ["n1"])
-        ts(T.n1[:, 0:1], T.n0[:, 0:1], pc(TH), pc(DF0), A.is_gt, A.mult, ["n0"] + pk(TH, DF0), ["n10"])
-        tt(T.n2[:], T.n1[:], T.tyj[:], A.add, ["n1", "n10", "tyj"], ["n2"])
-        cp(T.noff[:], T.n2[:], ["n2"], ["noff"])
-        cp(T.hs[:, 0:128], T.hp[:, 0:M].indirect(T.noff[:]), ["hp0", "noff"], ["hs0"])
+        scan(T.vb[:, 0:M], T.d8[:, 0:M], T.vd[:, 0:M], -HUGE, A.min, A.max, ["d8", "vd0"], ["vb0"])
+        scan(T.vb[:, M:128], T.d8[:, 0:M], T.vd[:, M:128], -HUGE, A.min, A.max, ["d8", "vd1", "vd2"], ["vb1"])
+        tt(T.n0[:, 1:8], T.vb[:, 15:M:8], T.vb[:, M + 15:128:8], A.is_gt, ["vb0", "vb1"], ["n0"])
+        ts(T.n0[:, 0:1], T.vb[:, 7:8], T.vb[:, M + 7:M + 8], pc(TH), A.subtract, A.is_gt, ["vb0", "vb1"] + pk(TH),
+           ["n00"])
+        tt(T.n1[:, 1:8], T.n0[:, 1:8], T.tq[:, 1:8], A.add, ["n0", "tq"], ["n1"])
+        ts(T.noff[:, 0:1], T.n0[:, 0:1], pc(DF0), pc(B0), A.mult, A.add, ["n00"] + pk(DF0, B0), ["noff0"])
+        ts(T.noff[:, 1:8], T.n1[:, 1:8], pc(DF), pc(B1), A.mult, A.add, ["n1"] + pk(DF, B1), ["noff"])
+        cp(T.hs[:, 0:128], T.hp[:, 0:M].indirect(T.noff[:]), ["hp0"] + NK, ["hs0"])
         for b in (1, 3, 2):
             act(T.hs[:, 128 * b:128 * b + 128], T.hp[:, M * b:M * b + M].indirect(T.noff[:]), F.Copy,
-                ["hp%d" % b, "noff"], ["hs%d" % b])
-            if b > 1:
-                n = C if b == 3 else CUT
-                act(T.hg[:, C * (b - 2):C * (b - 2) + n],
-                    T.hs[:, 128 * b:128 * b + 128].indirect(T.toff[:, 0:n // 16]), F.Copy,
-                    ["hs%d" % b, "toff"], ["hg%d" % b])
+                ["hp%d" % b] + NK, ["hs%d" % b])
+        for b, n in ((3, C), (2, CUT)):
+            act(T.hg[:, C * (b - 2):C * (b - 2) + n], T.hs[:, 128 * b:128 * b + 128].indirect(T.toff[:, 0:n // 16]),
+                F.Copy, ["hs%d" % b, "toff"], ["hg%d" % b])
         for b in range(2):
             tt(T.xt[:, b:4 * C:4], T.hs[:, 128 * b:128 * b + 128].indirect(T.toff[:]), fplane(b), A.add,
                ["hs%d" % b, "toff", "f%d" % b], ["xt%d" % b])
-        tt(T.xt[:, 3:4 * C:4], T.pf3[:, 0:C], T.hg[:, C:2 * C], A.add, ["hg3", "pf3"], ["xt3"])
         tt(T.xt[:, 4 * CUT + 2:4 * C:4], T.hs[:, 256:384].indirect(T.toff[:, CUT // 16:NT]),
            T.f0[:, PW + 1 + CUT:PW + 1 + C], A.add, ["hs2", "toff", "f2"], ["xt4"])
+        tt(T.xt[:, 3:4 * C:4], T.pf3[:, 0:C], T.hg[:, C:2 * C], A.add, ["hg3", "pf3"], ["xt3"])
         tt(T.xt[:, 2:4 * CUT:4], T.pf2[:, 0:CUT], T.hg[:, 0:CUT], A.add, ["hg2", "pf2"], ["xt2"])
         if r == R - 1:
-            act(T.ids[:], T.idp[:, 0:M].indirect(T.noff[:]), F.Copy, ["idp", "noff"], ["ids"])
+            act(T.ids[:], T.idp[:, 0:M].indirect(T.noff[:]), F.Copy, ["idp"] + NK, ["ids"])
             act(T.ndb[:], T.ids[:, 0:128].indirect(T.toff[:]), F.Copy, ["ids", "toff"], ["ndb"])
-            dma("s", T.nd[:], T.ndb[0:128:16, :], ["ndb"], [])
-        quant(T.qx[:], T.sx[:], T.xt[:], XK, ["qx"])
+        quant(T.qx[:, CUT:C], T.sx[:, CUT:C], T.xt[:, 4 * CUT:4 * C], ["xt0", "xt1", "xt3", "xt4"], ["qx2"])
+        quant(T.qx[:, 0:CUT], T.sx[:, 0:CUT], T.xt[:, 0:4 * CUT], ["xt0", "xt1", "xt2", "xt3"], ["qx"])
 
-    h = C // 2
-    mm("pa", h, T.qv[:], T.sv[:], T.qx[:, 0:h], T.sx[:, 0:h], ["qv", "qx"])
-    mm("pbk", h, T.qv[:], T.sv[:], T.qx[:, h:C], T.sx[:, h:C], ["qv", "qx"])
-    dma("y", T.oc[:], T.qx[:].bitcast(dt.uint8), ["qx"], [])
+    mm("pbk", C - CUT, T.qv[:], T.sv[:], T.qx[:, CUT:C], T.sx[:, CUT:C], ["qv", "qx2"])
+    mm("pa", 128, T.qv[:], T.sv[:], T.qx[:, 0:128], T.sx[:, 0:128], ["qv", "qx"])
+    mm("pd", 128, T.qv[:], T.sv[:], T.qx[:, 128:CUT], T.sx[:, 128:CUT], ["qv", "qx"])
+    dma("y", T.oc[:], T.qx[:].bitcast(dt.uint8), QX, [])
     for k in range(4):
-        dma("g" if k < 2 else "y", T.osc[4 * k:4 * k + 4, :], T.sx[32 * k:32 * k + 4, :], ["qx"], [])
-    cp(T.ys[:, 0:h], T.pa[:, 0:h], ["pa"], ["ys0"])
-    act(T.ys[:, h:C], T.pbk[:, 0:h], F.Copy, ["pbk"], ["ys1"])
-    dma("y", T.y[:, 0:h], T.ys[:, 0:h], ["ys0"], [])
-    dma("s", T.y[:, h:C], T.ys[:, h:C], ["ys1"], [])
+        dma("g" if k < 2 else "y", T.osc[4 * k:4 * k + 4, :], T.sx[32 * k:32 * k + 4, :], QX, [])
+    cp(T.ys[:, CUT:C], T.pbk[:, 0:C - CUT], ["pbk"], ["ys2"])
+    act(T.ys[:, 0:128], T.pa[:, 0:128], F.Copy, ["pa"], ["ys0"])
+    cp(T.ys[:, 128:CUT], T.pd[:, 0:128], ["pd"], ["ys1"])
+    dma("y", T.y[:, 128:C], T.ys[:, 128:C], ["ys1", "ys2"], [])
+    dma("s", T.y[:, 0:128], T.ys[:, 0:128], ["ys0"], [])
+    dma("s", T.nd[:], T.ndb[0:128:16, :], ["ndb"], [])
     for s in sorted(count):
         g.wait_ge(T.sem[s], count[s])

@@ -1,15 +1,26 @@
-from concourse.mybir import dt, AluOpType as A, ActivationFunctionType as F
+from concourse.mybir import dt, AluOpType as A, ActivationFunctionType as F, AxisListType
 
 C, NT, M, R = 384, 24, 64, 3
 HUGE = 2.0 ** 80
 BIG = 2.0 ** 20
-TINY = 2.0 ** -126
+TINY = 2.0 ** -120
+FOUR = 1.5 * 2.0 ** 25
 PW = 400
-SLOTS = [[0, 23, 22, 21], [20, 19, 18, 17], [16, 15, 14, 13], [12, 11, 10, 9], [8, 7, 6, 5], [4, 3, 2, 1]]
-WIDTH = [384, 320, 256, 192, 128, 128]
-START = [0, 384, 704, 960, 1152, 1280]
-ON_SCALAR = [23, 22, 21, 20, 19, 18]
-MID = [17]
+NEAR = 7
+SLOTS = [["d1", "d0", "d3", "d2"], ["d5", "d4", "d7", "d6"], [15, 14, 13, 12], [20, 21, 22, 23], [16, 17, 18, 19]]
+EARLY = [0, 1, 2, 3]
+WIDTH = [400, 320, 192, 256, 192]
+ORIGIN = [0, 80]
+START = [0, 400, 720, 912, 1168]
+QSTART = [0, 528, 848, 1040, 1296]
+BLANK = [(0, 0, 48), (1, 0, 32), (0, 384, 400), (1, 304, 320), (2, 80, 176), (3, 208, 256), (4, 144, 192)]
+PAIRS = [(0, 4, 0, 64), (4, 8, 16, 64), (8, 12, 0, 112), (12, 24, 16, 192)]
+PART = [(0, 128), (128, 256), (256, 384)]
+ON_SCALAR = [15, 14, 13, 23, 22, 21, 20, 19, 18, 17, 16]
+ON_VECTOR = [12, 0, 1, 2, 3]
+COLOUR_AT = 3
+SCAN = [(0, 204), (180, 420)]
+HALF = [(0, 8), (8, 17)]
 CUT = 256
 LAND = [0, 192, 256]
 VIEW = [0, 128, 256]
@@ -28,28 +39,28 @@ SCRATCH = {
     "vt": _s(512, BF), "qv": _s(128, X4), "sv": _s(128, U8), "qw": _s(512, X4), "sw": _s(512, U8),
     "pint": _s(1, I32), "ints": _s(8, I32), "pb": _s(8, F32), "pc": _s(40, F32), "t16": _s(NT, F32),
     "uoff": _s(NT, U16), "k16": _s(C, BF), "jp": _s(128, BF), "gcol": _s(128, BF), "r24": _s(432, BF),
-    "idc": _s(C, F32), "idf": _s(C, F32), "keep2": _s(272, BF), "idp": _s(M, BF), "par": _s(34, BF),
-    "eq": _s(C, BF), "kc": _s(C, BF), "d0": _s(C, BF), "ax": _s(C, BF), "keep16": _s(C, BF), "kx": _s(C, F32),
-    "dec0": _s(420, BF), "dec": _s(420, BF), "mka": _s(34, F32), "cst": _s(NT, F32), "keepr": _s(640, BF),
-    "et": _s(1040, BF), "qe": _s(512, X4), "se": _s(512, U8),
-    "gt": _s(512, BF), "qg": _s(128, X4), "sg": _s(128, U8), "zt": _s(512, BF),
-    "d1": _s(C, F32), "bb": _s(C, F32), "mt": _s(4 * 1408, BF), "qm": _s(1408, X4), "sm": _s(1408, U8),
-    "sgn": _s(7 * C, BF), "junk": _s(2 * C, BF), "rs": _s(NT, F32), "rd": _s(C, BF), "w1": _s(NT, F32),
-    "rsc": _s(2560, BF), "roff": _s(2, U16), "sig": _s(C, BF), "val": _s(C, F32),
+    "idc": _s(C, F32), "idf": _s(C, F32), "keep2": _s(144, BF), "idp": _s(M, BF), "par": _s(34, BF),
+    "eq": _s(C, BF), "kc": _s(128, BF), "d0": _s(128, BF), "ax": _s(C, BF), "keep16": _s(C, BF), "kx": _s(C, F32),
+    "dec0": _s(420, BF), "dec": _s(420, BF), "mka": _s(34, F32), "cst": _s(NT, F32),
+    "et": _s(1040, BF), "qe": _s(768, X4), "se": _s(768, U8),
+    "gt": _s(516, BF), "qg": _s(384, X4), "sg": _s(384, U8), "zt": _s(512, BF),
+    "d1": _s(C, F32), "bb": _s(C, F32), "o16": _s(C, F32),
+    "mt": _s(4 * 1424, BF), "qm": _s(1552, X4), "sm": _s(1552, U8),
+    "sgn": _s(2400, BF), "rs": _s(NT, F32), "rb": _s(C, F32), "w1": _s(NT, F32), "val": _s(C, F32),
     "ext": _s(C, F32), "poff": _s(NT, U16),
-    "srt": _s(420, F32), "scn": _s(C, F32), "scw": _s(48, F32), "tq": _s(8, F32),
+    "srt": _s(420, F32), "scn": _s(444, F32), "tq": _s(8, F32),
     "ab": _s(34, F32), "bi": _s(17, I32), "bj": _s(17, I32),
     "zoff": _s(18, U16), "f0": _s(2 * PW, BF), "f1": _s(2 * PW, BF), "gz": _s(544, BF), "zz": _s(544, BF),
     "yt": _s(512, BF), "qy": _s(128, X4), "sy": _s(128, U8), "ql": _s(448, X4), "sl": _s(448, U8),
     "ht": _s(512, BF), "qh": _s(128, X4), "sh": _s(128, U8), "hp": _s(256, BF), "hs": _s(512, BF),
-    "hg": _s(2 * C, BF), "vd": _s(128, F32), "vb": _s(128, F32), "k8": _s(128, BF), "kd0": _s(128, BF),
+    "hg": _s(4 * C, BF), "vd": _s(128, F32), "vb": _s(128, F32), "k8": _s(128, BF), "kd0": _s(128, BF),
     "kd": _s(128, BF), "d8": _s(128, BF), "n0": _s(8, F32), "n1": _s(8, F32), "noff": _s(8, U16),
-    "mo": _s(C, BF), "e1": _s(C, F32), "e2": _s(C, F32), "tt": _s(6 * NT, F32), "ki": _s(NT, I32),
-    "kj": _s(NT, I32), "toff": _s(NT, U16), "ids": _s(128, BF), "ndb": _s(C, F32), "ys": _s(C, F32),
+    "mv": _s(C, BF), "mo": _s(C, BF), "e1": _s(C, BF), "e2": _s(C, BF), "tt": _s(6 * NT, F32),
+    "toff": _s(NT, U16), "ids": _s(128, BF), "ndb": _s(C, F32), "ys": _s(C, F32),
 }
 SCRATCH.update({k: ("psum", [128, 512], F32) for k in PSUM})
 SEMAPHORES = (["cv", "cs", "ct", "cg"] + ["arr%d" % r for r in range(R)] + ["left%d" % r for r in range(R)]
-              + ["d%d" % k for k in range(20)])
+              + ["d%d" % k for k in range(24)])
 
 
 def rank_program(g, core, T, topo):
@@ -169,233 +180,340 @@ def rank_program(g, core, T, topo):
     QQ, PI, CC, BH, FL, GG, Q4 = range(7)
     SC, SB, BO, DD, P12, CQ, NO, Z0 = range(8)
     DCO, TA, TS_, TB, CA, QM, CB, WK, HH, AL, X1, GA = range(8, 20)
-    R1, R2, R3, R4, QN, OF, OG, CP, DF, DF0, WR, TH, B0, B1, RC = range(20, 35)
-
-    dma("s", T.ut[:], T.u[:], [], ["ut"])
-    dma("y", T.xin[:], T.x[:], [], ["xin"])
-
-    op("g", [], ["pint"], lambda: g.iota(T.pint[:], [[0, 1]], 0, 1))
-    for name, pattern, base, cm in [
-            ("t16", [[16, NT]], 0, 0), ("k16", [[0, NT], [1, 16]], 0, 0), ("gcol", [[1, 8], [0, 16]], 0, 0),
-            ("jp", [[1, 128]], 0, -1), ("idc", [[1, C]], 1, 0), ("r24", [[0, 18], [1, 24]], 0, 0),
-            ("par", [[0, 17], [1, 2]], 0, 0), ("keep2", [[0, 136], [1, 2]], 0, 0), ("idp", [[1, M]], 0, 0),
-            ("k8", [[0, 16], [1, 8]], 0, 0)]:
-        iota(T[name][:], pattern, base, cm, [], [name])
-
-    fill(T.zt[:], 0.0, ["zt"])
-    for k, (sh, mk) in enumerate([(0, 15), (3, 1), (2, 1), (1, 1), (0, 1), (4, 7), (2, 3)]):
-        ts(T.ints[:, k:k + 1], T.pint[:], sh, mk, A.arith_shift_right, A.bitwise_and, ["pint"], ["ints%d" % k])
-    fill(T.et[:], 0.0, ["et0", "et1"])
-    cp(T.pb[:, 0:7], T.ints[:, 0:7], ["ints%d" % k for k in range(7)], ["pb"])
-    cp(T.uoff[:, 0:8], T.t16[:, 0:8], ["t16"], ["uoff0"])
-    ts(T.uoff[:, 8:16], T.t16[:, 0:8], pb(PI), 1.0, A.add, A.add, ["t16", "pb"], ["uoff1"])
-    ts(T.uoff[:, 16:24], T.t16[:, 0:8], pb(PI), 2.0, A.subtract, A.add, ["t16", "pb"], ["uoff2"])
-    ts(T.eq[:], T.k16[:], pb(QQ), None, A.is_equal, None, ["k16", "pb"], ["eq"])
-
-    col(SC, pb(CC), 2.0, -1.0, ["pb"])
-    col(SB, pb(CC), -1.0, 0.5, ["pb"])
-    col(DD, pb(FL), -(2.0 ** -11), 2.0 ** -12, ["pb"])
-    col(P12, pb(PI), 12.0, 0.0, ["pb"])
-    col(CQ, pb(QQ), 511.0, -7665.0, ["pb"])
-    col(BO, pb(BH), float(PW), 0.0, ["pb"])
-    act(T.keep16[:], T.k16[:], F.Sign, ["k16"], ["keep16"])
-    act(T.kc[:], T.eq[:], F.Identity, ["eq"], ["kc"], bias=-HUGE, scale=2 * HUGE)
-    act(T.d0[:], T.keep16[:], F.Identity, ["keep16"], ["d0"], bias=-HUGE, scale=2 * HUGE)
-
-    def tail(u):
-        lo = 16 * SLOTS[u][3]
-        return T.mt[:, 4 * (START[u] + lo):4 * (START[u] + WIDTH[u])], 4 * (WIDTH[u] - lo), ["m%d" % t for t in SLOTS[u]]
-
-    for u in (0, 1, 5):
-        fill(tail(u)[0], 0.0, tail(u)[2])
-    for e in range(2):
-        fill(T["f%d" % e][:, 0:1], 0.0, ["fz%d" % e])
-        fill(T["f%d" % e][:, C + 1:PW + 1], 0.0, ["fy%d" % e])
-    fill(T.keepr[:], 1.0, ["keepr"])
-    for u in range(2, 6):
-        a = START[u] - START[2]
-        iota(T.keepr[:, a:a + 1], [[0, 1]], 0, 0, ["keepr"], ["keepr%d" % u])
-    quant(T.qu[:], T.su[:], T.ut[:], ["ut"], ["qu"])
-
-    def pick_u(a, b, names):
-        cp(T.qur[:, 16 * a:16 * b].bitcast(dt.uint32), T.qu[:, 0:128].bitcast(dt.uint32).indirect(T.uoff[:, a:b]),
-           ["qu"] + names, ["qur%d" % a])
-        act(T.sur[:, 16 * a:16 * b], T.su[:, 0:128].indirect(T.uoff[:, a:b]), F.Copy, ["qu"] + names, ["sur%d" % a])
-
-    pick_u(0, 16, ["uoff0", "uoff1"])
-    col(R1, pb(Q4), pb(Q4), pb(Q4), ["pb"])
-    col(Z0, T.eq[:, 0:1], -BIG, pc(CQ), ["eq"] + pk(CQ))
-    col(R2, pc(R1), -32.0, 2559.0, pk(R1))
-    act(tail(2)[0], T.zt[:, 0:tail(2)[1]], F.Copy, ["zt"], tail(2)[2])
-    col(R3, pb(BH), -1280.0, pc(R2), ["pb"] + pk(R2))
-    act(tail(3)[0], T.zt[:, 0:tail(3)[1]], F.Copy, ["zt"], tail(3)[2])
-    col(R4, pb(FL), -640.0, pc(R3), ["pb"] + pk(R3))
-    act(tail(4)[0], T.zt[:, 0:tail(4)[1]], F.Copy, ["zt"], tail(4)[2])
-    act(T.idf[:], T.idc[:], F.Identity, ["idc"], ["idf"], scale=2.0 ** -21)
-    for b in range(4):
-        ts(T.gt[:, b:512:4], T.gcol[:], pb(GG), None, A.is_equal, None, ["gcol", "pb"], ["gt%d" % b])
-    for h in range(2):
-        ts(T.et[:, 520 * h + 2 + h:520 * h + 514 + h:4], T.jp[:], 0.0, None, A.is_equal, None, ["jp"], ["et%d" % h])
-    quant(T.qg[:], T.sg[:], T.gt[:], ["gt%d" % b for b in range(4)], ["qg"])
-
-    def quant_e(b):
-        o = 520 * (b % 2) + 2 - 2 * (b // 2)
-        quant(T.qe[:, 128 * b:128 * b + 128], T.se[:, 128 * b:128 * b + 128], T.et[:, o:o + 512],
-              ["et%d" % (b % 2)], ["qe%d" % b])
-
-    quant_e(0)
-    quant_e(1)
-    act(T.kx[:, 0:C - 1], T.eq[:, 1:C], F.Identity, ["eq"], ["kx"], bias=512.0, scale=-(BIG + 512.0))
-    col(OF, T.eq[:, 0:1], BIG, 0.0, ["eq"])
-
-    dma("y", T.qw[:].bitcast(dt.uint8), T.wc[:], ["xin"], ["qw"])
-    dma("y", T.sw[:], T.ws[:], [], ["sw"])
-    dma("y", T.vt[:], T.v[:], [], ["vt"])
+    X2, QN, OF, OG, CP, DF, DF0, WR, TH, B0, B1, RC = range(20, 32)
 
     US = (T.qur[:, 0:128], T.sur[:, 0:128])
     UC = (T.qur[:, 128:256], T.sur[:, 128:256])
     UD = (T.qur[:, 256:384], T.sur[:, 256:384])
     UK = ["qur0", "sur0"]
-    QX = ["qx", "qx2"]
+    QX = ["qx0", "qx1"]
     NK = ["noff", "noff0"]
-    RB = ["pa", "pd", "pf0", "pf1"]
+    RB = ["pa", "pd", "pcl", "pbk"]
+    PIECE = [(0, CUT), (CUT, C)]
 
-    def fplane(b):
-        return T["f%d" % (b % 2)][:, PW * (b // 2) + 1:PW * (b // 2) + 1 + C]
+    def fplane(b, lo=0, hi=C):
+        o = PW * (b // 2) + 1
+        return T["f%d" % (b % 2)][:, o + lo:o + hi]
 
-    def slot(t, n):
-        for u in range(6):
+    def slot(t, lo, hi):
+        t = 15 - t if t in EARLY else t
+        for u in range(5):
             if t in SLOTS[u]:
                 a = 4 * START[u] + SLOTS[u].index(t)
-                return T.mt[:, a:a + 4 * n - 3:4]
+                return T.mt[:, a + 4 * lo:a + 4 * hi - 3:4]
+
+    def names(u):
+        return ["m%s" % t for t in SLOTS[u]] + (["md0_"], [], ["m%d" % t for t in EARLY], [], [])[u]
+
+    def reach(t):
+        return 16 * (t - NEAR)
+
+    def blank(u, lo, hi):
+        act(T.mt[:, 4 * (START[u] + lo):4 * (START[u] + hi)], T.zt[:, 0:4 * (hi - lo)], F.Copy, ["zt"], names(u))
 
     def qtile(u):
-        a, b = START[u], START[u] + WIDTH[u]
-        quant(T.qm[:, a:b], T.sm[:, a:b], T.mt[:, 4 * a:4 * b], ["m%d" % t for t in SLOTS[u]], ["qm%d" % u])
+        a, b, n = START[u], QSTART[u], WIDTH[u]
+        quant(T.qm[:, b:b + n], T.sm[:, b:b + n], T.mt[:, 4 * a:4 * (a + n)], names(u), ["qm%d" % u])
+
+    def const(name, k):
+        return T["q" + name][:, 128 * k:128 * k + 128], T["s" + name][:, 128 * k:128 * k + 128]
 
     def colsum(u, start, stop):
-        a, b = START[u], START[u] + WIDTH[u]
-        mm("pd", WIDTH[u], T.qg[:], T.sg[:], T.qm[:, a:b], T.sm[:, a:b], ["qg", "qm%d" % u], start, stop)
+        b, n = QSTART[u], WIDTH[u]
+        mm("pd", n, *const("g", 2), T.qm[:, b:b + n], T.sm[:, b:b + n], ["qg2", "qm%d" % u], start, stop)
 
-    def own(t):
-        return T.bb[:, 16 * t + 15:16 * t + 16]
+    def bandcols(u, h, start=False):
+        d = 4 * u + 2 * h
+        a, n = QSTART[u] - ORIGIN[u] + 16 * (d + 1), C - 16 * d
+        mm("pd", n, *const("g", h), T.qm[:, a:a + n], T.sm[:, a:a + n], ["qg%d" % h, "qm%d" % u], start, False)
+
+    def bandrows(u, h):
+        a = QSTART[u] - ORIGIN[u] + 16 * h
+        mm("pcl", C, *const("e", 4 + h), T.qm[:, a:a + C], T.sm[:, a:a + C], ["qe%d" % (4 + h), "qm%d" % u, "qmz"],
+           (u, h) == (0, 0), (u, h) == (1, 1))
+
+    def band(d, lo=0, hi=C, part=""):
+        lo = max(lo, 16 * d)
+        src = "o16" if d else "bb"
+        a = 16 * (1 - d % 2) - ORIGIN[d // 4]
+        tt(slot("d%d" % d, lo + a, hi + a), T[src][:, lo:hi], T.pa[:, lo - 16 * d:hi - 16 * d], A.is_gt,
+           ["pa"] + ["%s%d" % (src, k) for k in range(3) if lo < PART[k][1] and hi > PART[k][0]],
+           ["md%d%s" % (d, part)])
+
+    def sgn(t):
+        a = sum(reach(k) for k in ON_SCALAR if k < t)
+        return T.sgn[:, a:a + reach(t)]
+
+    def sign(t):
+        act(sgn(t), T.pbk[:, 0:reach(t)], F.Sign, ["pbk", "bb%d" % (t // 8)], ["sgn%d" % t],
+            bias=T.bb[:, 16 * t:16 * t + 1], scale=-1.0)
+
+    def relu(t):
+        act(slot(t, 0, reach(t)), sgn(t), F.Relu, ["sgn%d" % t], ["m%d" % t, "rs%d" % t], acc=T.rs[:, t:t + 1])
+
+    def span(t):
+        return (16 * (t + NEAR + 1), 192) if t in EARLY else (0, reach(t))
 
     def compare(t):
-        ts(slot(t, 16 * t), T.pa[:, 0:16 * t], own(t), None, A.is_lt, None, ["pa", "bb%d" % (16 * t // CUT)],
-           ["m%d" % t])
+        lo, hi = span(t)
+        ts(slot(t, lo, hi), T.pa[:, lo:hi], T.bb[:, 16 * t:16 * t + 1], None, A.is_le if t in EARLY else A.is_lt, None,
+           ["pa", "bb%d" % (t // 8)], ["m%d" % t])
 
-    def sign(k):
-        t = ON_SCALAR[k]
-        act(T.sgn[:, C * k:C * k + 16 * t], T.pbk[:, 0:16 * t], F.Sign, ["pbk", "bb1"], ["sgn%d" % k],
-            bias=own(t), scale=-1.0)
+    def total(t):
+        op("v", ["m%d" % t], ["rs%d" % t],
+           lambda: V.tensor_reduce(T.rs[:, t:t + 1], slot(t, *span(t)), AxisListType.X, A.add))
 
-    def relu(k):
-        t = ON_SCALAR[k]
-        act(slot(t, 16 * t), T.sgn[:, C * k:C * k + 16 * t], F.Relu, ["sgn%d" % k], ["m%d" % t, "rs%d" % t],
-            acc=T.rs[:, t:t + 1])
+    def keep(k):
+        lo, hi = PART[k]
+        bank, a = [("pbk", 0), ("pbk", 128), ("pd", 0)][k]
+        tt(T.d1[:, lo:hi], T[bank][:, a:a + 128], T.kc[:], A.min, [bank, "kc"], ["d1%d" % k])
 
-    def rows(b):
-        a = 4 * START[2] + b
-        scan(T.rsc[:, 640 * b:640 * b + 640], T.keepr[:], T.mt[:, a:a + 4 * 640 - 3:4], 0.0, A.mult, A.subtract,
-             ["keepr%d" % u for u in range(2, 6)] + ["m%d" % SLOTS[u][b] for u in range(2, 6)], ["rsc%d" % b])
+    def hold(k):
+        lo, hi = PART[k]
+        back = slice(hi - 1, lo - 1 if lo else None, -1)
+        scan(T.bb[:, back], T.d0[:], T.d1[:, back], -HUGE, A.min, A.max, ["d0", "d1%d" % k], ["bb%d" % k])
+
+    def spread(k):
+        lo, hi = PART[k]
+        scan(T.o16[:, lo:hi], T.d0[:], T.bb[:, lo:hi], -HUGE, A.min, A.max, ["d0", "bb%d" % k], ["o16%d" % k])
+
+    def quant_x(src, k, rd):
+        lo, hi = PIECE[k]
+        quant(T.qx[:, lo:hi], T.sx[:, lo:hi], src[:, 4 * lo:4 * hi], rd, ["qx%d" % k])
+
+    def scores(k):
+        lo, hi = PIECE[k]
+        mm(("pbk", "pd")[k], hi - lo, US[0], US[1], T.qx[:, lo:hi], T.sx[:, lo:hi], UK + ["qx%d" % k])
+
+    def colours(k):
+        lo, hi = PIECE[k]
+        bank = ("pcl", "pf0")[k]
+        act(T.val[:, lo:hi], T[bank][:, 0:hi - lo], F.Sign, [bank] + pk(SC, SB), ["val", "val%d" % k],
+            bias=pc(SB), scale=pc(SC))
+
+    def colour_scores(k):
+        lo, hi = PIECE[k]
+        mm(("pcl", "pf0")[k], hi - lo, UC[0], UC[1], T.qx[:, lo:hi], T.sx[:, lo:hi], ["qur8", "sur8", "qx%d" % k])
 
     def tk(k):
         return T.tt[:, NT * k:NT * k + NT]
 
-    quant(T.qx[:, CUT:C], T.sx[:, CUT:C], T.xin[:, 4 * CUT:4 * C], ["xin"], ["qx2"])
-    quant(T.qx[:, 0:CUT], T.sx[:, 0:CUT], T.xin[:, 0:4 * CUT], ["xin"], ["qx"])
-    for r in range(R):
-        mm("pd", C - CUT, US[0], US[1], T.qx[:, CUT:C], T.sx[:, CUT:C], UK + ["qx2"])
-        mm("pcl", C, UC[0], UC[1], T.qx[:], T.sx[:], UK + QX)
-        mm("pa", C, US[0], US[1], T.qx[:], T.sx[:], UK + QX)
-        mm("pbk", C, US[0], US[1], T.qx[:], T.sx[:], UK + QX)
-        tt(T.d1[:, CUT:C], T.pd[:, 0:C - CUT], T.kc[:, CUT:C], A.min, ["pd", "kc"], ["d11"])
-        if r == 0:
-            ts(T.dec0[:], T.r24[:, 0:420], pc(P12), -4.0, A.is_equal, A.mult, ["r24"] + pk(P12), ["dec0"])
-            quant_e(2)
-            quant_e(3)
-            cp(T.roff[:, 0:1], pc(R4), pk(R4), ["roff"])
-            ts(T.cst[:], T.t16[:], pc(Z0), None, A.add, None, ["t16"] + pk(Z0), ["cst"])
-        for b in range(4):
-            mm("pf%d" % b, C, T.qe[:, 128 * b:128 * b + 128], T.se[:, 128 * b:128 * b + 128], T.qx[:], T.sx[:],
-               ["qe%d" % b] + QX)
+    def pick_u(a, b, rd):
+        cp(T.qur[:, 16 * a:16 * b].bitcast(dt.uint32), T.qu[:, 0:128].bitcast(dt.uint32).indirect(T.uoff[:, a:b]),
+           ["qu"] + rd, ["qur%d" % a])
+        act(T.sur[:, 16 * a:16 * b], T.su[:, 0:128].indirect(T.uoff[:, a:b]), F.Copy, ["qu"] + rd, ["sur%d" % a])
 
-        scan(T.bb[:, CUT:C], T.d0[:, CUT:C], T.d1[:, CUT:C], -HUGE, A.min, A.max, ["d0", "d11"], ["bb1"])
-        tt(T.d1[:, 0:CUT], T.pa[:, 0:CUT], T.kc[:, 0:CUT], A.min, ["pa", "kc"], ["d10"])
-        for t in MID:
-            compare(t)
-        scan(T.bb[:, 0:CUT], T.d0[:, 0:CUT], T.d1[:, 0:CUT], -HUGE, A.min, A.max, ["d0", "d10"], ["bb0"])
-        compare(16)
-        tt(slot(0, C), T.bb[:], T.pa[:, 0:C], A.is_ge, ["pa", "bb0", "bb1"], ["m0"])
-        act(T.sig[:], T.pcl[:, 0:C], F.Sign, ["pcl"], ["sig"])
-        sign(0)
-        act(T.val[:], T.sig[:], F.Sign, ["sig"] + pk(SC, SB), ["val"], bias=pc(SB), scale=pc(SC))
-        dma("g", T.val[:], T.idf[:], ["idf", "val"], ["val"], accum_op=A.add)
-        for k in range(1, len(ON_SCALAR)):
-            sign(k)
-            relu(k - 1)
-        relu(len(ON_SCALAR) - 1)
-        for k, t in enumerate(MID):
-            act(T.junk[:, C * k:C * k + 16 * t], slot(t, 16 * t), F.Identity, ["m%d" % t], ["junk%d" % k, "rs%d" % t],
-                acc=T.rs[:, t:t + 1])
+    def quant_e(b):
+        o = 520 * (b % 2) + (0 if b // 2 == 1 else 2)
+        quant(*const("e", b), T.et[:, o:o + 512], ["et%d%d" % (b % 2, a) for a in (0, 2, 4)], ["qe%d" % b])
+
+    def quant_g(k):
+        o = 0 if k else 2
+        quant(*const("g", k), T.gt[:, o:o + 512], ["gt%d" % b for b in range(4)], ["qg%d" % k])
+
+    dma("s", T.ut[:], T.u[:], [], ["ut"])
+    dma("y", T.xin[:, 0:4 * CUT], T.x[:, 0:4 * CUT], [], ["xin0"])
+    dma("y", T.xin[:, 4 * CUT:4 * C], T.x[:, 4 * CUT:4 * C], [], ["xin1"])
+
+    op("g", [], ["pint"], lambda: g.iota(T.pint[:], [[0, 1]], 0, 1))
+    for name, pattern, base, cm in [
+            ("jp", [[1, 128]], 0, -1), ("gcol", [[1, 8], [0, 16]], 0, 0), ("t16", [[16, NT]], 0, 0),
+            ("k16", [[0, NT], [1, 16]], 0, 0), ("idc", [[1, C]], 1, 0), ("r24", [[0, 18], [1, 24]], 0, 0),
+            ("par", [[0, 17], [1, 2]], 0, 0), ("keep2", [[0, 72], [1, 2]], 0, 0), ("idp", [[1, M]], 0, 0),
+            ("k8", [[0, 16], [1, 8]], 0, 0)]:
+        iota(T[name][:], pattern, base, cm, [], [name])
+    for a, b, step, base in PAIRS:
+        iota(T.cst[:, a:b], [[step, b - a]], base, 0, [], ["cst%d" % a])
+
+    def ones_e(h, a):
+        o = 520 * h + a + h
+        ts(T.et[:, o:o + 512:4], T.jp[:], 0.0, None, A.is_equal, None, ["jp"], ["et%d%d" % (h, a)])
+
+    def ones_g(b):
+        ts(T.gt[:, b:512:4], T.gcol[:], pb(GG), None, A.is_equal, None, ["gcol", "pb"], ["gt%d" % b])
+
+    fill(T.zt[:], 0.0, ["zt"])
+    for e in range(2):
+        fill(T.et[:, 520 * e + 1 - e:520 * e + 520:2], 0.0, ["et%d0" % e])
+        fill(T.gt[:, e:516:4], 0.0, ["gt%d" % e])
+    for k, (sh, mk) in enumerate([(0, 15), (3, 1), (2, 1), (1, 1), (0, 1), (4, 7), (2, 3)]):
+        ts(T.ints[:, k:k + 1], T.pint[:], sh, mk, A.arith_shift_right, A.bitwise_and, ["pint"], ["ints%d" % k])
+    for a in (2, 4):
+        for h in range(2):
+            ones_e(h, a)
+    cp(T.pb[:, 0:7], T.ints[:, 0:7], ["ints%d" % k for k in range(7)], ["pb"])
+    quant_e(4)
+    quant_e(5)
+    for b in (2, 3):
+        ones_g(b)
+    cp(T.uoff[:, 0:8], T.t16[:, 0:8], ["t16"], ["uoff0"])
+    ts(T.uoff[:, 8:16], T.t16[:, 0:8], pb(PI), 1.0, A.add, A.add, ["t16", "pb"], ["uoff1"])
+    fill(T.rs[:, 4:12], 0.0, ["rs4"])
+    quant_g(0)
+    quant_g(1)
+    ts(T.eq[:], T.k16[:], pb(QQ), None, A.is_equal, None, ["k16", "pb"], ["eq"])
+    for b in (0, 1):
+        ones_g(b)
+
+    for b in BLANK:
+        blank(*b)
+    col(SC, pb(CC), 2.0, -1.0, ["pb"])
+    col(SB, pb(CC), -2.0 * TINY, TINY, ["pb"])
+    col(CQ, pb(QQ), 513.0, -7680.0, ["pb"])
+    col(P12, pb(PI), 12.0, 0.0, ["pb"])
+    act(T.keep16[:], T.k16[:], F.Sign, ["k16"], ["keep16"])
+    act(T.kc[:], T.eq[:, 0:128], F.Identity, ["eq"], ["kc"], bias=-HUGE, scale=2 * HUGE)
+    act(T.d0[:], T.keep16[:, 0:128], F.Identity, ["keep16"], ["d0"], bias=-HUGE, scale=2 * HUGE)
+    quant(T.qu[:], T.su[:], T.ut[:], ["ut"], ["qu"])
+    quant_g(2)
+    pick_u(0, 8, ["uoff0"])
+
+    dma("y", T.qw[:].bitcast(dt.uint8), T.wc[:], ["xin1"], ["qw"])
+    dma("y", T.sw[:], T.ws[:], [], ["sw"])
+    dma("y", T.vt[:], T.v[:], [], ["vt"])
+
+    quant_x(T.xin, 0, ["xin0"])
+    scores(0)
+    quant_x(T.xin, 1, ["xin1"])
+    scores(1)
+    pick_u(8, 16, ["uoff1"])
+    colour_scores(0)
+    col(Z0, T.eq[:, 0:1], -BIG, pc(CQ), ["eq"] + pk(CQ))
+    act(T.idf[:], T.idc[:], F.Identity, ["idc"], ["idf"], scale=2.0 ** -21)
+    colours(0)
+    keep(1)
+    keep(0)
+    quant(T.qm[:, QSTART[1] - 128:QSTART[1]], T.sm[:, QSTART[1] - 128:QSTART[1]], T.zt[:], ["zt"], ["qmz"])
+    hold(1)
+
+    def planes(*bs):
+        for b in bs:
+            mm("pf%d" % b, C, *const("e", b), T.qx[:], T.sx[:], ["qe%d" % b] + QX)
+
+    def planes_out():
+        for b in (0, 2, 3, 1):
+            act(fplane(b), T["pf%d" % b][:, 0:C], F.Copy, ["pf%d" % b], ["f%d" % b])
+
+    late = [lambda: ts(T.cst[:], T.cst[:], pc(Z0), None, A.add, None, ["cst%d" % a[0] for a in PAIRS] + pk(Z0), ["cst"])]
+    late += [lambda h=h: fill(T.et[:, 521 * h:520 * h + 520:4], 0.0, ["et%d4" % h]) for h in range(2)]
+    late += [lambda: ts(T.dec0[:], T.r24[:, 0:420], pc(P12), -4.0, A.is_equal, A.mult, ["r24"] + pk(P12), ["dec0"])]
+    late += [lambda b=b: quant_e(b) for b in range(4)]
+    late += [lambda: ts(T.mka[:], T.par[:], pb(PI), 2.0 ** 21, A.is_equal, A.mult, ["par", "pb"], ["mka"])]
+    for e in range(2):
+        late += [lambda e=e: fill(T["f%d" % e][:, 0:1], 0.0, ["fz%d" % e]),
+                 lambda e=e: fill(T["f%d" % e][:, C + 1:PW + 1], 0.0, ["fy%d" % e])]
+    late += [lambda: ts(T.uoff[:, 16:24], T.t16[:, 0:8], pb(PI), 2.0, A.subtract, A.add, ["t16", "pb"], ["uoff2"])]
+
+    def spare(n):
+        for _ in range(min(n, len(late))):
+            late.pop(0)()
+
+    for r in range(R):
+        mm("pa", C, US[0], US[1], T.qx[:], T.sx[:], UK + QX)
+        colour_scores(1)
+        if r:
+            planes(1, 2, 3)
+
+        hold(0)
+        spread(1)
+        keep(2)
+        spread(0)
+        hold(2)
+        band(0, 0, CUT)
+        spread(2)
+        band(0, CUT, C, "_")
+        for k, t in enumerate(ON_SCALAR):
+            sign(t)
+            if k:
+                relu(ON_SCALAR[k - 1])
+            if k == COLOUR_AT:
+                colours(1)
+                dma("g", T.val[:], T.idf[:], ["idf", "val0", "val1"], ["val", "val0", "val1"], accum_op=A.add)
+                if r:
+                    planes(0)
+        relu(ON_SCALAR[-1])
+        if r == 0:
+            act(T.kx[:, 0:C - 1], T.eq[:, 1:C], F.Identity, ["eq"], ["kx"], bias=512.0, scale=-(BIG + 512.0))
+            col(OF, T.eq[:, 0:1], BIG, 0.0, ["eq"])
+            col(DD, pb(FL), -(2.0 ** -11), 2.0 ** -12, ["pb"])
+            col(BO, pb(BH), float(PW), 0.0, ["pb"])
+        for u in range(2):
+            for d in range(max(1, 4 * u), 4 * u + 4):
+                band(d)
+            for t in ON_VECTOR[2 * u:2 * u + 2]:
+                compare(t)
+            qtile(u)
+            for h in range(2):
+                bandrows(u, h)
+            for h in range(2):
+                bandcols(u, h, u + h == 0)
+        compare(ON_VECTOR[4])
+        for t in ON_VECTOR[:4]:
+            total(t)
+        for u in (3, 2):
+            qtile(u)
+            colsum(u, False, False)
+        total(ON_VECTOR[4])
+        scan(T.rb[:], T.keep16[:], T.pcl[:, 0:C], 0.0, A.mult, A.subtract, ["keep16", "pcl"], ["rb"])
+        qtile(4)
+        colsum(4, False, True)
+        if r:
+            planes_out()
+        spare(5)
+        tt(T.w1[:], T.cst[:], T.rs[:], A.subtract, ["cst", "rs4"] + ["rs%d" % t for t in ON_SCALAR + ON_VECTOR], ["w1"])
+        tt(T.kx[:, 15:C:16], T.w1[:], T.rb[:, 15:C:16], A.add, ["w1", "kx", "rb"], ["kx1"])
+        scan(T.ext[:], T.pd[:, 0:C], T.kx[:], -HUGE, A.max, A.add, ["kx", "kx1", "pd"], ["ext"])
+        spare(1)
+        ts(T.poff[:], T.ext[:, 15:C:16], pc(OF), None, A.add, None, ["ext"] + pk(OF), ["poff"])
+        spare(2)
         if r == 0:
             act(T.dec[:], T.dec0[:], F.Identity, ["dec0"] + pk(DD), ["dec"], bias=pc(DD))
-        for b in range(4):
-            act(fplane(b), T["pf%d" % b][:, 0:C], F.Copy, ["pf%d" % b], ["f%d" % b])
-        for t in (15, 14, 13, 12):
-            compare(t)
-        scan(T.rd[:], T.keep16[:], slot(0, C), 0.0, A.mult, A.add, ["keep16", "m0"], ["rd"])
-        qtile(2)
-        for t in (11, 10, 9, 8, 7):
-            compare(t)
-        tt(T.w1[:], T.cst[:], T.rd[:, 15:C:16], A.subtract, ["cst", "rd"], ["w1"])
-        qtile(3)
-        for t in (6, 5, 4, 3, 2, 1):
-            compare(t)
-        qtile(0)
-        qtile(4)
-        qtile(5)
-        colsum(0, True, False)
-        for u in (2, 3, 4, 5):
-            colsum(u, False, False)
-        for b in range(3):
-            rows(b)
-        cp(T.kx[:, 15:16], T.w1[:, 0:1], ["w1", "kx"], ["kx0"])
-        if r == 0:
-            ts(T.mka[:], T.par[:], pb(PI), 2.0 ** 21, A.is_equal, A.mult, ["par", "pb"], ["mka"])
-        qtile(1)
-        colsum(1, False, True)
-        rows(3)
-        tt(T.kx[:, 287:C:16], T.w1[:, 17:NT], T.rs[:, 17:NT], A.subtract,
-           ["w1", "kx"] + ["rs%d" % t for t in range(17, NT)], ["kx2"])
-        tt(T.kx[:, 31:272:16], T.rsc[:, 0:2560].indirect(T.roff[:, 0:1]), T.w1[:, 1:17], A.add,
-           ["roff", "w1", "kx", "rsc0", "rsc1", "rsc2", "rsc3"], ["kx1"])
-        scan(T.ext[:], T.pd[:, 0:C], T.kx[:], -HUGE, A.max, A.add, ["kx", "kx0", "kx1", "kx2", "pd"], ["ext"])
-        ts(T.poff[:], T.ext[:, 15:C:16], pc(OF), None, A.add, None, ["ext"] + pk(OF), ["poff"])
+            planes(0, 1, 2, 3)
+            planes_out()
+            act(T.yt[:, 256:512], T.zt[:, 0:256], F.Copy, ["zt"], ["ytz"])
 
         cp(T.srt[:, 0:C].indirect(T.poff[:]), T.val[:], ["poff", "val"], ["srt"])
-        cp(T.srt[:, C:420], T.srt[:, 0:36], ["srt"], ["srt2"])
-        scan(T.scn[:, 0:C], T.dec[:, 0:C], T.srt[:, 0:C], 0.0, A.add, A.max, ["dec", "srt"], ["scn"])
-        scan(T.scw[:], T.dec[:, 372:420], T.srt[:, 372:420], 0.0, A.add, A.max, ["dec", "srt", "srt2"], ["scw"])
-        tt(T.ab[:, 0:31], T.scn[:, 23:C:12], T.mka[:, 0:31], A.mult, ["scn", "mka"], ["ab"])
-        tt(T.ab[:, 31:34], T.scw[:, 23:48:12], T.mka[:, 31:34], A.mult, ["scw", "mka"], ["ab2"])
-        tt(T.bi[:], T.ab[:, 0:34:2], T.ab[:, 1:34:2], A.max, ["ab", "ab2"], ["bi"])
-        ts(T.bj[:], T.bi[:], 511, None, A.bitwise_and, None, ["bi"], ["bj"])
-        ts(T.zoff[:, 0:17], T.bj[:], pc(BO), None, A.add, None, ["bj"] + pk(BO), ["zoff"])
-
-        ts(T.gz[:, 0:272], T.f0[:, 0:PW + C + 1].indirect(T.zoff[:, 0:17]), 0.25, None, A.mult, None,
-           ["zoff", "f0", "f2", "fz0", "fy0"], ["gz0"])
-        act(T.gz[:, 272:544], T.f1[:, 0:PW + C + 1].indirect(T.zoff[:, 0:17]), F.Identity,
-            ["zoff", "f1", "f3", "fz1", "fy1"], ["gz1"], scale=0.25)
+        spare(1)
+        cp(T.srt[:, C:420], T.srt[:, 0:36], ["srt"], ["srt1"])
+        for h, (lo, hi) in enumerate(SCAN):
+            scan(T.scn[:, lo + 24 * h:hi + 24 * h], T.dec[:, lo:hi], T.srt[:, lo:hi], 0.0, A.add, A.max,
+                 ["dec", "srt", "srt%d" % h], ["scn%d" % h])
+        for h, (a, b) in enumerate(HALF):
+            tt(T.ab[:, 2 * a:2 * b], T.scn[:, 23 + 24 * (a + h):24 * (b + h) + 12:12], T.mka[:, 2 * a:2 * b], A.mult,
+               ["scn%d" % h, "mka"], ["ab%d" % h])
+            spare(1 - h)
+        for h, (a, b) in enumerate(HALF):
+            tt(T.bi[:, a:b], T.ab[:, 2 * a:2 * b:2], T.ab[:, 2 * a + 1:2 * b:2], A.max, ["ab%d" % h], ["bi%d" % h])
+            spare(1 - h)
+        for h, (a, b) in enumerate(HALF):
+            ts(T.bj[:, a:b], T.bi[:, a:b], 511, None, A.bitwise_and, None, ["bi%d" % h], ["bj%d" % h])
+            spare(1 - h)
+        for h, (a, b) in enumerate(HALF):
+            ts(T.zoff[:, a:b], T.bj[:, a:b], pc(BO), None, A.add, None, ["bj%d" % h] + pk(BO), ["zoff%d" % h])
+            spare(2 - 2 * h)
+        if r:
+            mm("pbk", C, UD[0], UD[1], T.qx[:], T.sx[:], ["qur16", "sur16"] + QX)
+        for h, (a, b) in enumerate(HALF):
+            ts(T.gz[:, 16 * a:16 * b], T.f0[:, 0:PW + C + 1].indirect(T.zoff[:, a:b]), 0.25, None, A.mult, None,
+               ["zoff%d" % h, "f0", "f2", "fz0", "fy0"], ["gz0%d" % h])
+            act(T.gz[:, 272 + 16 * a:272 + 16 * b], T.f1[:, 0:PW + C + 1].indirect(T.zoff[:, a:b]), F.Identity,
+                ["zoff%d" % h, "f1", "f3", "fz1", "fy1"], ["gz1%d" % h], scale=0.25)
         if r == 0:
-            act(T.yt[:, 256:512], T.zt[:, 0:256], F.Copy, ["zt"], ["ytz"])
-        for e in range(2):
-            scan(T.zz[:, 272 * e:272 * e + 272], T.keep2[:], T.gz[:, 272 * e:272 * e + 272], 0.0,
-                 A.mult, A.add, ["keep2", "gz%d" % e], ["zz%d" % e])
-        for e in range(2):
-            tt(T.yt[:, e:256:2], T.zz[:, 272 * e + 1:272 * e + 256:2], T.zz[:, 272 * e + 9:272 * e + 264:2], A.add,
-               ["zz%d" % e], ["yt%d" % e])
-        quant(T.qy[:], T.sy[:], T.yt[:], ["yt0", "yt1", "ytz"], ["qy"])
+            act(T.ax[:], T.eq[:], F.Identity, ["eq"], ["ax"], bias=4.0, scale=-132.0)
+        act(T.mv[:], T.val[:], F.Sign, ["val"], ["mv"])
+        if r:
+            act(T.mo[:], T.pbk[:, 0:C], F.Sign, ["pbk"], ["mo"], bias=-TINY)
+        for h, (a, b) in enumerate(HALF):
+            for e in range(2):
+                o = slice(272 * e + 16 * a, 272 * e + 16 * b)
+                scan(T.zz[:, o], T.keep2[:, 0:16 * (b - a)], T.gz[:, o], 0.0, A.mult, A.add,
+                     ["keep2", "gz%d%d" % (e, h)], ["zz%d%d" % (e, h)])
+        for h, (a, b) in enumerate([(0, 120), (120, 256)]):
+            for e in range(2):
+                o = 272 * e
+                tt(T.yt[:, a + e:b:2], T.zz[:, o + a + 1:o + b:2], T.zz[:, o + a + 9:o + b + 8:2], A.add,
+                   ["zz%d0" % e, "zz%d%d" % (e, h)], ["yt%d%d" % (e, h)])
+        quant(T.qy[:], T.sy[:], T.yt[:], ["yt00", "yt10", "yt01", "yt11", "ytz"], ["qy"])
 
         order("g", ["qy"], [])
         a = LAND[r]
@@ -408,57 +526,55 @@ def rank_program(g, core, T, topo):
 
         if r == 0:
             pick_u(16, 24, ["uoff2"])
-            quant(T.ql[:, 64:192], T.sl[:, 64:192], T.zt[:], ["zt"], ["qlz0"])
-            quant(T.ql[:, 320:448], T.sl[:, 320:448], T.zt[:], ["zt"], ["qlz1"])
+            mm("pbk", C, UD[0], UD[1], T.qx[:], T.sx[:], ["qur16", "sur16"] + QX)
             col(OG, pc(OF), 1.0, -5.5, pk(OF))
-            act(T.ax[:], T.eq[:], F.Identity, ["eq"], ["ax"], bias=512.0, scale=-(BIG + 512.0))
+            col(WK, pb(PI), 0.5, 0.5, ["pb"])
+            col(HH, pb(PI), -0.5, 1.0, ["pb"])
+            col(NO, pb(QQ), 4.0, -60.0, ["pb"])
             col(DCO, pb(BH), -1.0, pb(FL), ["pb"])
+            col(AL, pc(HH), pc(SC), 0.0, pk(HH, SC))
+            col(X2, pc(HH), 1.0, pc(WK), pk(HH, WK))
             col(TS_, pb(BH), 1.0, pb(FL), ["pb"])
+            col(X1, pc(AL), 1.0, pc(WK), pk(AL, WK))
             col(QM, pb(Q4), 2.0, 0.0, ["pb"])
             col(QN, pb(Q4), 2.0, -2.0, ["pb"])
-            col(WK, pb(PI), 1.0, 1.0, ["pb"])
-            col(HH, pb(PI), -0.5, 1.0, ["pb"])
-            col(NO, pb(QQ), 512.0, -7680.0, ["pb"])
+            col(GA, pc(X1), pc(NO), pc(X2), pk(X1, NO, X2))
+            act(T.mo[:], T.pbk[:, 0:C], F.Sign, ["pbk"], ["mo"], bias=-TINY)
             col(TA, pc(DCO), pb(CC), pb(BH), ["pb"] + pk(DCO))
-            col(AL, pc(HH), pc(SC), 0.0, pk(HH, SC))
             act(pc(WR), pb(Q4), F.Relu, ["pb"], pk(WR), bias=1.0, scale=-1.0)
             act(T.kd[:], T.k8[:], F.Sign, ["k8"], ["kd"])
             col(TB, pc(TA), -1.0, pc(TS_), pk(TA, TS_))
             col(CA, pc(TA), 1.0, pc(QM), pk(TA, QM))
-            col(X1, pc(AL), 1.0, pc(WK), pk(AL, WK))
             col(TH, pc(WR), -TINY, 0.0, pk(WR))
             col(CB, pc(TB), 1.0, pc(QN), pk(TB, QN))
             col(CP, pc(TB), 1.0, pc(QM), pk(TB, QM))
-            col(GA, pc(X1), pc(NO), pc(HH), pk(X1, NO, HH))
             act(T.d8[:], T.kd[:], F.Identity, ["kd"], ["d8"], bias=-HUGE, scale=2 * HUGE)
             col(DF, pc(CB), -1.0, pc(CA), pk(CA, CB))
             col(B1, pc(CB), 1.0, 0.25, pk(CB))
             act(T.ht[:, 256:512], T.zt[:, 0:256], F.Copy, ["zt"], ["htz"])
             col(DF0, pc(WR), -float(M), pc(DF), pk(WR, DF))
             col(B0, pc(WR), float(M), pc(B1), pk(WR, B1))
-        mm("pbk", C, UD[0], UD[1], T.qx[:], T.sx[:], ["qur16", "sur16"] + QX)
-        ts(tk(0), T.ext[:, 15:C:16], pc(OG), 1.0 / 12.0, A.add, A.mult, ["ext"] + pk(OG), ["tt0"])
-        ts(T.mo[:], T.pbk[:, 0:C], 0.0, None, A.is_gt, None, ["pbk"], ["mo"])
-        cp(T.ki[:], tk(0), ["tt0"], ["ki"])
-        scan(T.e1[:], T.ax[:], T.val[:], 0.0, A.add, A.max, ["ax", "val"], ["e1"])
-        ts(tk(2), T.ki[:], 4.0, None, A.mult, None, ["ki"], ["tt2"])
+            quant(T.ql[:, 64:192], T.sl[:, 64:192], T.zt[:], ["zt"], ["qlz0"])
+            quant(T.ql[:, 320:448], T.sl[:, 320:448], T.zt[:], ["zt"], ["qlz1"])
+        ts(tk(0), T.ext[:, 15:C:16], pc(OG), 1.0 / 3.0, A.add, A.mult, ["ext"] + pk(OG), ["tt0"])
+        scan(T.e1[:], T.ax[:], T.mv[:], 0.0, A.add, A.max, ["ax", "mv"], ["e1"])
+        ts(tk(2), tk(0), FOUR, FOUR, A.add, A.subtract, ["tt0"], ["tt2"])
         scan(T.e2[:], T.ax[:], T.mo[:], 0.0, A.add, A.max, ["ax", "mo"], ["e2"])
         ts(tk(1), T.e1[:, 15:C:16], pc(AL), pc(GA), A.mult, A.add, ["e1"] + pk(AL, GA), ["tt1"])
-        ts(tk(4), T.e2[:, 15:C:16], pc(WK), None, A.mult, None, ["e2"] + pk(WK), ["tt4"])
-        tt(tk(3), tk(1), tk(2), A.add, ["tt1", "tt2"], ["tt3"])
         if r == 0:
             op("v", pk(DF), pk(RC), lambda: V.reciprocal(pc(RC), pc(DF)))
-        tt(tk(5), tk(3), tk(4), A.add, ["tt3", "tt4"], ["tt5"])
+        ts(tk(4), T.e2[:, 15:C:16], pc(WK), None, A.mult, None, ["e2"] + pk(WK), ["tt4"])
+        tt(tk(3), tk(1), tk(2), A.add, ["tt1", "tt2"], ["tt3"])
         if r == 0:
             ts(T.kd0[:, 0:M], T.k8[:, 0:M], pc(CA), 0.5, A.is_equal, A.subtract, ["k8"] + pk(CA), ["kd00"])
             ts(T.kd0[:, M:128], T.k8[:, 0:M], pc(CP), 0.5, A.is_equal, A.subtract, ["k8"] + pk(CP), ["kd01"])
             act(T.kd[:], T.kd0[:], F.Identity, ["kd00", "kd01"], ["kd"], scale=2 * HUGE)
-        cp(T.kj[:], tk(5), ["tt5"], ["kj"])
+        tt(tk(5), tk(3), tk(4), A.add, ["tt3", "tt4"], ["tt5"])
         if r == 0:
             ts(T.tq[:], T.t16[:, 0:8], 0.5, pc(RC), A.mult, A.mult, ["t16"] + pk(RC), ["tq"])
         if r == 1:
             quant(T.qv[:], T.sv[:], T.vt[:], ["vt"], ["qv"])
-        cp(T.toff[:], T.kj[:], ["kj"], ["toff"])
+        cp(T.toff[:], tk(5), ["tt5"], ["toff"])
 
         w0 = VIEW[r]
         o = LAND[r] - VIEW[r]
@@ -487,37 +603,74 @@ def rank_program(g, core, T, topo):
         tt(T.n1[:, 1:8], T.n0[:, 1:8], T.tq[:, 1:8], A.add, ["n0", "tq"], ["n1"])
         ts(T.noff[:, 0:1], T.n0[:, 0:1], pc(DF0), pc(B0), A.mult, A.add, ["n00"] + pk(DF0, B0), ["noff0"])
         ts(T.noff[:, 1:8], T.n1[:, 1:8], pc(DF), pc(B1), A.mult, A.add, ["n1"] + pk(DF, B1), ["noff"])
-        cp(T.hs[:, 0:128], T.hp[:, 0:M].indirect(T.noff[:]), ["hp0"] + NK, ["hs0"])
-        for b in (1, 3, 2):
-            act(T.hs[:, 128 * b:128 * b + 128], T.hp[:, M * b:M * b + M].indirect(T.noff[:]), F.Copy,
-                ["hp%d" % b] + NK, ["hs%d" % b])
-        for b, n in ((3, C), (2, CUT)):
-            act(T.hg[:, C * (b - 2):C * (b - 2) + n], T.hs[:, 128 * b:128 * b + 128].indirect(T.toff[:, 0:n // 16]),
-                F.Copy, ["hs%d" % b, "toff"], ["hg%d" % b])
+
+        def by_kind(q, b):
+            src = T.hp[:, M * b:M * b + M].indirect(T.noff[:])
+            if q == "v":
+                cp(T.hs[:, 128 * b:128 * b + 128], src, ["hp%d" % b] + NK, ["hs%d" % b])
+            else:
+                act(T.hs[:, 128 * b:128 * b + 128], src, F.Copy, ["hp%d" % b] + NK, ["hs%d" % b])
+
+        def picked(b, k):
+            lo, hi = PIECE[k]
+            return T.hs[:, 128 * b:128 * b + 128].indirect(T.toff[:, lo // 16:hi // 16])
+
+        def xs(b, k):
+            lo, hi = PIECE[k]
+            return T.xt[:, 4 * lo + b:4 * hi:4]
+
+        def direct(b, k):
+            tt(xs(b, k), picked(b, k), fplane(b, *PIECE[k]), A.add, ["hs%d" % b, "toff", "f%d" % b], ["xt%d%d" % (b, k)])
+
+        def fetch(b, k):
+            lo, hi = PIECE[k]
+            act(T.hg[:, C * b + lo:C * b + hi], picked(b, k), F.Copy, ["hs%d" % b, "toff"], ["hg%d%d" % (b, k)])
+
+        def add(b, k):
+            lo, hi = PIECE[k]
+            tt(xs(b, k), T["pf%d" % b][:, lo:hi], T.hg[:, C * b + lo:C * b + hi], A.add,
+               ["hg%d%d" % (b, k), "pf%d" % b], ["xt%d%d" % (b, k)])
+
+        last = r == R - 1
         for b in range(2):
-            tt(T.xt[:, b:4 * C:4], T.hs[:, 128 * b:128 * b + 128].indirect(T.toff[:]), fplane(b), A.add,
-               ["hs%d" % b, "toff", "f%d" % b], ["xt%d" % b])
-        tt(T.xt[:, 4 * CUT + 2:4 * C:4], T.hs[:, 256:384].indirect(T.toff[:, CUT // 16:NT]),
-           T.f0[:, PW + 1 + CUT:PW + 1 + C], A.add, ["hs2", "toff", "f2"], ["xt4"])
-        tt(T.xt[:, 3:4 * C:4], T.pf3[:, 0:C], T.hg[:, C:2 * C], A.add, ["hg3", "pf3"], ["xt3"])
-        tt(T.xt[:, 2:4 * CUT:4], T.pf2[:, 0:CUT], T.hg[:, 0:CUT], A.add, ["hg2", "pf2"], ["xt2"])
-        if r == R - 1:
+            by_kind("v", b)
+            by_kind("s", b + 2)
+        for b, k in ((2, 0), (3, 0), (3, 1), (2, 1)):
+            fetch(b, k)
+        for b in range(2):
+            direct(b, 0)
+        for b in (2, 3):
+            add(b, 0)
+        direct(0, 1)
+        quant_x(T.xt, 0, ["xt%d0" % b for b in range(4)])
+        if last:
+            mm("pbk", CUT, T.qv[:], T.sv[:], T.qx[:, 0:CUT], T.sx[:, 0:CUT], ["qv", "qx0"])
+            dma("y", T.oc[:, 0:4 * CUT], T.qx[:, 0:CUT].bitcast(dt.uint8), ["qx0"], [])
             act(T.ids[:], T.idp[:, 0:M].indirect(T.noff[:]), F.Copy, ["idp"] + NK, ["ids"])
             act(T.ndb[:], T.ids[:, 0:128].indirect(T.toff[:]), F.Copy, ["ids", "toff"], ["ndb"])
-        quant(T.qx[:, CUT:C], T.sx[:, CUT:C], T.xt[:, 4 * CUT:4 * C], ["xt0", "xt1", "xt3", "xt4"], ["qx2"])
-        quant(T.qx[:, 0:CUT], T.sx[:, 0:CUT], T.xt[:, 0:4 * CUT], ["xt0", "xt1", "xt2", "xt3"], ["qx"])
+            act(T.ys[:, 0:CUT], T.pbk[:, 0:CUT], F.Copy, ["pbk"], ["ys0"])
+            dma("y", T.y[:, 0:CUT], T.ys[:, 0:CUT], ["ys0"], [])
+        else:
+            scores(0)
+            colour_scores(0)
+            colours(0)
+        direct(1, 1)
+        for b in (3, 2):
+            add(b, 1)
+        if not last:
+            keep(1)
+        quant_x(T.xt, 1, ["xt%d1" % b for b in range(4)])
+        if not last:
+            scores(1)
+            keep(0)
+            hold(1)
 
-    mm("pbk", C - CUT, T.qv[:], T.sv[:], T.qx[:, CUT:C], T.sx[:, CUT:C], ["qv", "qx2"])
-    mm("pa", 128, T.qv[:], T.sv[:], T.qx[:, 0:128], T.sx[:, 0:128], ["qv", "qx"])
-    mm("pd", 128, T.qv[:], T.sv[:], T.qx[:, 128:CUT], T.sx[:, 128:CUT], ["qv", "qx"])
-    dma("y", T.oc[:], T.qx[:].bitcast(dt.uint8), QX, [])
+    mm("pd", C - CUT, T.qv[:], T.sv[:], T.qx[:, CUT:C], T.sx[:, CUT:C], ["qv", "qx1"])
+    dma("y", T.oc[:, 4 * CUT:4 * C], T.qx[:, CUT:C].bitcast(dt.uint8), ["qx1"], [])
     for k in range(4):
-        dma("g" if k < 2 else "y", T.osc[4 * k:4 * k + 4, :], T.sx[32 * k:32 * k + 4, :], QX, [])
-    cp(T.ys[:, CUT:C], T.pbk[:, 0:C - CUT], ["pbk"], ["ys2"])
-    act(T.ys[:, 0:128], T.pa[:, 0:128], F.Copy, ["pa"], ["ys0"])
-    cp(T.ys[:, 128:CUT], T.pd[:, 0:128], ["pd"], ["ys1"])
-    dma("y", T.y[:, 128:C], T.ys[:, 128:C], ["ys1", "ys2"], [])
-    dma("s", T.y[:, 0:128], T.ys[:, 0:128], ["ys0"], [])
+        dma("gy"[k % 2], T.osc[4 * k:4 * k + 4, :], T.sx[32 * k:32 * k + 4, :], QX, [])
+    cp(T.ys[:, CUT:C], T.pd[:, 0:C - CUT], ["pd"], ["ys1"])
+    dma("y", T.y[:, CUT:C], T.ys[:, CUT:C], ["ys1"], [])
     dma("s", T.nd[:], T.ndb[0:128:16, :], ["ndb"], [])
     for s in sorted(count):
         g.wait_ge(T.sem[s], count[s])

@@ -5,6 +5,7 @@ HUGE = 2.0 ** 80
 BIG = 2.0 ** 20
 TINY = 2.0 ** -120
 FOUR = 1.5 * 2.0 ** 25
+ONE = 2.0 ** 21
 PW = 400
 NEAR = 7
 SLOTS = [["d1", "d0", "d3", "d2"], ["d5", "d4", "d7", "d6"], [15, 14, 13, 12], [20, 21, 22, 23], [16, 17, 18, 19]]
@@ -19,7 +20,7 @@ PART = [(0, 128), (128, 256), (256, 384)]
 ON_SCALAR = [15, 14, 13, 23, 22, 21, 20, 19, 18, 17, 16]
 ON_VECTOR = [12, 0, 1, 2, 3]
 COLOUR_AT = 3
-SCAN = [(0, 204), (180, 420)]
+SCAN = [(0, 221), (208, 455)]
 HALF = [(0, 8), (8, 17)]
 CUT = 256
 LAND = [0, 192, 256]
@@ -37,19 +38,18 @@ SCRATCH = {
     "xin": _s(4 * C, BF), "xt": _s(4 * C, BF), "qx": _s(C, X4), "sx": _s(C, U8),
     "ut": _s(512, BF), "qu": _s(128, X4), "su": _s(128, U8), "qur": _s(384, X4), "sur": _s(384, U8),
     "vt": _s(512, BF), "qv": _s(128, X4), "sv": _s(128, U8), "qw": _s(512, X4), "sw": _s(512, U8),
-    "pint": _s(1, I32), "ints": _s(8, I32), "pb": _s(8, F32), "pc": _s(40, F32), "t16": _s(NT, F32),
-    "uoff": _s(NT, U16), "k16": _s(C, BF), "jp": _s(128, BF), "gcol": _s(128, BF), "r24": _s(432, BF),
-    "idc": _s(C, F32), "idf": _s(C, F32), "keep2": _s(144, BF), "idp": _s(M, BF), "par": _s(34, BF),
+    "pint": _s(1, I32), "ints": _s(8, I32), "pb": _s(8, F32), "pc": _s(44, F32), "t16": _s(NT, F32),
+    "uoff": _s(NT, U16), "k16": _s(C, BF), "k16a": _s(128, BF), "jp": _s(128, BF), "gcol": _s(128, BF),
+    "idc": _s(C, F32), "idf": _s(128, F32), "keep2": _s(144, BF), "idp": _s(M, BF),
     "eq": _s(C, BF), "kc": _s(128, BF), "d0": _s(128, BF), "ax": _s(C, BF), "keep16": _s(C, BF), "kx": _s(C, F32),
-    "dec0": _s(420, BF), "dec": _s(420, BF), "mka": _s(34, F32), "cst": _s(NT, F32),
+    "dec": _s(456, F32), "cst": _s(NT, F32),
     "et": _s(1040, BF), "qe": _s(768, X4), "se": _s(768, U8),
     "gt": _s(516, BF), "qg": _s(384, X4), "sg": _s(384, U8), "zt": _s(512, BF),
     "d1": _s(C, F32), "bb": _s(C, F32), "o16": _s(C, F32),
     "mt": _s(4 * 1424, BF), "qm": _s(1552, X4), "sm": _s(1552, U8),
     "sgn": _s(2400, BF), "rs": _s(NT, F32), "rb": _s(C, F32), "w1": _s(NT, F32), "val": _s(C, F32),
     "ext": _s(C, F32), "poff": _s(NT, U16),
-    "srt": _s(420, F32), "scn": _s(444, F32), "tq": _s(8, F32),
-    "ab": _s(34, F32), "bi": _s(17, I32), "bj": _s(17, I32),
+    "srt": _s(456, F32), "scn": _s(484, F32), "tq": _s(8, F32), "bi": _s(17, I32), "bj": _s(17, I32),
     "zoff": _s(18, U16), "f0": _s(2 * PW, BF), "f1": _s(2 * PW, BF), "gz": _s(544, BF), "zz": _s(544, BF),
     "yt": _s(512, BF), "qy": _s(128, X4), "sy": _s(128, U8), "ql": _s(448, X4), "sl": _s(448, U8),
     "ht": _s(512, BF), "qh": _s(128, X4), "sh": _s(128, U8), "hp": _s(256, BF), "hs": _s(512, BF),
@@ -60,7 +60,7 @@ SCRATCH = {
 }
 SCRATCH.update({k: ("psum", [128, 512], F32) for k in PSUM})
 SEMAPHORES = (["cv", "cs", "ct", "cg"] + ["arr%d" % r for r in range(R)] + ["left%d" % r for r in range(R)]
-              + ["d%d" % k for k in range(24)])
+              + ["d%d" % k for k in range(28)])
 
 
 def rank_program(g, core, T, topo):
@@ -70,7 +70,7 @@ def rank_program(g, core, T, topo):
     nxt = T.cores[(rank + 1) % len(T.cores)]
     rid, pid = topo.addr(nxt)[0], topo.addr(nxt)[1]
     mask = topo.mask(core, nxt)
-    lanes = len(topo.engines(core, nxt))
+    lanes = topo.engines(core, nxt)
 
     queue = {"v": g.vector, "s": g.scalar, "t": g.tensor, "g": g, "y": g.sync}
     count = {"cv": 0, "cs": 0, "ct": 0, "cg": 0}
@@ -178,9 +178,10 @@ def rank_program(g, core, T, topo):
         act(pc(k), src, F.Identity, rd, pk(k), bias=bias, scale=scale)
 
     QQ, PI, CC, BH, FL, GG, Q4 = range(7)
-    SC, SB, BO, DD, P12, CQ, NO, Z0 = range(8)
+    SC, SB, BO, DD, OH, CQ, NO, Z0 = range(8)
     DCO, TA, TS_, TB, CA, QM, CB, WK, HH, AL, X1, GA = range(8, 20)
     X2, QN, OF, OG, CP, DF, DF0, WR, TH, B0, B1, RC = range(20, 32)
+    S2, SN, G0, G1, G2, G3, G4, G5, G6, G7 = range(32, 42)
 
     US = (T.qur[:, 0:128], T.sur[:, 0:128])
     UC = (T.qur[:, 128:256], T.sur[:, 128:256])
@@ -266,16 +267,16 @@ def rank_program(g, core, T, topo):
     def keep(k):
         lo, hi = PART[k]
         bank, a = [("pbk", 0), ("pbk", 128), ("pd", 0)][k]
-        tt(T.d1[:, lo:hi], T[bank][:, a:a + 128], T.kc[:], A.min, [bank, "kc"], ["d1%d" % k])
+        tt(T.d1[:, lo:hi], T[bank][:, a:a + 128], T.kc[:], A.subtract, [bank, "kc"], ["d1%d" % k])
 
     def hold(k):
         lo, hi = PART[k]
         back = slice(hi - 1, lo - 1 if lo else None, -1)
-        scan(T.bb[:, back], T.d0[:], T.d1[:, back], -HUGE, A.min, A.max, ["d0", "d1%d" % k], ["bb%d" % k])
+        scan(T.bb[:, back], T.d0[:], T.d1[:, back], -HUGE, A.add, A.max, ["d0", "d1%d" % k], ["bb%d" % k])
 
     def spread(k):
         lo, hi = PART[k]
-        scan(T.o16[:, lo:hi], T.d0[:], T.bb[:, lo:hi], -HUGE, A.min, A.max, ["d0", "bb%d" % k], ["o16%d" % k])
+        scan(T.o16[:, lo:hi], T.d0[:], T.bb[:, lo:hi], -HUGE, A.add, A.max, ["d0", "bb%d" % k], ["o16%d" % k])
 
     def quant_x(src, k, rd):
         lo, hi = PIECE[k]
@@ -286,10 +287,13 @@ def rank_program(g, core, T, topo):
         mm(("pbk", "pd")[k], hi - lo, US[0], US[1], T.qx[:, lo:hi], T.sx[:, lo:hi], UK + ["qx%d" % k])
 
     def colours(k):
-        lo, hi = PIECE[k]
-        bank = ("pcl", "pf0")[k]
-        act(T.val[:, lo:hi], T[bank][:, 0:hi - lo], F.Sign, [bank] + pk(SC, SB), ["val", "val%d" % k],
-            bias=pc(SB), scale=pc(SC))
+        if k == 0:
+            act(T.mv[:, 0:CUT], T.pcl[:, 0:CUT], F.Sign, ["pcl"] + pk(SC, SB), ["mv0"], bias=pc(SB), scale=pc(SC))
+            act(T.val[:, 0:CUT], T.mv[:, 0:CUT], F.Identity, ["mv0"], ["val", "val0"], scale=ONE)
+            dma("g", T.val[:, 0:CUT], T.idc[:, 0:CUT], ["idc", "val0"], ["val0"], accum_op=A.add)
+        else:
+            ts(T.val[:, CUT:C], T.pf0[:, 0:C - CUT], 0.0, pc(S2), A.is_gt, A.mult, ["pf0"] + pk(S2), ["val", "val1"])
+            dma("g", T.val[:, CUT:C], T.idf[:], ["idf", "val1"], ["val1"], accum_op=A.add)
 
     def colour_scores(k):
         lo, hi = PIECE[k]
@@ -318,9 +322,7 @@ def rank_program(g, core, T, topo):
     op("g", [], ["pint"], lambda: g.iota(T.pint[:], [[0, 1]], 0, 1))
     for name, pattern, base, cm in [
             ("jp", [[1, 128]], 0, -1), ("gcol", [[1, 8], [0, 16]], 0, 0), ("t16", [[16, NT]], 0, 0),
-            ("k16", [[0, NT], [1, 16]], 0, 0), ("idc", [[1, C]], 1, 0), ("r24", [[0, 18], [1, 24]], 0, 0),
-            ("par", [[0, 17], [1, 2]], 0, 0), ("keep2", [[0, 72], [1, 2]], 0, 0), ("idp", [[1, M]], 0, 0),
-            ("k8", [[0, 16], [1, 8]], 0, 0)]:
+            ("k16a", [[0, 8], [1, 16]], 0, 0), ("k16", [[0, NT], [1, 16]], 0, 0), ("idc", [[1, C]], 1, 0)]:
         iota(T[name][:], pattern, base, cm, [], [name])
     for a, b, step, base in PAIRS:
         iota(T.cst[:, a:b], [[step, b - a]], base, 0, [], ["cst%d" % a])
@@ -333,6 +335,8 @@ def rank_program(g, core, T, topo):
         ts(T.gt[:, b:512:4], T.gcol[:], pb(GG), None, A.is_equal, None, ["gcol", "pb"], ["gt%d" % b])
 
     fill(T.zt[:], 0.0, ["zt"])
+    op("g", ["zt"], ["keep16"],
+       lambda: g.affine_select(T.keep16[:], T.zt[:, 0:C], [[0, NT], [1, 16]], A.is_equal, 1.0, 0, 0))
     for e in range(2):
         fill(T.et[:, 520 * e + 1 - e:520 * e + 520:2], 0.0, ["et%d0" % e])
         fill(T.gt[:, e:516:4], 0.0, ["gt%d" % e])
@@ -351,7 +355,8 @@ def rank_program(g, core, T, topo):
     fill(T.rs[:, 4:12], 0.0, ["rs4"])
     quant_g(0)
     quant_g(1)
-    ts(T.eq[:], T.k16[:], pb(QQ), None, A.is_equal, None, ["k16", "pb"], ["eq"])
+    ts(T.kc[:], T.k16a[:], pb(QQ), HUGE, A.not_equal, A.mult, ["k16a", "pb"], ["kc"])
+    ts(T.d0[:], T.k16a[:], 0.0, -2 * HUGE, A.is_equal, A.mult, ["k16a"], ["d0"])
     for b in (0, 1):
         ones_g(b)
 
@@ -360,10 +365,12 @@ def rank_program(g, core, T, topo):
     col(SC, pb(CC), 2.0, -1.0, ["pb"])
     col(SB, pb(CC), -2.0 * TINY, TINY, ["pb"])
     col(CQ, pb(QQ), 513.0, -7680.0, ["pb"])
-    col(P12, pb(PI), 12.0, 0.0, ["pb"])
-    act(T.keep16[:], T.k16[:], F.Sign, ["k16"], ["keep16"])
-    act(T.kc[:], T.eq[:, 0:128], F.Identity, ["eq"], ["kc"], bias=-HUGE, scale=2 * HUGE)
-    act(T.d0[:], T.keep16[:, 0:128], F.Identity, ["keep16"], ["d0"], bias=-HUGE, scale=2 * HUGE)
+    col(S2, pb(CC), 4.0 * ONE, -2.0 * ONE, ["pb"])
+    col(SN, pb(CC), -2.0 * ONE, ONE, ["pb"])
+    col(DD, pb(FL), -1024.0, 512.0, ["pb"])
+    col(G4, pb(PI), HUGE, -HUGE, ["pb"])
+    col(G5, pb(PI), -HUGE, 0.0, ["pb"])
+    col(G6, pc(DD), 1.0, 6 * ONE, pk(DD))
     quant(T.qu[:], T.su[:], T.ut[:], ["ut"], ["qu"])
     quant_g(2)
     pick_u(0, 8, ["uoff0"])
@@ -378,8 +385,15 @@ def rank_program(g, core, T, topo):
     scores(1)
     pick_u(8, 16, ["uoff1"])
     colour_scores(0)
+    ts(T.eq[:], T.k16[:], pb(QQ), None, A.is_equal, None, ["k16", "pb"], ["eq"])
+    act(T.idf[:], T.idc[:, CUT:C], F.Identity, ["idc"] + pk(SN), ["idf"], bias=pc(SN))
+    for k in range(2):
+        act(T.srt[:, 12 + 13 * k:416:26], T.zt[:, 0:16], F.Identity, ["zt"] + pk(G4 + k), ["gap%d" % k], bias=pc(G4 + k))
+    col(G0, pb(PI), pc(G6), -4 * ONE, ["pb"] + pk(G6))
+    col(G2, pb(PI), 2 * ONE, -2 * ONE, ["pb"])
+    col(G3, pb(PI), -2 * ONE, 0.0, ["pb"])
+    col(G7, pc(DD), 1.0, -2 * ONE, pk(DD))
     col(Z0, T.eq[:, 0:1], -BIG, pc(CQ), ["eq"] + pk(CQ))
-    act(T.idf[:], T.idc[:], F.Identity, ["idc"], ["idf"], scale=2.0 ** -21)
     colours(0)
     keep(1)
     keep(0)
@@ -396,9 +410,7 @@ def rank_program(g, core, T, topo):
 
     late = [lambda: ts(T.cst[:], T.cst[:], pc(Z0), None, A.add, None, ["cst%d" % a[0] for a in PAIRS] + pk(Z0), ["cst"])]
     late += [lambda h=h: fill(T.et[:, 521 * h:520 * h + 520:4], 0.0, ["et%d4" % h]) for h in range(2)]
-    late += [lambda: ts(T.dec0[:], T.r24[:, 0:420], pc(P12), -4.0, A.is_equal, A.mult, ["r24"] + pk(P12), ["dec0"])]
     late += [lambda b=b: quant_e(b) for b in range(4)]
-    late += [lambda: ts(T.mka[:], T.par[:], pb(PI), 2.0 ** 21, A.is_equal, A.mult, ["par", "pb"], ["mka"])]
     for e in range(2):
         late += [lambda e=e: fill(T["f%d" % e][:, 0:1], 0.0, ["fz%d" % e]),
                  lambda e=e: fill(T["f%d" % e][:, C + 1:PW + 1], 0.0, ["fy%d" % e])]
@@ -428,63 +440,69 @@ def rank_program(g, core, T, topo):
                 relu(ON_SCALAR[k - 1])
             if k == COLOUR_AT:
                 colours(1)
-                dma("g", T.val[:], T.idf[:], ["idf", "val0", "val1"], ["val", "val0", "val1"], accum_op=A.add)
                 if r:
                     planes(0)
+                else:
+                    for name, pattern in [("keep2", [[0, 72], [1, 2]]), ("k8", [[0, 16], [1, 8]]), ("idp", [[1, M]])]:
+                        iota(T[name][:], pattern, 0, 0, [], [name])
         relu(ON_SCALAR[-1])
         if r == 0:
             act(T.kx[:, 0:C - 1], T.eq[:, 1:C], F.Identity, ["eq"], ["kx"], bias=512.0, scale=-(BIG + 512.0))
             col(OF, T.eq[:, 0:1], BIG, 0.0, ["eq"])
-            col(DD, pb(FL), -(2.0 ** -11), 2.0 ** -12, ["pb"])
+            col(OH, T.eq[:, 0:1], BIG, -0.4375, ["eq"])
+            act(T.dec[:], T.zt[:, 0:456], F.Identity, ["zt"] + pk(DD), ["dec"], bias=pc(DD))
+            col(G1, pc(G0), -1.0, pc(G7), pk(G0, G7))
             col(BO, pb(BH), float(PW), 0.0, ["pb"])
-        for u in range(2):
-            for d in range(max(1, 4 * u), 4 * u + 4):
+        for u, ds, ts_ in ((0, (1, 2, 3, 4), ()), (1, (5, 6, 7), ON_VECTOR[:2])):
+            for d in ds:
                 band(d)
-            for t in ON_VECTOR[2 * u:2 * u + 2]:
+            for t in ts_:
                 compare(t)
             qtile(u)
             for h in range(2):
                 bandrows(u, h)
             for h in range(2):
                 bandcols(u, h, u + h == 0)
-        compare(ON_VECTOR[4])
-        for t in ON_VECTOR[:4]:
-            total(t)
-        for u in (3, 2):
+        for t in ON_VECTOR[2:]:
+            compare(t)
+        spare(1)
+        for u, ts_ in ((3, ON_VECTOR[:2]), (2, ON_VECTOR[2:])):
+            for t in ts_:
+                total(t)
             qtile(u)
             colsum(u, False, False)
-        total(ON_VECTOR[4])
         scan(T.rb[:], T.keep16[:], T.pcl[:, 0:C], 0.0, A.mult, A.subtract, ["keep16", "pcl"], ["rb"])
+        spare(2)
         qtile(4)
         colsum(4, False, True)
         if r:
             planes_out()
-        spare(5)
         tt(T.w1[:], T.cst[:], T.rs[:], A.subtract, ["cst", "rs4"] + ["rs%d" % t for t in ON_SCALAR + ON_VECTOR], ["w1"])
+        spare(1)
         tt(T.kx[:, 15:C:16], T.w1[:], T.rb[:, 15:C:16], A.add, ["w1", "kx", "rb"], ["kx1"])
+        spare(2)
         scan(T.ext[:], T.pd[:, 0:C], T.kx[:], -HUGE, A.max, A.add, ["kx", "kx1", "pd"], ["ext"])
         spare(1)
-        ts(T.poff[:], T.ext[:, 15:C:16], pc(OF), None, A.add, None, ["ext"] + pk(OF), ["poff"])
+        ts(T.poff[:], T.ext[:, 15:C:16], pc(OH), 13.0 / 12.0, A.add, A.mult, ["ext"] + pk(OH), ["poff"])
         spare(2)
         if r == 0:
-            act(T.dec[:], T.dec0[:], F.Identity, ["dec0"] + pk(DD), ["dec"], bias=pc(DD))
+            for k, a in enumerate((0, 13, 12, 25)):
+                act(T.dec[:, a:455:26], T.zt[:, 0:len(range(a, 455, 26))], F.Identity, ["zt", "dec"] + pk(G0 + k),
+                    ["dec%d" % k], bias=pc(G0 + k))
             planes(0, 1, 2, 3)
             planes_out()
             act(T.yt[:, 256:512], T.zt[:, 0:256], F.Copy, ["zt"], ["ytz"])
 
-        cp(T.srt[:, 0:C].indirect(T.poff[:]), T.val[:], ["poff", "val"], ["srt"])
+        cp(T.srt[:, 0:416].indirect(T.poff[:]), T.val[:], ["poff", "val", "val0", "val1", "gap0", "gap1"], ["srt"])
         spare(1)
-        cp(T.srt[:, C:420], T.srt[:, 0:36], ["srt"], ["srt1"])
+        cp(T.srt[:, 416:455], T.srt[:, 0:39], ["srt"], ["srt1"])
         for h, (lo, hi) in enumerate(SCAN):
-            scan(T.scn[:, lo + 24 * h:hi + 24 * h], T.dec[:, lo:hi], T.srt[:, lo:hi], 0.0, A.add, A.max,
-                 ["dec", "srt", "srt%d" % h], ["scn%d" % h])
+            scan(T.scn[:, lo + 26 * h:hi + 26 * h], T.dec[:, lo:hi], T.srt[:, lo:hi], 0.0, A.add, A.max,
+                 ["dec%d" % k for k in range(4)] + ["srt", "srt%d" % h], ["scn%d" % h])
         for h, (a, b) in enumerate(HALF):
-            tt(T.ab[:, 2 * a:2 * b], T.scn[:, 23 + 24 * (a + h):24 * (b + h) + 12:12], T.mka[:, 2 * a:2 * b], A.mult,
-               ["scn%d" % h, "mka"], ["ab%d" % h])
-            spare(1 - h)
-        for h, (a, b) in enumerate(HALF):
-            tt(T.bi[:, a:b], T.ab[:, 2 * a:2 * b:2], T.ab[:, 2 * a + 1:2 * b:2], A.max, ["ab%d" % h], ["bi%d" % h])
-            spare(1 - h)
+            o, n = 26 * (a + h) + 25, 26 * (b - a - 1) + 1
+            tt(T.bi[:, a:b], T.scn[:, o:o + n:26], T.scn[:, o + 13:o + 13 + n:26], A.max, ["scn%d" % h], ["bi%d" % h])
+            spare(2 - 2 * h)
         for h, (a, b) in enumerate(HALF):
             ts(T.bj[:, a:b], T.bi[:, a:b], 511, None, A.bitwise_and, None, ["bi%d" % h], ["bj%d" % h])
             spare(1 - h)
@@ -500,7 +518,7 @@ def rank_program(g, core, T, topo):
                 ["zoff%d" % h, "f1", "f3", "fz1", "fy1"], ["gz1%d" % h], scale=0.25)
         if r == 0:
             act(T.ax[:], T.eq[:], F.Identity, ["eq"], ["ax"], bias=4.0, scale=-132.0)
-        act(T.mv[:], T.val[:], F.Sign, ["val"], ["mv"])
+        act(T.mv[:, CUT:C], T.val[:, CUT:C], F.Sign, ["val", "val1"], ["mv"])
         if r:
             act(T.mo[:], T.pbk[:, 0:C], F.Sign, ["pbk"], ["mo"], bias=-TINY)
         for h, (a, b) in enumerate(HALF):
@@ -520,9 +538,10 @@ def rank_program(g, core, T, topo):
         g.remote_dma(T.ql[:, a:a + M].bitcast(dt.uint8), T.qy[:, 0:M].bitcast(dt.uint8), T.sem["arr%d" % r],
                      T.sem["left%d" % r], pid, rid, mask)
         g.remote_dma(T.sl[:, a:a + M], T.sy[:, 0:M], T.sem["arr%d" % r], T.sem["left%d" % r], pid, rid, mask)
-        count["left%d" % r] = 2 * lanes
-        note("g", ("left%d" % r, 2 * lanes), ["qy"], [])
-        wrote["land%d" % r] = ("arr%d" % r, 2 * lanes)
+        n = 2 * len(lanes)
+        count["left%d" % r] = n
+        note("g", ("left%d" % r, n), ["qy"], [])
+        wrote["land%d" % r] = ("arr%d" % r, n)
 
         if r == 0:
             pick_u(16, 24, ["uoff2"])
@@ -557,7 +576,7 @@ def rank_program(g, core, T, topo):
             quant(T.ql[:, 64:192], T.sl[:, 64:192], T.zt[:], ["zt"], ["qlz0"])
             quant(T.ql[:, 320:448], T.sl[:, 320:448], T.zt[:], ["zt"], ["qlz1"])
         ts(tk(0), T.ext[:, 15:C:16], pc(OG), 1.0 / 3.0, A.add, A.mult, ["ext"] + pk(OG), ["tt0"])
-        scan(T.e1[:], T.ax[:], T.mv[:], 0.0, A.add, A.max, ["ax", "mv"], ["e1"])
+        scan(T.e1[:], T.ax[:], T.mv[:], 0.0, A.add, A.max, ["ax", "mv", "mv0"], ["e1"])
         ts(tk(2), tk(0), FOUR, FOUR, A.add, A.subtract, ["tt0"], ["tt2"])
         scan(T.e2[:], T.ax[:], T.mo[:], 0.0, A.add, A.max, ["ax", "mo"], ["e2"])
         ts(tk(1), T.e1[:, 15:C:16], pc(AL), pc(GA), A.mult, A.add, ["e1"] + pk(AL, GA), ["tt1"])
@@ -632,23 +651,23 @@ def rank_program(g, core, T, topo):
                ["hg%d%d" % (b, k), "pf%d" % b], ["xt%d%d" % (b, k)])
 
         last = r == R - 1
+        first_store = used[0]
         for b in range(2):
             by_kind("v", b)
             by_kind("s", b + 2)
-        for b, k in ((2, 0), (3, 0), (3, 1), (2, 1)):
+        for b, k in ((2, 0), (3, 0), (0, 1), (3, 1), (2, 1)):
             fetch(b, k)
         for b in range(2):
             direct(b, 0)
-        for b in (2, 3):
-            add(b, 0)
-        direct(0, 1)
+        for b, k in ((2, 0), (3, 0), (0, 1)):
+            add(b, k)
         quant_x(T.xt, 0, ["xt%d0" % b for b in range(4)])
         if last:
             mm("pbk", CUT, T.qv[:], T.sv[:], T.qx[:, 0:CUT], T.sx[:, 0:CUT], ["qv", "qx0"])
             dma("y", T.oc[:, 0:4 * CUT], T.qx[:, 0:CUT].bitcast(dt.uint8), ["qx0"], [])
             act(T.ids[:], T.idp[:, 0:M].indirect(T.noff[:]), F.Copy, ["idp"] + NK, ["ids"])
-            act(T.ndb[:], T.ids[:, 0:128].indirect(T.toff[:]), F.Copy, ["ids", "toff"], ["ndb"])
             act(T.ys[:, 0:CUT], T.pbk[:, 0:CUT], F.Copy, ["pbk"], ["ys0"])
+            act(T.ndb[:], T.ids[:, 0:128].indirect(T.toff[:]), F.Copy, ["ids", "toff"], ["ndb"])
             dma("y", T.y[:, 0:CUT], T.ys[:, 0:CUT], ["ys0"], [])
         else:
             scores(0)
@@ -668,9 +687,10 @@ def rank_program(g, core, T, topo):
     mm("pd", C - CUT, T.qv[:], T.sv[:], T.qx[:, CUT:C], T.sx[:, CUT:C], ["qv", "qx1"])
     dma("y", T.oc[:, 4 * CUT:4 * C], T.qx[:, CUT:C].bitcast(dt.uint8), ["qx1"], [])
     for k in range(4):
-        dma("gy"[k % 2], T.osc[4 * k:4 * k + 4, :], T.sx[32 * k:32 * k + 4, :], QX, [])
+        dma("ys"[k % 2], T.osc[4 * k:4 * k + 4, :], T.sx[32 * k:32 * k + 4, :], QX, [])
     cp(T.ys[:, CUT:C], T.pd[:, 0:C - CUT], ["pd"], ["ys1"])
-    dma("y", T.y[:, CUT:C], T.ys[:, CUT:C], ["ys1"], [])
     dma("s", T.nd[:], T.ndb[0:128:16, :], ["ndb"], [])
-    for s in sorted(count):
+    dma("y", T.y[:, CUT:C], T.ys[:, CUT:C], ["ys1"], [])
+    stores = ["d%d" % k for k in range(first_store, used[0])]
+    for s in [s for s in count if s not in stores] + stores:
         g.wait_ge(T.sem[s], count[s])

from concourse.mybir import dt, AluOpType as A, ActivationFunctionType as F, AxisListType

C, NT, M, R = 384, 24, 64, 3
HUGE = 2.0 ** 80
BIG = 2.0 ** 20
TINY = 2.0 ** -120
FOUR = 1.5 * 2.0 ** 25
ONE = 2.0 ** 21
PW = 400
NEAR = 7
SLOTS = [["d1", "d0", "d3", "d2"], ["d5", "d4", "d7", "d6"], [15, 14, 13, 12], [20, 21, 22, 23], [16, 17, 18, 19]]
EARLY = [0, 1, 2, 3]
WIDTH = [400, 320, 192, 256, 192]
ORIGIN = [0, 80]
START = [0, 400, 720, 912, 1168]
QSTART = [0, 528, 848, 1040, 1296]
BLANK = [(0, 0, 48), (1, 0, 32), (0, 384, 400), (1, 304, 320), (2, 80, 176), (3, 208, 256), (4, 144, 192)]
PAIRS = [(0, 4, 0, 64), (4, 8, 16, 64), (8, 12, 0, 112), (12, 24, 16, 192)]
PART = [(0, 128), (128, 256), (256, 384)]
ON_SCALAR = [15, 14, 13, 23, 22, 21, 20, 19, 18, 17, 16]
ON_VECTOR = [12, 0, 1, 2, 3]
COLOUR_AT = 3
SCAN = [(0, 221), (208, 455)]
HALF = [(0, 8), (8, 17)]
CUT = 256
LAND = [0, 192, 256]
VIEW = [0, 128, 256]

BF, F32, I32, U16, X4, U8 = "bfloat16", "float32", "int32", "uint16", "float8_e4m3fn_x4", "uint8"


def _s(n, d):
    return ("sbuf", [128, n], d)


PSUM = ["pa", "pbk", "pcl", "pd", "pf0", "pf1", "pf2", "pf3"]
SCRATCH = {
    "xin": _s(4 * C, BF), "xt": _s(4 * C, BF), "qx": _s(C, X4), "sx": _s(C, U8),
    "ut": _s(512, BF), "qu": _s(128, X4), "su": _s(128, U8), "qur": _s(384, X4), "sur": _s(384, U8),
    "vt": _s(512, BF), "qv": _s(128, X4), "sv": _s(128, U8), "qw": _s(512, X4), "sw": _s(512, U8),
    "pint": _s(1, I32), "ints": _s(8, I32), "pb": _s(8, F32), "pc": _s(44, F32), "t16": _s(NT, F32),
    "uoff": _s(NT, U16), "k16": _s(C, BF), "k16a": _s(128, BF), "jp": _s(128, BF), "gcol": _s(128, BF),
    "idc": _s(C, F32), "idf": _s(128, F32), "keep2": _s(144, BF), "idp": _s(M, BF),
    "eq": _s(C, BF), "kc": _s(128, BF), "d0": _s(128, BF), "ax": _s(C, BF), "keep16": _s(C, BF), "kx": _s(C, F32),
    "dec": _s(456, F32), "cst": _s(NT, F32),
    "et": _s(1040, BF), "qe": _s(768, X4), "se": _s(768, U8),
    "gt": _s(516, BF), "qg": _s(384, X4), "sg": _s(384, U8), "zt": _s(512, BF),
    "d1": _s(C, F32), "bb": _s(C, F32), "o16": _s(C, F32),
    "mt": _s(4 * 1424, BF), "qm": _s(1552, X4), "sm": _s(1552, U8),
    "sgn": _s(2400, BF), "rs": _s(NT, F32), "rb": _s(C, F32), "w1": _s(NT, F32), "val": _s(C, F32),
    "ext": _s(C, F32), "poff": _s(NT, U16),
    "srt": _s(456, F32), "scn": _s(484, F32), "tq": _s(8, F32), "bi": _s(17, I32), "bj": _s(17, I32),
    "zoff": _s(18, U16), "f0": _s(2 * PW, BF), "f1": _s(2 * PW, BF), "gz": _s(544, BF), "zz": _s(544, BF),
    "yt": _s(512, BF), "qy": _s(128, X4), "sy": _s(128, U8), "ql": _s(448, X4), "sl": _s(448, U8),
    "ht": _s(512, BF), "qh": _s(128, X4), "sh": _s(128, U8), "hp": _s(256, BF), "hs": _s(512, BF),
    "hg": _s(4 * C, BF), "vd": _s(128, F32), "vb": _s(128, F32), "k8": _s(128, BF), "kd0": _s(128, BF),
    "kd": _s(128, BF), "d8": _s(128, BF), "n0": _s(8, F32), "n1": _s(8, F32), "noff": _s(8, U16),
    "mv": _s(C, BF), "mo": _s(C, BF), "e1": _s(C, BF), "e2": _s(C, BF), "tt": _s(6 * NT, F32),
    "toff": _s(NT, U16), "ids": _s(128, BF), "ndb": _s(C, F32), "ys": _s(C, F32),
}
SCRATCH.update({k: ("psum", [128, 512], F32) for k in PSUM})
SEMAPHORES = (["cv", "cs", "ct", "cg"] + ["arr%d" % r for r in range(R)] + ["left%d" % r for r in range(R)]
              + ["d%d" % k for k in range(28)])


def rank_program(g, core, T, topo):
    rank = T.rank_of(core)
    if rank is None:
        return
    nxt = T.cores[(rank + 1) % len(T.cores)]
    rid, pid = topo.addr(nxt)[0], topo.addr(nxt)[1]
    mask = topo.mask(core, nxt)
    lanes = topo.engines(core, nxt)

    queue = {"v": g.vector, "s": g.scalar, "t": g.tensor, "g": g, "y": g.sync}
    count = {"cv": 0, "cs": 0, "ct": 0, "cg": 0}
    known = {k: {} for k in queue}
    clock, wrote, read, used = {}, {}, {}, [0]

    def after(q, events):
        need = {}
        for s, c in events:
            if known[q].get(s, 0) < c and need.get(s, 0) < c:
                need[s] = c
        for s, c in sorted(need.items()):
            if any(o != s and clock.get((o, d), {}).get(s, 0) >= c for o, d in need.items()):
                continue
            queue[q].wait_ge(T.sem[s], c)
        for s, c in need.items():
            for o, d in list(clock.get((s, c), {}).items()) + [(s, c)]:
                if known[q].get(o, 0) < d:
                    known[q][o] = d

    def order(q, rd, wr, skip=()):
        ev = []
        for k in rd:
            if k in wrote:
                ev.append(wrote[k])
            if k in PSUM:
                ev += [e for e in read.get(k, []) if e[0] != "c" + q]
        for k in wr:
            if k in wrote and k not in skip:
                ev.append(wrote[k])
            ev += read.get(k, [])
        after(q, ev)

    def note(q, e, rd, wr):
        clock[e] = dict(known[q])
        for k in rd:
            read.setdefault(k, []).append(e)
        for k in wr:
            wrote[k] = e
            read[k] = []

    def op(q, rd, wr, call, skip=()):
        order(q, rd, wr, skip)
        s = "c" + q
        count[s] += 1
        call().then_inc(T.sem[s], 1)
        note(q, (s, count[s]), rd, wr)

    def dma(q, out, in_, rd, wr, **kw):
        order(q, rd, wr)
        s = "d%d" % used[0]
        used[0] += 1
        count[s] = 16
        queue[q].dma_start(out, in_, **kw).then_inc(T.sem[s], 16)
        note(q, (s, 16), rd, wr)

    V, S, P = g.vector, g.scalar, g.tensor

    def ts(out, in0, s1, s2, o0, o1, rd, wr):
        if o1 is None:
            op("v", rd, wr, lambda: V.tensor_scalar(out, in0, s1, None, o0))
        else:
            op("v", rd, wr, lambda: V.tensor_scalar(out, in0, s1, s2, o0, o1))

    def tt(out, a, b, o, rd, wr):
        op("v", rd, wr, lambda: V.tensor_tensor(out, a, b, o))

    def cp(out, in_, rd, wr):
        op("v", rd, wr, lambda: V.tensor_copy(out, in_))

    def scan(out, a, b, init, o0, o1, rd, wr):
        op("v", rd, wr, lambda: V.tensor_tensor_scan(out, a, b, init, o0, o1))

    def fill(ap, c, wr):
        op("v", [], wr, lambda: V.memset(ap, c))

    def quant(q, s, in_, rd, wr):
        op("v", rd, wr, lambda: V.quantize_mx(q, s, in_))

    def act(out, in_, f, rd, wr, bias=0.0, scale=1.0, acc=None):
        if f == F.Copy:
            op("s", rd, wr, lambda: S.activation(out, in_, f))
        elif acc is None:
            op("s", rd, wr, lambda: S.activation(out, in_, f, bias=bias, scale=scale))
        else:
            op("s", rd, wr, lambda: S.activation(out, in_, f, bias=bias, scale=scale, accum_out=acc))

    def mm(bank, n, wq, ws, xq, xs, rd, start=True, stop=True):
        op("t", rd, [bank], lambda: P.matmul_mx(T[bank][:, 0:n], wq, ws, xq, xs, start, stop),
           skip=() if start else (bank,))

    def iota(ap, pattern, base, cm, rd, wr):
        op("g", rd, wr, lambda: g.iota(ap, pattern, base, cm, allow_small_or_imprecise_dtypes=True))

    def pb(k):
        return T.pb[:, k:k + 1]

    def pc(k):
        return T.pc[:, k:k + 1]

    def pk(*ks):
        return ["pc%d" % k for k in ks]

    def col(k, src, scale, bias, rd):
        act(pc(k), src, F.Identity, rd, pk(k), bias=bias, scale=scale)

    QQ, PI, CC, BH, FL, GG, Q4 = range(7)
    SC, SB, BO, DD, OH, CQ, NO, Z0 = range(8)
    DCO, TA, TS_, TB, CA, QM, CB, WK, HH, AL, X1, GA = range(8, 20)
    X2, QN, OF, OG, CP, DF, DF0, WR, TH, B0, B1, RC = range(20, 32)
    S2, SN, G0, G1, G2, G3, G4, G5, G6, G7 = range(32, 42)

    US = (T.qur[:, 0:128], T.sur[:, 0:128])
    UC = (T.qur[:, 128:256], T.sur[:, 128:256])
    UD = (T.qur[:, 256:384], T.sur[:, 256:384])
    UK = ["qur0", "sur0"]
    QX = ["qx0", "qx1"]
    NK = ["noff", "noff0"]
    RB = ["pa", "pd", "pcl", "pbk"]
    PIECE = [(0, CUT), (CUT, C)]

    def fplane(b, lo=0, hi=C):
        o = PW * (b // 2) + 1
        return T["f%d" % (b % 2)][:, o + lo:o + hi]

    def slot(t, lo, hi):
        t = 15 - t if t in EARLY else t
        for u in range(5):
            if t in SLOTS[u]:
                a = 4 * START[u] + SLOTS[u].index(t)
                return T.mt[:, a + 4 * lo:a + 4 * hi - 3:4]

    def names(u):
        return ["m%s" % t for t in SLOTS[u]] + (["md0_"], [], ["m%d" % t for t in EARLY], [], [])[u]

    def reach(t):
        return 16 * (t - NEAR)

    def blank(u, lo, hi):
        act(T.mt[:, 4 * (START[u] + lo):4 * (START[u] + hi)], T.zt[:, 0:4 * (hi - lo)], F.Copy, ["zt"], names(u))

    def qtile(u):
        a, b, n = START[u], QSTART[u], WIDTH[u]
        quant(T.qm[:, b:b + n], T.sm[:, b:b + n], T.mt[:, 4 * a:4 * (a + n)], names(u), ["qm%d" % u])

    def const(name, k):
        return T["q" + name][:, 128 * k:128 * k + 128], T["s" + name][:, 128 * k:128 * k + 128]

    def colsum(u, start, stop):
        b, n = QSTART[u], WIDTH[u]
        mm("pd", n, *const("g", 2), T.qm[:, b:b + n], T.sm[:, b:b + n], ["qg2", "qm%d" % u], start, stop)

    def bandcols(u, h, start=False):
        d = 4 * u + 2 * h
        a, n = QSTART[u] - ORIGIN[u] + 16 * (d + 1), C - 16 * d
        mm("pd", n, *const("g", h), T.qm[:, a:a + n], T.sm[:, a:a + n], ["qg%d" % h, "qm%d" % u], start, False)

    def bandrows(u, h):
        a = QSTART[u] - ORIGIN[u] + 16 * h
        mm("pcl", C, *const("e", 4 + h), T.qm[:, a:a + C], T.sm[:, a:a + C], ["qe%d" % (4 + h), "qm%d" % u, "qmz"],
           (u, h) == (0, 0), (u, h) == (1, 1))

    def band(d, lo=0, hi=C, part=""):
        lo = max(lo, 16 * d)
        src = "o16" if d else "bb"
        a = 16 * (1 - d % 2) - ORIGIN[d // 4]
        tt(slot("d%d" % d, lo + a, hi + a), T[src][:, lo:hi], T.pa[:, lo - 16 * d:hi - 16 * d], A.is_gt,
           ["pa"] + ["%s%d" % (src, k) for k in range(3) if lo < PART[k][1] and hi > PART[k][0]],
           ["md%d%s" % (d, part)])

    def sgn(t):
        a = sum(reach(k) for k in ON_SCALAR if k < t)
        return T.sgn[:, a:a + reach(t)]

    def sign(t):
        act(sgn(t), T.pbk[:, 0:reach(t)], F.Sign, ["pbk", "bb%d" % (t // 8)], ["sgn%d" % t],
            bias=T.bb[:, 16 * t:16 * t + 1], scale=-1.0)

    def relu(t):
        act(slot(t, 0, reach(t)), sgn(t), F.Relu, ["sgn%d" % t], ["m%d" % t, "rs%d" % t], acc=T.rs[:, t:t + 1])

    def span(t):
        return (16 * (t + NEAR + 1), 192) if t in EARLY else (0, reach(t))

    def compare(t):
        lo, hi = span(t)
        ts(slot(t, lo, hi), T.pa[:, lo:hi], T.bb[:, 16 * t:16 * t + 1], None, A.is_le if t in EARLY else A.is_lt, None,
           ["pa", "bb%d" % (t // 8)], ["m%d" % t])

    def total(t):
        op("v", ["m%d" % t], ["rs%d" % t],
           lambda: V.tensor_reduce(T.rs[:, t:t + 1], slot(t, *span(t)), AxisListType.X, A.add))

    def keep(k):
        lo, hi = PART[k]
        bank, a = [("pbk", 0), ("pbk", 128), ("pd", 0)][k]
        tt(T.d1[:, lo:hi], T[bank][:, a:a + 128], T.kc[:], A.subtract, [bank, "kc"], ["d1%d" % k])

    def hold(k):
        lo, hi = PART[k]
        back = slice(hi - 1, lo - 1 if lo else None, -1)
        scan(T.bb[:, back], T.d0[:], T.d1[:, back], -HUGE, A.add, A.max, ["d0", "d1%d" % k], ["bb%d" % k])

    def spread(k):
        lo, hi = PART[k]
        scan(T.o16[:, lo:hi], T.d0[:], T.bb[:, lo:hi], -HUGE, A.add, A.max, ["d0", "bb%d" % k], ["o16%d" % k])

    def quant_x(src, k, rd):
        lo, hi = PIECE[k]
        quant(T.qx[:, lo:hi], T.sx[:, lo:hi], src[:, 4 * lo:4 * hi], rd, ["qx%d" % k])

    def scores(k):
        lo, hi = PIECE[k]
        mm(("pbk", "pd")[k], hi - lo, US[0], US[1], T.qx[:, lo:hi], T.sx[:, lo:hi], UK + ["qx%d" % k])

    def colours(k):
        if k == 0:
            act(T.mv[:, 0:CUT], T.pcl[:, 0:CUT], F.Sign, ["pcl"] + pk(SC, SB), ["mv0"], bias=pc(SB), scale=pc(SC))
            act(T.val[:, 0:CUT], T.mv[:, 0:CUT], F.Identity, ["mv0"], ["val", "val0"], scale=ONE)
            dma("g", T.val[:, 0:CUT], T.idc[:, 0:CUT], ["idc", "val0"], ["val0"], accum_op=A.add)
        else:
            ts(T.val[:, CUT:C], T.pf0[:, 0:C - CUT], 0.0, pc(S2), A.is_gt, A.mult, ["pf0"] + pk(S2), ["val", "val1"])
            dma("g", T.val[:, CUT:C], T.idf[:], ["idf", "val1"], ["val1"], accum_op=A.add)

    def colour_scores(k):
        lo, hi = PIECE[k]
        mm(("pcl", "pf0")[k], hi - lo, UC[0], UC[1], T.qx[:, lo:hi], T.sx[:, lo:hi], ["qur8", "sur8", "qx%d" % k])

    def tk(k):
        return T.tt[:, NT * k:NT * k + NT]

    def pick_u(a, b, rd):
        cp(T.qur[:, 16 * a:16 * b].bitcast(dt.uint32), T.qu[:, 0:128].bitcast(dt.uint32).indirect(T.uoff[:, a:b]),
           ["qu"] + rd, ["qur%d" % a])
        act(T.sur[:, 16 * a:16 * b], T.su[:, 0:128].indirect(T.uoff[:, a:b]), F.Copy, ["qu"] + rd, ["sur%d" % a])

    def quant_e(b):
        o = 520 * (b % 2) + (0 if b // 2 == 1 else 2)
        quant(*const("e", b), T.et[:, o:o + 512], ["et%d%d" % (b % 2, a) for a in (0, 2, 4)], ["qe%d" % b])

    def quant_g(k):
        o = 0 if k else 2
        quant(*const("g", k), T.gt[:, o:o + 512], ["gt%d" % b for b in range(4)], ["qg%d" % k])

    dma("s", T.ut[:], T.u[:], [], ["ut"])
    dma("y", T.xin[:, 0:4 * CUT], T.x[:, 0:4 * CUT], [], ["xin0"])
    dma("y", T.xin[:, 4 * CUT:4 * C], T.x[:, 4 * CUT:4 * C], [], ["xin1"])

    op("g", [], ["pint"], lambda: g.iota(T.pint[:], [[0, 1]], 0, 1))
    for name, pattern, base, cm in [
            ("jp", [[1, 128]], 0, -1), ("gcol", [[1, 8], [0, 16]], 0, 0), ("t16", [[16, NT]], 0, 0),
            ("k16a", [[0, 8], [1, 16]], 0, 0), ("k16", [[0, NT], [1, 16]], 0, 0), ("idc", [[1, C]], 1, 0)]:
        iota(T[name][:], pattern, base, cm, [], [name])
    for a, b, step, base in PAIRS:
        iota(T.cst[:, a:b], [[step, b - a]], base, 0, [], ["cst%d" % a])

    def ones_e(h, a):
        o = 520 * h + a + h
        ts(T.et[:, o:o + 512:4], T.jp[:], 0.0, None, A.is_equal, None, ["jp"], ["et%d%d" % (h, a)])

    def ones_g(b):
        ts(T.gt[:, b:512:4], T.gcol[:], pb(GG), None, A.is_equal, None, ["gcol", "pb"], ["gt%d" % b])

    fill(T.zt[:], 0.0, ["zt"])
    op("g", ["zt"], ["keep16"],
       lambda: g.affine_select(T.keep16[:], T.zt[:, 0:C], [[0, NT], [1, 16]], A.is_equal, 1.0, 0, 0))
    for e in range(2):
        fill(T.et[:, 520 * e + 1 - e:520 * e + 520:2], 0.0, ["et%d0" % e])
        fill(T.gt[:, e:516:4], 0.0, ["gt%d" % e])
    for k, (sh, mk) in enumerate([(0, 15), (3, 1), (2, 1), (1, 1), (0, 1), (4, 7), (2, 3)]):
        ts(T.ints[:, k:k + 1], T.pint[:], sh, mk, A.arith_shift_right, A.bitwise_and, ["pint"], ["ints%d" % k])
    for a in (2, 4):
        for h in range(2):
            ones_e(h, a)
    cp(T.pb[:, 0:7], T.ints[:, 0:7], ["ints%d" % k for k in range(7)], ["pb"])
    quant_e(4)
    quant_e(5)
    for b in (2, 3):
        ones_g(b)
    cp(T.uoff[:, 0:8], T.t16[:, 0:8], ["t16"], ["uoff0"])
    ts(T.uoff[:, 8:16], T.t16[:, 0:8], pb(PI), 1.0, A.add, A.add, ["t16", "pb"], ["uoff1"])
    fill(T.rs[:, 4:12], 0.0, ["rs4"])
    quant_g(0)
    quant_g(1)
    ts(T.kc[:], T.k16a[:], pb(QQ), HUGE, A.not_equal, A.mult, ["k16a", "pb"], ["kc"])
    ts(T.d0[:], T.k16a[:], 0.0, -2 * HUGE, A.is_equal, A.mult, ["k16a"], ["d0"])
    for b in (0, 1):
        ones_g(b)

    for b in BLANK:
        blank(*b)
    col(SC, pb(CC), 2.0, -1.0, ["pb"])
    col(SB, pb(CC), -2.0 * TINY, TINY, ["pb"])
    col(CQ, pb(QQ), 513.0, -7680.0, ["pb"])
    col(S2, pb(CC), 4.0 * ONE, -2.0 * ONE, ["pb"])
    col(SN, pb(CC), -2.0 * ONE, ONE, ["pb"])
    col(DD, pb(FL), -1024.0, 512.0, ["pb"])
    col(G4, pb(PI), HUGE, -HUGE, ["pb"])
    col(G5, pb(PI), -HUGE, 0.0, ["pb"])
    col(G6, pc(DD), 1.0, 6 * ONE, pk(DD))
    quant(T.qu[:], T.su[:], T.ut[:], ["ut"], ["qu"])
    quant_g(2)
    pick_u(0, 8, ["uoff0"])

    dma("y", T.qw[:].bitcast(dt.uint8), T.wc[:], ["xin1"], ["qw"])
    dma("y", T.sw[:], T.ws[:], [], ["sw"])
    dma("y", T.vt[:], T.v[:], [], ["vt"])

    quant_x(T.xin, 0, ["xin0"])
    scores(0)
    quant_x(T.xin, 1, ["xin1"])
    scores(1)
    pick_u(8, 16, ["uoff1"])
    colour_scores(0)
    ts(T.eq[:], T.k16[:], pb(QQ), None, A.is_equal, None, ["k16", "pb"], ["eq"])
    act(T.idf[:], T.idc[:, CUT:C], F.Identity, ["idc"] + pk(SN), ["idf"], bias=pc(SN))
    for k in range(2):
        act(T.srt[:, 12 + 13 * k:416:26], T.zt[:, 0:16], F.Identity, ["zt"] + pk(G4 + k), ["gap%d" % k], bias=pc(G4 + k))
    col(G0, pb(PI), pc(G6), -4 * ONE, ["pb"] + pk(G6))
    col(G2, pb(PI), 2 * ONE, -2 * ONE, ["pb"])
    col(G3, pb(PI), -2 * ONE, 0.0, ["pb"])
    col(G7, pc(DD), 1.0, -2 * ONE, pk(DD))
    col(Z0, T.eq[:, 0:1], -BIG, pc(CQ), ["eq"] + pk(CQ))
    colours(0)
    keep(1)
    keep(0)
    quant(T.qm[:, QSTART[1] - 128:QSTART[1]], T.sm[:, QSTART[1] - 128:QSTART[1]], T.zt[:], ["zt"], ["qmz"])
    hold(1)

    def planes(*bs):
        for b in bs:
            mm("pf%d" % b, C, *const("e", b), T.qx[:], T.sx[:], ["qe%d" % b] + QX)

    def planes_out():
        for b in (0, 2, 3, 1):
            act(fplane(b), T["pf%d" % b][:, 0:C], F.Copy, ["pf%d" % b], ["f%d" % b])

    late = [lambda: ts(T.cst[:], T.cst[:], pc(Z0), None, A.add, None, ["cst%d" % a[0] for a in PAIRS] + pk(Z0), ["cst"])]
    late += [lambda h=h: fill(T.et[:, 521 * h:520 * h + 520:4], 0.0, ["et%d4" % h]) for h in range(2)]
    late += [lambda b=b: quant_e(b) for b in range(4)]
    for e in range(2):
        late += [lambda e=e: fill(T["f%d" % e][:, 0:1], 0.0, ["fz%d" % e]),
                 lambda e=e: fill(T["f%d" % e][:, C + 1:PW + 1], 0.0, ["fy%d" % e])]
    late += [lambda: ts(T.uoff[:, 16:24], T.t16[:, 0:8], pb(PI), 2.0, A.subtract, A.add, ["t16", "pb"], ["uoff2"])]

    def spare(n):
        for _ in range(min(n, len(late))):
            late.pop(0)()

    for r in range(R):
        mm("pa", C, US[0], US[1], T.qx[:], T.sx[:], UK + QX)
        colour_scores(1)
        if r:
            planes(1, 2, 3)

        hold(0)
        spread(1)
        keep(2)
        spread(0)
        hold(2)
        band(0, 0, CUT)
        spread(2)
        band(0, CUT, C, "_")
        for k, t in enumerate(ON_SCALAR):
            sign(t)
            if k:
                relu(ON_SCALAR[k - 1])
            if k == COLOUR_AT:
                colours(1)
                if r:
                    planes(0)
                else:
                    for name, pattern in [("keep2", [[0, 72], [1, 2]]), ("k8", [[0, 16], [1, 8]]), ("idp", [[1, M]])]:
                        iota(T[name][:], pattern, 0, 0, [], [name])
        relu(ON_SCALAR[-1])
        if r == 0:
            act(T.kx[:, 0:C - 1], T.eq[:, 1:C], F.Identity, ["eq"], ["kx"], bias=512.0, scale=-(BIG + 512.0))
            col(OF, T.eq[:, 0:1], BIG, 0.0, ["eq"])
            col(OH, T.eq[:, 0:1], BIG, -0.4375, ["eq"])
            act(T.dec[:], T.zt[:, 0:456], F.Identity, ["zt"] + pk(DD), ["dec"], bias=pc(DD))
            col(G1, pc(G0), -1.0, pc(G7), pk(G0, G7))
            col(BO, pb(BH), float(PW), 0.0, ["pb"])
        for u, ds, ts_ in ((0, (1, 2, 3, 4), ()), (1, (5, 6, 7), ON_VECTOR[:2])):
            for d in ds:
                band(d)
            for t in ts_:
                compare(t)
            qtile(u)
            for h in range(2):
                bandrows(u, h)
            for h in range(2):
                bandcols(u, h, u + h == 0)
        for t in ON_VECTOR[2:]:
            compare(t)
        spare(1)
        for u, ts_ in ((3, ON_VECTOR[:2]), (2, ON_VECTOR[2:])):
            for t in ts_:
                total(t)
            qtile(u)
            colsum(u, False, False)
        scan(T.rb[:], T.keep16[:], T.pcl[:, 0:C], 0.0, A.mult, A.subtract, ["keep16", "pcl"], ["rb"])
        spare(2)
        qtile(4)
        colsum(4, False, True)
        if r:
            planes_out()
        tt(T.w1[:], T.cst[:], T.rs[:], A.subtract, ["cst", "rs4"] + ["rs%d" % t for t in ON_SCALAR + ON_VECTOR], ["w1"])
        spare(1)
        tt(T.kx[:, 15:C:16], T.w1[:], T.rb[:, 15:C:16], A.add, ["w1", "kx", "rb"], ["kx1"])
        spare(2)
        scan(T.ext[:], T.pd[:, 0:C], T.kx[:], -HUGE, A.max, A.add, ["kx", "kx1", "pd"], ["ext"])
        spare(1)
        ts(T.poff[:], T.ext[:, 15:C:16], pc(OH), 13.0 / 12.0, A.add, A.mult, ["ext"] + pk(OH), ["poff"])
        spare(2)
        if r == 0:
            for k, a in enumerate((0, 13, 12, 25)):
                act(T.dec[:, a:455:26], T.zt[:, 0:len(range(a, 455, 26))], F.Identity, ["zt", "dec"] + pk(G0 + k),
                    ["dec%d" % k], bias=pc(G0 + k))
            planes(0, 1, 2, 3)
            planes_out()
            act(T.yt[:, 256:512], T.zt[:, 0:256], F.Copy, ["zt"], ["ytz"])

        cp(T.srt[:, 0:416].indirect(T.poff[:]), T.val[:], ["poff", "val", "val0", "val1", "gap0", "gap1"], ["srt"])
        spare(1)
        cp(T.srt[:, 416:455], T.srt[:, 0:39], ["srt"], ["srt1"])
        for h, (lo, hi) in enumerate(SCAN):
            scan(T.scn[:, lo + 26 * h:hi + 26 * h], T.dec[:, lo:hi], T.srt[:, lo:hi], 0.0, A.add, A.max,
                 ["dec%d" % k for k in range(4)] + ["srt", "srt%d" % h], ["scn%d" % h])
        for h, (a, b) in enumerate(HALF):
            o, n = 26 * (a + h) + 25, 26 * (b - a - 1) + 1
            tt(T.bi[:, a:b], T.scn[:, o:o + n:26], T.scn[:, o + 13:o + 13 + n:26], A.max, ["scn%d" % h], ["bi%d" % h])
            spare(2 - 2 * h)
        for h, (a, b) in enumerate(HALF):
            ts(T.bj[:, a:b], T.bi[:, a:b], 511, None, A.bitwise_and, None, ["bi%d" % h], ["bj%d" % h])
            spare(1 - h)
        for h, (a, b) in enumerate(HALF):
            ts(T.zoff[:, a:b], T.bj[:, a:b], pc(BO), None, A.add, None, ["bj%d" % h] + pk(BO), ["zoff%d" % h])
            spare(2 - 2 * h)
        if r:
            mm("pbk", C, UD[0], UD[1], T.qx[:], T.sx[:], ["qur16", "sur16"] + QX)
        for h, (a, b) in enumerate(HALF):
            ts(T.gz[:, 16 * a:16 * b], T.f0[:, 0:PW + C + 1].indirect(T.zoff[:, a:b]), 0.25, None, A.mult, None,
               ["zoff%d" % h, "f0", "f2", "fz0", "fy0"], ["gz0%d" % h])
            act(T.gz[:, 272 + 16 * a:272 + 16 * b], T.f1[:, 0:PW + C + 1].indirect(T.zoff[:, a:b]), F.Identity,
                ["zoff%d" % h, "f1", "f3", "fz1", "fy1"], ["gz1%d" % h], scale=0.25)
        if r == 0:
            act(T.ax[:], T.eq[:], F.Identity, ["eq"], ["ax"], bias=4.0, scale=-132.0)
        act(T.mv[:, CUT:C], T.val[:, CUT:C], F.Sign, ["val", "val1"], ["mv"])
        if r:
            act(T.mo[:], T.pbk[:, 0:C], F.Sign, ["pbk"], ["mo"], bias=-TINY)
        for h, (a, b) in enumerate(HALF):
            for e in range(2):
                o = slice(272 * e + 16 * a, 272 * e + 16 * b)
                scan(T.zz[:, o], T.keep2[:, 0:16 * (b - a)], T.gz[:, o], 0.0, A.mult, A.add,
                     ["keep2", "gz%d%d" % (e, h)], ["zz%d%d" % (e, h)])
        for h, (a, b) in enumerate([(0, 120), (120, 256)]):
            for e in range(2):
                o = 272 * e
                tt(T.yt[:, a + e:b:2], T.zz[:, o + a + 1:o + b:2], T.zz[:, o + a + 9:o + b + 8:2], A.add,
                   ["zz%d0" % e, "zz%d%d" % (e, h)], ["yt%d%d" % (e, h)])
        quant(T.qy[:], T.sy[:], T.yt[:], ["yt00", "yt10", "yt01", "yt11", "ytz"], ["qy"])

        order("g", ["qy"], [])
        a = LAND[r]
        g.remote_dma(T.ql[:, a:a + M].bitcast(dt.uint8), T.qy[:, 0:M].bitcast(dt.uint8), T.sem["arr%d" % r],
                     T.sem["left%d" % r], pid, rid, mask)
        g.remote_dma(T.sl[:, a:a + M], T.sy[:, 0:M], T.sem["arr%d" % r], T.sem["left%d" % r], pid, rid, mask)
        n = 2 * len(lanes)
        count["left%d" % r] = n
        note("g", ("left%d" % r, n), ["qy"], [])
        wrote["land%d" % r] = ("arr%d" % r, n)

        if r == 0:
            pick_u(16, 24, ["uoff2"])
            mm("pbk", C, UD[0], UD[1], T.qx[:], T.sx[:], ["qur16", "sur16"] + QX)
            col(OG, pc(OF), 1.0, -5.5, pk(OF))
            col(WK, pb(PI), 0.5, 0.5, ["pb"])
            col(HH, pb(PI), -0.5, 1.0, ["pb"])
            col(NO, pb(QQ), 4.0, -60.0, ["pb"])
            col(DCO, pb(BH), -1.0, pb(FL), ["pb"])
            col(AL, pc(HH), pc(SC), 0.0, pk(HH, SC))
            col(X2, pc(HH), 1.0, pc(WK), pk(HH, WK))
            col(TS_, pb(BH), 1.0, pb(FL), ["pb"])
            col(X1, pc(AL), 1.0, pc(WK), pk(AL, WK))
            col(QM, pb(Q4), 2.0, 0.0, ["pb"])
            col(QN, pb(Q4), 2.0, -2.0, ["pb"])
            col(GA, pc(X1), pc(NO), pc(X2), pk(X1, NO, X2))
            act(T.mo[:], T.pbk[:, 0:C], F.Sign, ["pbk"], ["mo"], bias=-TINY)
            col(TA, pc(DCO), pb(CC), pb(BH), ["pb"] + pk(DCO))
            act(pc(WR), pb(Q4), F.Relu, ["pb"], pk(WR), bias=1.0, scale=-1.0)
            act(T.kd[:], T.k8[:], F.Sign, ["k8"], ["kd"])
            col(TB, pc(TA), -1.0, pc(TS_), pk(TA, TS_))
            col(CA, pc(TA), 1.0, pc(QM), pk(TA, QM))
            col(TH, pc(WR), -TINY, 0.0, pk(WR))
            col(CB, pc(TB), 1.0, pc(QN), pk(TB, QN))
            col(CP, pc(TB), 1.0, pc(QM), pk(TB, QM))
            act(T.d8[:], T.kd[:], F.Identity, ["kd"], ["d8"], bias=-HUGE, scale=2 * HUGE)
            col(DF, pc(CB), -1.0, pc(CA), pk(CA, CB))
            col(B1, pc(CB), 1.0, 0.25, pk(CB))
            act(T.ht[:, 256:512], T.zt[:, 0:256], F.Copy, ["zt"], ["htz"])
            col(DF0, pc(WR), -float(M), pc(DF), pk(WR, DF))
            col(B0, pc(WR), float(M), pc(B1), pk(WR, B1))
            quant(T.ql[:, 64:192], T.sl[:, 64:192], T.zt[:], ["zt"], ["qlz0"])
            quant(T.ql[:, 320:448], T.sl[:, 320:448], T.zt[:], ["zt"], ["qlz1"])
        ts(tk(0), T.ext[:, 15:C:16], pc(OG), 1.0 / 3.0, A.add, A.mult, ["ext"] + pk(OG), ["tt0"])
        scan(T.e1[:], T.ax[:], T.mv[:], 0.0, A.add, A.max, ["ax", "mv", "mv0"], ["e1"])
        ts(tk(2), tk(0), FOUR, FOUR, A.add, A.subtract, ["tt0"], ["tt2"])
        scan(T.e2[:], T.ax[:], T.mo[:], 0.0, A.add, A.max, ["ax", "mo"], ["e2"])
        ts(tk(1), T.e1[:, 15:C:16], pc(AL), pc(GA), A.mult, A.add, ["e1"] + pk(AL, GA), ["tt1"])
        if r == 0:
            op("v", pk(DF), pk(RC), lambda: V.reciprocal(pc(RC), pc(DF)))
        ts(tk(4), T.e2[:, 15:C:16], pc(WK), None, A.mult, None, ["e2"] + pk(WK), ["tt4"])
        tt(tk(3), tk(1), tk(2), A.add, ["tt1", "tt2"], ["tt3"])
        if r == 0:
            ts(T.kd0[:, 0:M], T.k8[:, 0:M], pc(CA), 0.5, A.is_equal, A.subtract, ["k8"] + pk(CA), ["kd00"])
            ts(T.kd0[:, M:128], T.k8[:, 0:M], pc(CP), 0.5, A.is_equal, A.subtract, ["k8"] + pk(CP), ["kd01"])
            act(T.kd[:], T.kd0[:], F.Identity, ["kd00", "kd01"], ["kd"], scale=2 * HUGE)
        tt(tk(5), tk(3), tk(4), A.add, ["tt3", "tt4"], ["tt5"])
        if r == 0:
            ts(T.tq[:], T.t16[:, 0:8], 0.5, pc(RC), A.mult, A.mult, ["t16"] + pk(RC), ["tq"])
        if r == 1:
            quant(T.qv[:], T.sv[:], T.vt[:], ["vt"], ["qv"])
        cp(T.toff[:], tk(5), ["tt5"], ["toff"])

        w0 = VIEW[r]
        o = LAND[r] - VIEW[r]
        for b in (2, 0, 3, 1):
            mm(RB[b], 128, T.qw[:, 128 * b:128 * b + 128], T.sw[:, 128 * b:128 * b + 128],
               T.ql[:, w0:w0 + 128], T.sl[:, w0:w0 + 128], ["qw", "sw", "land%d" % r, "qlz0", "qlz1"])
        for b in (2, 0, 3, 1):
            src = T[RB[b]][:, o:o + M]
            if b < 2:
                ts(T.ht[:, b:256:4], src, 0.03125, None, A.mult, None, [RB[b]], ["ht%d" % b])
            else:
                act(T.ht[:, b:256:4], src, F.Identity, [RB[b]], ["ht%d" % b], scale=0.03125)
        quant(T.qh[:], T.sh[:], T.ht[:], ["ht0", "ht1", "ht2", "ht3", "htz"], ["qh"])
        mm("pcl", 128, US[0], US[1], T.qh[:], T.sh[:], UK + ["qh"])
        for b in range(4):
            act(T.hp[:, M * b:M * b + M], T.ht[:, b:256:4], F.Copy, ["ht%d" % b], ["hp%d" % b])

        tt(T.vd[:, 0:M], T.pcl[:, 0:M], T.kd[:, 0:M], A.min, ["pcl", "kd"], ["vd0"])
        tt(T.vd[:, M + 2:128], T.pcl[:, 0:M - 2], T.kd[:, M + 2:128], A.min, ["pcl", "kd"], ["vd1"])
        tt(T.vd[:, M:M + 2], T.pcl[:, M - 2:M], T.kd[:, M:M + 2], A.min, ["pcl", "kd"], ["vd2"])
        scan(T.vb[:, 0:M], T.d8[:, 0:M], T.vd[:, 0:M], -HUGE, A.min, A.max, ["d8", "vd0"], ["vb0"])
        scan(T.vb[:, M:128], T.d8[:, 0:M], T.vd[:, M:128], -HUGE, A.min, A.max, ["d8", "vd1", "vd2"], ["vb1"])
        tt(T.n0[:, 1:8], T.vb[:, 15:M:8], T.vb[:, M + 15:128:8], A.is_gt, ["vb0", "vb1"], ["n0"])
        ts(T.n0[:, 0:1], T.vb[:, 7:8], T.vb[:, M + 7:M + 8], pc(TH), A.subtract, A.is_gt, ["vb0", "vb1"] + pk(TH),
           ["n00"])
        tt(T.n1[:, 1:8], T.n0[:, 1:8], T.tq[:, 1:8], A.add, ["n0", "tq"], ["n1"])
        ts(T.noff[:, 0:1], T.n0[:, 0:1], pc(DF0), pc(B0), A.mult, A.add, ["n00"] + pk(DF0, B0), ["noff0"])
        ts(T.noff[:, 1:8], T.n1[:, 1:8], pc(DF), pc(B1), A.mult, A.add, ["n1"] + pk(DF, B1), ["noff"])

        def by_kind(q, b):
            src = T.hp[:, M * b:M * b + M].indirect(T.noff[:])
            if q == "v":
                cp(T.hs[:, 128 * b:128 * b + 128], src, ["hp%d" % b] + NK, ["hs%d" % b])
            else:
                act(T.hs[:, 128 * b:128 * b + 128], src, F.Copy, ["hp%d" % b] + NK, ["hs%d" % b])

        def picked(b, k):
            lo, hi = PIECE[k]
            return T.hs[:, 128 * b:128 * b + 128].indirect(T.toff[:, lo // 16:hi // 16])

        def xs(b, k):
            lo, hi = PIECE[k]
            return T.xt[:, 4 * lo + b:4 * hi:4]

        def direct(b, k):
            tt(xs(b, k), picked(b, k), fplane(b, *PIECE[k]), A.add, ["hs%d" % b, "toff", "f%d" % b], ["xt%d%d" % (b, k)])

        def fetch(b, k):
            lo, hi = PIECE[k]
            act(T.hg[:, C * b + lo:C * b + hi], picked(b, k), F.Copy, ["hs%d" % b, "toff"], ["hg%d%d" % (b, k)])

        def add(b, k):
            lo, hi = PIECE[k]
            tt(xs(b, k), T["pf%d" % b][:, lo:hi], T.hg[:, C * b + lo:C * b + hi], A.add,
               ["hg%d%d" % (b, k), "pf%d" % b], ["xt%d%d" % (b, k)])

        last = r == R - 1
        first_store = used[0]
        for b in range(2):
            by_kind("v", b)
            by_kind("s", b + 2)
        for b, k in ((2, 0), (3, 0), (0, 1), (3, 1), (2, 1)):
            fetch(b, k)
        for b in range(2):
            direct(b, 0)
        for b, k in ((2, 0), (3, 0), (0, 1)):
            add(b, k)
        quant_x(T.xt, 0, ["xt%d0" % b for b in range(4)])
        if last:
            mm("pbk", CUT, T.qv[:], T.sv[:], T.qx[:, 0:CUT], T.sx[:, 0:CUT], ["qv", "qx0"])
            dma("y", T.oc[:, 0:4 * CUT], T.qx[:, 0:CUT].bitcast(dt.uint8), ["qx0"], [])
            act(T.ids[:], T.idp[:, 0:M].indirect(T.noff[:]), F.Copy, ["idp"] + NK, ["ids"])
            act(T.ys[:, 0:CUT], T.pbk[:, 0:CUT], F.Copy, ["pbk"], ["ys0"])
            act(T.ndb[:], T.ids[:, 0:128].indirect(T.toff[:]), F.Copy, ["ids", "toff"], ["ndb"])
            dma("y", T.y[:, 0:CUT], T.ys[:, 0:CUT], ["ys0"], [])
        else:
            scores(0)
            colour_scores(0)
            colours(0)
        direct(1, 1)
        for b in (3, 2):
            add(b, 1)
        if not last:
            keep(1)
        quant_x(T.xt, 1, ["xt%d1" % b for b in range(4)])
        if not last:
            scores(1)
            keep(0)
            hold(1)

    mm("pd", C - CUT, T.qv[:], T.sv[:], T.qx[:, CUT:C], T.sx[:, CUT:C], ["qv", "qx1"])
    dma("y", T.oc[:, 4 * CUT:4 * C], T.qx[:, CUT:C].bitcast(dt.uint8), ["qx1"], [])
    for k in range(4):
        dma("ys"[k % 2], T.osc[4 * k:4 * k + 4, :], T.sx[32 * k:32 * k + 4, :], QX, [])
    cp(T.ys[:, CUT:C], T.pd[:, 0:C - CUT], ["pd"], ["ys1"])
    dma("s", T.nd[:], T.ndb[0:128:16, :], ["ndb"], [])
    dma("y", T.y[:, CUT:C], T.ys[:, CUT:C], ["ys1"], [])
    stores = ["d%d" % k for k in range(first_store, used[0])]
    for s in [s for s in count if s not in stores] + stores:
        g.wait_ge(T.sem[s], count[s])
